import numpy as np
import ml_dtypes


def mxq(x, axis, fmt="e4m3"):
    dtype, down = {"e4m3": (ml_dtypes.float8_e4m3fn, 7), "e5m2": (ml_dtypes.float8_e5m2, 14)}[fmt]
    v = np.moveaxis(np.asarray(x, np.float32).astype(ml_dtypes.bfloat16).astype(np.float64), axis, -1)
    blocks = v.reshape(v.shape[:-1] + (-1, 32))
    amax = np.abs(blocks).max(-1, keepdims=True)
    byte = np.maximum(np.where(amax > 0, np.frexp(amax)[1] - 1 + 127, 0) - down, 1)
    scale = np.exp2(byte - 127.0)
    codes = (blocks / scale).astype(np.float32).astype(dtype).astype(np.float64)
    return np.moveaxis((codes * scale).reshape(v.shape), -1, axis)


WIDE = False


def mx_kscale(k):
    if not WIDE:
        return np.ones(k)
    levels = np.array([10, -10, 5, -5, 0])
    if k % 512:
        return np.exp2(np.random.permutation(np.resize(levels, k // 32))).repeat(32)
    a = np.empty((k // 512, 16))
    for p in range(k // 512):
        a[p, :8] = np.random.permutation(np.resize(levels, 8))
        for g in range(8):
            far = levels[np.abs(levels - a[p, g]) >= 10]
            a[p, g + 8] = far[np.random.randint(len(far))]
    return np.exp2(a.ravel()).repeat(32)


def f64(x):
    return np.asarray(x).astype(np.float64)


def striped(idx):
    return np.tile(idx.reshape(-1, 16).T, (8, 1)).astype(np.uint16)


def unstriped(offs):
    return offs[:16].T.reshape(-1).astype(np.int64)


def pack_weight(w):
    k, n = w.shape
    w = f64(np.asarray(w, np.float32).astype(ml_dtypes.bfloat16)).reshape(k // 32, 32, n)
    amax = np.abs(w).max(1)
    byte = np.clip(np.where(amax > 0, np.frexp(amax)[1] - 1 + 127 - 7, 1), 1, 254)
    scaled = (w * np.exp2(127.0 - byte)[:, None, :]).reshape(k, n).astype(np.float32)
    words = np.ascontiguousarray(scaled.reshape(k // 512, 128, 4, n).transpose(0, 1, 3, 2)).astype(ml_dtypes.float8_e4m3fn).view(np.uint8)
    return words, np.ascontiguousarray(byte.astype(np.uint8).reshape(k // 512, 16, n))


def unpack_weight(words, scales):
    g, p, n, _ = words.shape
    vals = np.ascontiguousarray(words).view(ml_dtypes.float8_e4m3fn).astype(np.float64) * np.repeat(np.exp2(scales.astype(np.float64) - 127.0), 8, axis=1)[..., None]
    return vals.transpose(0, 1, 3, 2).reshape(g * 512, n)


def planes(y):
    n, m = y.shape
    v = y.astype(np.float32).astype(ml_dtypes.bfloat16).astype(np.float64).reshape(n // 32, 32, m)
    top = np.abs(v).max(1)
    byte = np.clip(np.where(top > 0, np.frexp(top)[1] - 1 + 127 - 7, 1), 1, 254)
    codes = (v * np.exp2(127.0 - byte)[:, None, :]).reshape(n, m).astype(np.float32).astype(ml_dtypes.float8_e4m3fn).view(np.uint8)
    words = codes.reshape(n // 512, 128, 4, m).transpose(0, 1, 3, 2)
    return np.ascontiguousarray(words), np.ascontiguousarray(byte.astype(np.uint8).reshape(n // 512, 16, m))


def silu(v):
    return v / (1.0 + np.exp(-np.maximum(v, -700.0)))


K, T, S, H, N, R = 1024, 4096, 1024, 512, 512, 256
P = 2 ** 7


def setup_inputs():
    n = np.random.standard_normal
    s = mx_kscale(K)[:, None]
    u = mx_kscale(H)
    packed_xT = pack_weight(n((K, T)) * s)
    return {
        "x_words": packed_xT[0],
        "x_scales": packed_xT[1],
        "w1": (n((K, H)) / np.sqrt(K) / s * u).astype(np.float32),
        "w2": (n((H, N)) / np.sqrt(H) / u[:, None]).astype(np.float32),
        "temb": (n((H, R)) * u[:, None]).astype(np.float32),
        "lat": (n((N, S))).astype(np.float32),
        "csig": (np.tile(np.random.uniform(1.0, 1.2, R), (P, 1))).astype(np.float32),
        "cnoise": (np.tile(np.random.uniform(0.1, 0.8, R), (P, 1))).astype(np.float32),
        "offs": striped(np.random.permutation(T)[:S]),
        "step": striped(np.random.permutation(np.concatenate([np.arange(R), np.random.randint(0, R, S - R)]))),
    }


def reference(x_words, x_scales, w1, w2, temb, lat, csig, cnoise, offs, step):
    xq = unpack_weight(x_words, x_scales)[:, unstriped(offs)]
    h = silu((mxq(f64(w1), 0, "e4m3").T @ xq) + f64(temb)[:, unstriped(step)])
    ee = mxq(f64(w2), 0, "e4m3").T @ mxq(h, 0, "e4m3")
    out_0 = f64(lat) * (f64(csig)[:1][:, unstriped(step)]) - (ee * (f64(cnoise)[:1][:, unstriped(step)]))
    return (out_0,) + planes(out_0)

@@ -1,0 +1,279 @@
+from contextlib import ExitStack
+
+import concourse.mybir as mybir
+from concourse.masks import make_identity
+
+K, T, S, H, N, R = 1024, 4096, 1024, 512, 512, 256
+FLOPS = 2 * S * (K * H + H * N)
+
+F32 = mybir.dt.float32
+BF16 = mybir.dt.bfloat16
+I32 = mybir.dt.int32
+U32 = mybir.dt.uint32
+U16 = mybir.dt.uint16
+U8 = mybir.dt.uint8
+FP8X4 = mybir.dt.float8_e4m3fn_x4
+ALU = mybir.AluOpType
+ACT = mybir.ActivationFunctionType
+
+P = 128
+PACK = 4
+BANK = 512
+HALF = 512
+TEMB = 512
+TEMB_WINDOW = 704
+COEF_WINDOW = 528
+WIDTHS = [256,256,256,128,128]
+LAT = 256
+ON_TENSOR = []
+ROUND_ON_VECTOR = [0,1,2,3]
+ROUND_ON_GPSIMD = []
+
+
+def tile_picked_yddpm_silu_po_kernel(
+    tc, x_words, x_scales, w1, w2, temb, lat, csig, cnoise, offs, step, out_0, out_1, out_2
+):
+    nc = tc.nc
+    passes = K // (P * PACK)
+    halves = S // HALF
+    chunks = len(WIDTHS)
+    starts = [sum(WIDTHS[:c]) for c in range(chunks)]
+
+    with ExitStack() as ctx:
+        keep = ctx.enter_context(tc.tile_pool(name="keep", bufs=1))
+        ring = ctx.enter_context(tc.tile_pool(name="ring", bufs=2))
+        psum = ctx.enter_context(tc.psum_pool(name="psum", bufs=1))
+
+        step_list = keep.tile([P, S // 16], U16, name="step_list")
+        offs_list = keep.tile([P, S // 16], U16, name="offs_list")
+        temb_rows = keep.tile([P, (PACK - 1) * R + TEMB_WINDOW], F32, name="temb_rows")
+        coef_rows = keep.tile([P, COEF_WINDOW], F32, name="coef_rows")
+        xs_all = keep.tile([P, T], U8, name="xs_all", align_bytes=64)
+        xw_all = [keep.tile([P, T], U32, name="xw_all%d" % o, align_bytes=64) for o in range(passes)]
+        w1_raw = [keep.tile([P, PACK, H], F32, name="w1_raw%d" % o) for o in range(passes)]
+        w2_raw = keep.tile([P, PACK, N], F32, name="w2_raw")
+        lat_rows = [keep.tile([P, PACK, LAT], F32, name="lat_rows%d" % c) for c in range(S // LAT)]
+        ident = keep.tile([P, P], F32, name="ident")
+
+        nc.gpsimd.memset(xs_all[:].bitcast(I32), 0)
+        nc.vector.memset(coef_rows[:, R:], 0.0)
+        nc.vector.memset(temb_rows[:, PACK * R :], 0.0)
+        make_identity(nc, ident[:])
+
+        def load_words(o):
+            nc.sync.dma_start(
+                out=xw_all[o][:].bitcast(I32), in_=x_words[o].rearrange("p c r -> p (c r)").bitcast(I32)
+            )
+
+        def load_rows(raw, rows):
+            nc.sync.dma_start(out=raw, in_=rows.rearrange("(p j) c -> p j c", j=PACK))
+
+        def load_lat(c):
+            load_rows(lat_rows[c][:], lat[:, c * LAT : (c + 1) * LAT])
+
+        nc.sync.dma_start(step_list[:], step)
+        nc.sync.dma_start(out=coef_rows[: P // 2, :R], in_=csig[: P // 2, :])
+        nc.sync.dma_start(out=coef_rows[P // 2 :, :R], in_=cnoise[P // 2 :, :])
+        nc.sync.dma_start(out=temb_rows[:, : PACK * R], in_=temb.rearrange("(p t) r -> p (t r)", t=PACK))
+        nc.sync.dma_start(offs_list[:], offs)
+        load_lat(0)
+        load_lat(1)
+        for q in range(4):
+            nc.sync.dma_start(
+                out=xs_all[32 * q : 32 * q + 4 * passes, :].bitcast(I32),
+                in_=x_scales[:, 4 * q : 4 * q + 4, :].bitcast(I32),
+            )
+        load_words(0)
+        load_rows(w1_raw[0][:], w1[:512, :])
+        load_rows(w1_raw[1][:], w1[512:, :])
+        load_words(1)
+        load_rows(w2_raw[:], w2)
+        load_lat(2)
+        load_lat(3)
+
+        def entries(lst, first, count):
+            return lst[:, first // 16 : (first + count) // 16]
+
+        temb_of = {}
+        coef_of = [keep.tile([P, HALF], F32, name="coef_of%d" % h) for h in range(halves)]
+        coef = keep.tile([P, S // P, 2], F32, name="coef")
+        minus_cn = keep.tile([P, S // P], F32, name="minus_cn")
+        xs = keep.tile([P, S], U8, name="xs", align_bytes=64)
+        xw = [
+            [keep.tile([P, HALF], U32, name="xw%d_%d" % (o, h), align_bytes=64) for h in range(halves)]
+            for o in range(passes)
+        ]
+
+        def gather_temb(h):
+            temb_of[h] = ring.tile([P, PACK, TEMB], F32, name="temb_of", bufs=2)
+            for t in range(PACK):
+                nc.vector.tensor_copy(
+                    temb_of[h][:, t, :],
+                    temb_rows[:, t * R : t * R + TEMB_WINDOW].indirect(entries(step_list, h * TEMB, TEMB)),
+                )
+
+        def gather_coef(h):
+            nc.vector.tensor_copy(coef_of[h][:], coef_rows[:].indirect(entries(step_list, h * HALF, HALF)))
+            bank = psum.tile([P, HALF // P, P], F32, name="turn", bufs=2)
+            for b in range(HALF // P):
+                nc.tensor.transpose(bank[:, b, :], coef_of[h][:, b * P : (b + 1) * P], ident[:])
+            nc.scalar.copy(coef[:, h * (HALF // P) : (h + 1) * (HALF // P), :], bank[:, :, 0 : P : P // 2])
+
+        def gather_words(o, h):
+            nc.vector.tensor_copy(xw[o][h][:], xw_all[o][:].indirect(entries(offs_list, h * HALF, HALF)))
+
+        def deal(raw, name):
+            dealt = keep.tile([P, PACK * 512], BF16, name=name, align_bytes=64)
+            nc.scalar.copy(
+                dealt[:].rearrange("p (t m j) -> p m j t", t=PACK, j=PACK),
+                raw[:].rearrange("p j (m t) -> p m j t", t=PACK),
+            )
+            return dealt
+
+        def quantise(values, width, name, pool):
+            codes = pool.tile([P, width], U32, name=name + "_codes", align_bytes=64)
+            scales = pool.tile([P, width], U8, name=name + "_scales", align_bytes=64)
+            nc.vector.quantize_mx(out=codes[:].bitcast(FP8X4), scales=scales[:], in_=values)
+            return codes, scales
+
+        signals = {}
+
+        def signal(g):
+            c, c0 = divmod(g * P, LAT)
+            turned = psum.tile([P, PACK, P], F32, name="turn", bufs=2)
+            for t in range(PACK):
+                nc.tensor.transpose(turned[:, t, :], lat_rows[c][:, t, c0 : c0 + P], ident[:])
+            signals[g] = ring.tile([P, N], F32, name="signal", bufs=8)
+            nc.scalar.activation(
+                signals[g][:], turned[:].rearrange("p t m -> p (t m)"), ACT.Copy, scale=coef[:, g, 0:1]
+            )
+
+        warm = keep.tile([P, 1], F32, name="warm")
+        nc.scalar.activation(warm[:], ident[:, 0:1], ACT.Silu)
+
+        gather_coef(0)
+        gather_coef(1)
+        gather_temb(0)
+        nc.vector.tensor_copy(xs[:], xs_all[:].indirect(offs_list[:]))
+        w1_dealt = [deal(w1_raw[o], "w1_dealt%d" % o) for o in range(passes)]
+        w2_dealt = deal(w2_raw, "w2_dealt")
+        gather_words(0, 0)
+        gather_words(0, 1)
+        w1_q = [quantise(w1_dealt[o][:], H, "w1_%d" % o, keep) for o in range(passes)]
+        gather_temb(1)
+        w2_codes, w2_scales = quantise(w2_dealt[:], N, "w2", keep)
+        gather_words(1, 0)
+        gather_words(1, 1)
+
+
+        out_codes = keep.tile([P, S], U32, name="out_codes", align_bytes=64)
+        out_scales = keep.tile([P, S], U8, name="out_scales", align_bytes=64)
+        hidden = {}
+        result = {}
+        rounded = {}
+
+        def weave(ap):
+            return ap.rearrange("p (c i t) -> p c t i", i=4, t=PACK)
+
+        def planes(ap):
+            return ap.rearrange("p t (c i) -> p c t i", i=4)
+
+        def layer1(c):
+            width = WIDTHS[c]
+            h, c0 = divmod(starts[c], HALF)
+            e, e0 = divmod(starts[c], TEMB)
+            per_bank = BANK // width
+            pre = ring.tile([P, PACK, width], F32, name="pre")
+            for t0 in range(0, PACK, per_bank):
+                acc = psum.tile([P, per_bank, width], F32, name="acc", bufs=2)
+                for t in range(t0, t0 + per_bank):
+                    for o in reversed(range(passes)):
+                        codes, scales = w1_q[o]
+                        nc.tensor.matmul_mx(
+                            out=acc[:, t - t0, :],
+                            lhsT=codes[:, t * P : (t + 1) * P].bitcast(FP8X4),
+                            lhsT_scale=scales[:, t * P : (t + 1) * P],
+                            rhs=xw[o][h][:, c0 : c0 + width].bitcast(FP8X4),
+                            rhs_scale=xs[4 * o :, starts[c] : starts[c] + width],
+                            start=(o == passes - 1),
+                            stop=(o == 0),
+                        )
+                nc.vector.tensor_tensor(
+                    pre[:, t0 : t0 + per_bank, :], acc[:], temb_of[e][:, t0 : t0 + per_bank, e0 : e0 + width], ALU.add
+                )
+            hidden[c] = ring.tile([P, width * PACK], BF16, name="hidden", align_bytes=64)
+            nc.scalar.activation(weave(hidden[c][:]), planes(pre[:]), ACT.Silu)
+
+        def layer2(c):
+            width = WIDTHS[c]
+            h_codes, h_scales = quantise(hidden[c][:], width, "h", ring)
+            final = ring.tile([P, PACK, width], F32, name="final", bufs=3)
+            rounded[c] = ring.tile([P, width * PACK], BF16, name="rounded", align_bytes=64)
+            for b in range(width // P):
+                g = starts[c] // P + b
+                toks = slice(b * P, (b + 1) * P)
+                if g not in signals:
+                    signal(g)
+                noise = psum.tile([P, N], F32, name="noise", bufs=2)
+                nc.tensor.matmul_mx(
+                    out=noise[:],
+                    lhsT=h_codes[:, toks].bitcast(FP8X4),
+                    lhsT_scale=h_scales[:, toks],
+                    rhs=w2_codes[:].bitcast(FP8X4),
+                    rhs_scale=w2_scales[:],
+                    start=True,
+                    stop=True,
+                )
+                minus = ring.tile([P, N], F32, name="minus", bufs=3)
+                back = psum.tile([P, PACK, P], F32, name="back", bufs=2)
+                if g in ON_TENSOR:
+                    sign = 1.0
+                    nc.scalar.activation(minus[:], noise[:], ACT.Copy, scale=minus_cn[:, g : g + 1])
+                    for t in range(PACK):
+                        for part, first in ((minus, True), (signals[g], False)):
+                            nc.tensor.matmul(
+                                back[:, t, :], part[:, t * P : (t + 1) * P], ident[:],
+                                start=first, stop=not first, is_transpose=True,
+                            )
+                else:
+                    sign = -1.0
+                    nc.vector.scalar_tensor_tensor(
+                        minus[:], noise[:], coef[:, g, 1:2], signals[g][:], ALU.mult, ALU.subtract
+                    )
+                    for t in range(PACK):
+                        nc.tensor.transpose(back[:, t, :], minus[:, t * P : (t + 1) * P], ident[:])
+                if c not in ROUND_ON_VECTOR and c not in ROUND_ON_GPSIMD:
+                    nc.scalar.activation(
+                        weave(rounded[c][:, b * P * PACK : (b + 1) * P * PACK]), planes(back[:]), ACT.Copy, scale=sign
+                    )
+                nc.scalar.activation(final[:, :, toks], back[:], ACT.Copy, scale=sign)
+                if c in ROUND_ON_GPSIMD:
+                    nc.gpsimd.tensor_scalar(
+                        weave(rounded[c][:, b * P * PACK : (b + 1) * P * PACK]), planes(final[:, :, toks]), 1.0, 0.0, ALU.mult, ALU.add
+                    )
+            nc.sync.dma_start(
+                out=out_0[:, starts[c] : starts[c] + width].rearrange("(p t) s -> p t s", t=PACK), in_=final[:]
+            )
+            result[c] = final
+
+        def hand_on(c):
+            cols = slice(starts[c], starts[c] + WIDTHS[c])
+            if c in ROUND_ON_VECTOR:
+                nc.vector.tensor_copy(weave(rounded[c][:]), planes(result[c][:]))
+            nc.vector.quantize_mx(out=out_codes[:, cols].bitcast(FP8X4), scales=out_scales[:, cols], in_=rounded[c][:])
+            nc.sync.dma_start(
+                out=out_1[0].rearrange("p c r -> p (c r)").bitcast(I32)[:, cols], in_=out_codes[:, cols].bitcast(I32)
+            )
+
+        for s in range(chunks + 2):
+
+            if s < chunks:
+                layer1(s)
+            if 1 <= s < chunks + 1:
+                layer2(s - 1)
+            if s >= 2:
+                hand_on(s - 2)
+        for q in range(4):
+            nc.scalar.dma_start(
+                out=out_2[0, 4 * q : 4 * q + 4, :].bitcast(I32), in_=out_scales[32 * q : 32 * q + 4, :].bitcast(I32)
+            )

@@ -24,9 +24,10 @@ TEMB = 512
 TEMB_WINDOW = 704
 COEF_WINDOW = 528
 WIDTHS = [256,256,256,128,128]
+STORE_AFTER = {1: 0, 2: 512, 4: 768}
 LAT = 256
 ON_TENSOR = []
-ROUND_ON_VECTOR = [0,1,2,3]
+ROUND_ON_VECTOR = [0,1,2,3,4,5,6,7]
 ROUND_ON_GPSIMD = []
 
 
@@ -76,18 +77,18 @@ def tile_picked_yddpm_silu_po_kernel(
         nc.sync.dma_start(out=coef_rows[P // 2 :, :R], in_=cnoise[P // 2 :, :])
         nc.sync.dma_start(out=temb_rows[:, : PACK * R], in_=temb.rearrange("(p t) r -> p (t r)", t=PACK))
         nc.sync.dma_start(offs_list[:], offs)
-        load_lat(0)
-        load_lat(1)
         for q in range(4):
             nc.sync.dma_start(
                 out=xs_all[32 * q : 32 * q + 4 * passes, :].bitcast(I32),
                 in_=x_scales[:, 4 * q : 4 * q + 4, :].bitcast(I32),
             )
+        load_lat(0)
         load_words(0)
         load_rows(w1_raw[0][:], w1[:512, :])
         load_rows(w1_raw[1][:], w1[512:, :])
         load_words(1)
         load_rows(w2_raw[:], w2)
+        load_lat(1)
         load_lat(2)
         load_lat(3)
 
@@ -183,7 +184,7 @@ def tile_picked_yddpm_silu_po_kernel(
             h, c0 = divmod(starts[c], HALF)
             e, e0 = divmod(starts[c], TEMB)
             per_bank = BANK // width
-            pre = ring.tile([P, PACK, width], F32, name="pre")
+            pre = ring.tile([P, PACK, width], F32, name="pre", bufs=2)
             for t0 in range(0, PACK, per_bank):
                 acc = psum.tile([P, per_bank, width], F32, name="acc", bufs=2)
                 for t in range(t0, t0 + per_bank):
@@ -201,14 +202,14 @@ def tile_picked_yddpm_silu_po_kernel(
                 nc.vector.tensor_tensor(
                     pre[:, t0 : t0 + per_bank, :], acc[:], temb_of[e][:, t0 : t0 + per_bank, e0 : e0 + width], ALU.add
                 )
-            hidden[c] = ring.tile([P, width * PACK], BF16, name="hidden", align_bytes=64)
+            hidden[c] = ring.tile([P, width * PACK], BF16, name="hidden", bufs=2, align_bytes=64)
             nc.scalar.activation(weave(hidden[c][:]), planes(pre[:]), ACT.Silu)
 
         def layer2(c):
             width = WIDTHS[c]
             h_codes, h_scales = quantise(hidden[c][:], width, "h", ring)
-            final = ring.tile([P, PACK, width], F32, name="final", bufs=3)
-            rounded[c] = ring.tile([P, width * PACK], BF16, name="rounded", align_bytes=64)
+            final = ring.tile([P, PACK, width], F32, name="final", bufs=5)
+            rounded[c] = ring.tile([P, width * PACK], BF16, name="rounded", bufs=4, align_bytes=64)
             for b in range(width // P):
                 g = starts[c] // P + b
                 toks = slice(b * P, (b + 1) * P)
@@ -224,7 +225,7 @@ def tile_picked_yddpm_silu_po_kernel(
                     start=True,
                     stop=True,
                 )
-                minus = ring.tile([P, N], F32, name="minus", bufs=3)
+                minus = ring.tile([P, N], F32, name="minus", bufs=4)
                 back = psum.tile([P, PACK, P], F32, name="back", bufs=2)
                 if g in ON_TENSOR:
                     sign = 1.0
@@ -242,16 +243,16 @@ def tile_picked_yddpm_silu_po_kernel(
                     )
                     for t in range(PACK):
                         nc.tensor.transpose(back[:, t, :], minus[:, t * P : (t + 1) * P], ident[:])
+                nc.scalar.activation(final[:, :, toks], back[:], ACT.Copy, scale=sign)
                 if c not in ROUND_ON_VECTOR and c not in ROUND_ON_GPSIMD:
                     nc.scalar.activation(
                         weave(rounded[c][:, b * P * PACK : (b + 1) * P * PACK]), planes(back[:]), ACT.Copy, scale=sign
                     )
-                nc.scalar.activation(final[:, :, toks], back[:], ACT.Copy, scale=sign)
                 if c in ROUND_ON_GPSIMD:
                     nc.gpsimd.tensor_scalar(
                         weave(rounded[c][:, b * P * PACK : (b + 1) * P * PACK]), planes(final[:, :, toks]), 1.0, 0.0, ALU.mult, ALU.add
                     )
-            nc.sync.dma_start(
+            (nc.scalar if c >= chunks - 1 else nc.sync).dma_start(
                 out=out_0[:, starts[c] : starts[c] + width].rearrange("(p t) s -> p t s", t=PACK), in_=final[:]
             )
             result[c] = final
@@ -261,19 +262,21 @@ def tile_picked_yddpm_silu_po_kernel(
             if c in ROUND_ON_VECTOR:
                 nc.vector.tensor_copy(weave(rounded[c][:]), planes(result[c][:]))
             nc.vector.quantize_mx(out=out_codes[:, cols].bitcast(FP8X4), scales=out_scales[:, cols], in_=rounded[c][:])
-            nc.sync.dma_start(
-                out=out_1[0].rearrange("p c r -> p (c r)").bitcast(I32)[:, cols], in_=out_codes[:, cols].bitcast(I32)
-            )
+            if c in STORE_AFTER:
+                done = slice(STORE_AFTER[c], cols.stop)
+                nc.sync.dma_start(
+                    out=out_1[0].rearrange("p c r -> p (c r)").bitcast(I32)[:, done], in_=out_codes[:, done].bitcast(I32)
+                )
 
-        for s in range(chunks + 2):
+        for s in range(chunks + 8):
 
             if s < chunks:
                 layer1(s)
             if 1 <= s < chunks + 1:
                 layer2(s - 1)
-            if s >= 2:
-                hand_on(s - 2)
+            if s >= 8:
+                hand_on(s - 8)
         for q in range(4):
-            nc.scalar.dma_start(
-                out=out_2[0, 4 * q : 4 * q + 4, :].bitcast(I32), in_=out_scales[32 * q : 32 * q + 4, :].bitcast(I32)
+            nc.sync.dma_start(
+                out=out_2[0, q : 16 : 4, :].bitcast(I32), in_=out_scales[q : P : 32, :].bitcast(I32)
             )

@@ -25,9 +25,10 @@ TEMB_WINDOW = 704
 COEF_WINDOW = 528
 WIDTHS = [256,256,256,128,128]
 STORE_AFTER = {1: 0, 2: 512, 4: 768}
-LAT = 256
+FINAL_ON_VECTOR = []
+LAT = 512
 ON_TENSOR = []
-ROUND_ON_VECTOR = [0,1,2,3,4,5,6,7]
+ROUND_ON_VECTOR = [0,1,2,3,4,5]
 ROUND_ON_GPSIMD = []
 
 
@@ -51,12 +52,13 @@ def tile_picked_yddpm_silu_po_kernel(
         coef_rows = keep.tile([P, COEF_WINDOW], F32, name="coef_rows")
         xs_all = keep.tile([P, T], U8, name="xs_all", align_bytes=64)
         xw_all = [keep.tile([P, T], U32, name="xw_all%d" % o, align_bytes=64) for o in range(passes)]
-        w1_raw = [keep.tile([P, PACK, H], F32, name="w1_raw%d" % o) for o in range(passes)]
-        w2_raw = keep.tile([P, PACK, N], F32, name="w2_raw")
-        lat_rows = [keep.tile([P, PACK, LAT], F32, name="lat_rows%d" % c) for c in range(S // LAT)]
+        w1_raw = [ring.tile([P, PACK, H], F32, name="w1_raw%d" % o, tag="raw") for o in range(passes)]
+        w2_raw = ring.tile([P, PACK, N], F32, name="w2_raw", tag="raw")
+        lat_rows = [keep.tile([P, PACK, LAT], F32, name="lat_rows0"), ring.tile([P, PACK, LAT], F32, name="lat_rows1", tag="raw")]
         ident = keep.tile([P, P], F32, name="ident")
 
-        nc.gpsimd.memset(xs_all[:].bitcast(I32), 0)
+        nc.gpsimd.memset(xs_all[32:64, :].bitcast(I32), 0)
+        nc.vector.memset(xs_all[64:, :].bitcast(I32), 0)
         nc.vector.memset(coef_rows[:, R:], 0.0)
         nc.vector.memset(temb_rows[:, PACK * R :], 0.0)
         make_identity(nc, ident[:])
@@ -72,25 +74,17 @@ def tile_picked_yddpm_silu_po_kernel(
         def load_lat(c):
             load_rows(lat_rows[c][:], lat[:, c * LAT : (c + 1) * LAT])
 
+        nc.sync.dma_start(offs_list[:], offs)
+        nc.sync.dma_start(out=xs_all[:32, :].bitcast(I32), in_=x_scales.rearrange("o q c -> (o q) c").bitcast(I32))
         nc.sync.dma_start(step_list[:], step)
         nc.sync.dma_start(out=coef_rows[: P // 2, :R], in_=csig[: P // 2, :])
         nc.sync.dma_start(out=coef_rows[P // 2 :, :R], in_=cnoise[P // 2 :, :])
         nc.sync.dma_start(out=temb_rows[:, : PACK * R], in_=temb.rearrange("(p t) r -> p (t r)", t=PACK))
-        nc.sync.dma_start(offs_list[:], offs)
-        for q in range(4):
-            nc.sync.dma_start(
-                out=xs_all[32 * q : 32 * q + 4 * passes, :].bitcast(I32),
-                in_=x_scales[:, 4 * q : 4 * q + 4, :].bitcast(I32),
-            )
         load_lat(0)
         load_words(0)
         load_rows(w1_raw[0][:], w1[:512, :])
         load_rows(w1_raw[1][:], w1[512:, :])
         load_words(1)
-        load_rows(w2_raw[:], w2)
-        load_lat(1)
-        load_lat(2)
-        load_lat(3)
 
         def entries(lst, first, count):
             return lst[:, first // 16 : (first + count) // 16]
@@ -115,7 +109,7 @@ def tile_picked_yddpm_silu_po_kernel(
 
         def gather_coef(h):
             nc.vector.tensor_copy(coef_of[h][:], coef_rows[:].indirect(entries(step_list, h * HALF, HALF)))
-            bank = psum.tile([P, HALF // P, P], F32, name="turn", bufs=2)
+            bank = psum.tile([P, HALF // P, P], F32, name="turn", bufs=1)
             for b in range(HALF // P):
                 nc.tensor.transpose(bank[:, b, :], coef_of[h][:, b * P : (b + 1) * P], ident[:])
             nc.scalar.copy(coef[:, h * (HALF // P) : (h + 1) * (HALF // P), :], bank[:, :, 0 : P : P // 2])
@@ -126,8 +120,8 @@ def tile_picked_yddpm_silu_po_kernel(
         def deal(raw, name):
             dealt = keep.tile([P, PACK * 512], BF16, name=name, align_bytes=64)
             nc.scalar.copy(
-                dealt[:].rearrange("p (t m j) -> p m j t", t=PACK, j=PACK),
-                raw[:].rearrange("p j (m t) -> p m j t", t=PACK),
+                dealt[:].rearrange("p (t m j) -> p m t j", t=PACK, j=PACK),
+                raw[:].rearrange("p j (m t) -> p m t j", t=PACK),
             )
             return dealt
 
@@ -141,7 +135,7 @@ def tile_picked_yddpm_silu_po_kernel(
 
         def signal(g):
             c, c0 = divmod(g * P, LAT)
-            turned = psum.tile([P, PACK, P], F32, name="turn", bufs=2)
+            turned = psum.tile([P, PACK, P], F32, name="turn", bufs=1)
             for t in range(PACK):
                 nc.tensor.transpose(turned[:, t, :], lat_rows[c][:, t, c0 : c0 + P], ident[:])
             signals[g] = ring.tile([P, N], F32, name="signal", bufs=8)
@@ -152,11 +146,21 @@ def tile_picked_yddpm_silu_po_kernel(
         warm = keep.tile([P, 1], F32, name="warm")
         nc.scalar.activation(warm[:], ident[:, 0:1], ACT.Silu)
 
+        picked = keep.tile([P, S], U8, name="picked", align_bytes=64)
+        nc.gpsimd.memset(xs[:].bitcast(I32), 0)
+        nc.vector.tensor_copy(picked[:], xs_all[:].indirect(offs_list[:]))
+        for o in range(passes):
+            for q in range(4):
+                nc.gpsimd.dma_start(
+                    out=xs[32 * q + 4 * o : 32 * q + 4 * o + 4, :].bitcast(I32),
+                    in_=picked[16 * o + 4 * q : 16 * o + 4 * q + 4, :].bitcast(I32),
+                )
         gather_coef(0)
         gather_coef(1)
         gather_temb(0)
-        nc.vector.tensor_copy(xs[:], xs_all[:].indirect(offs_list[:]))
         w1_dealt = [deal(w1_raw[o], "w1_dealt%d" % o) for o in range(passes)]
+        load_rows(w2_raw[:], w2)
+        load_lat(1)
         w2_dealt = deal(w2_raw, "w2_dealt")
         gather_words(0, 0)
         gather_words(0, 1)
@@ -186,7 +190,7 @@ def tile_picked_yddpm_silu_po_kernel(
             per_bank = BANK // width
             pre = ring.tile([P, PACK, width], F32, name="pre", bufs=2)
             for t0 in range(0, PACK, per_bank):
-                acc = psum.tile([P, per_bank, width], F32, name="acc", bufs=2)
+                acc = psum.tile([P, per_bank, width], F32, name="acc", bufs=3)
                 for t in range(t0, t0 + per_bank):
                     for o in reversed(range(passes)):
                         codes, scales = w1_q[o]
@@ -202,12 +206,12 @@ def tile_picked_yddpm_silu_po_kernel(
                 nc.vector.tensor_tensor(
                     pre[:, t0 : t0 + per_bank, :], acc[:], temb_of[e][:, t0 : t0 + per_bank, e0 : e0 + width], ALU.add
                 )
-            hidden[c] = ring.tile([P, width * PACK], BF16, name="hidden", bufs=2, align_bytes=64)
+            hidden[c] = ring.tile([P, width * PACK], BF16, name="hidden", bufs=3, align_bytes=64)
             nc.scalar.activation(weave(hidden[c][:]), planes(pre[:]), ACT.Silu)
 
         def layer2(c):
             width = WIDTHS[c]
-            h_codes, h_scales = quantise(hidden[c][:], width, "h", ring)
+            h_codes, h_scales = quantise(hidden[c][:], width, "h%d" % c, keep)
             final = ring.tile([P, PACK, width], F32, name="final", bufs=5)
             rounded[c] = ring.tile([P, width * PACK], BF16, name="rounded", bufs=4, align_bytes=64)
             for b in range(width // P):
@@ -243,7 +247,10 @@ def tile_picked_yddpm_silu_po_kernel(
                     )
                     for t in range(PACK):
                         nc.tensor.transpose(back[:, t, :], minus[:, t * P : (t + 1) * P], ident[:])
-                nc.scalar.activation(final[:, :, toks], back[:], ACT.Copy, scale=sign)
+                if g in FINAL_ON_VECTOR:
+                    nc.vector.tensor_scalar(final[:, :, toks], back[:], sign, None, ALU.mult)
+                else:
+                    nc.scalar.activation(final[:, :, toks], back[:], ACT.Copy, scale=sign)
                 if c not in ROUND_ON_VECTOR and c not in ROUND_ON_GPSIMD:
                     nc.scalar.activation(
                         weave(rounded[c][:, b * P * PACK : (b + 1) * P * PACK]), planes(back[:]), ACT.Copy, scale=sign
@@ -268,14 +275,14 @@ def tile_picked_yddpm_silu_po_kernel(
                     out=out_1[0].rearrange("p c r -> p (c r)").bitcast(I32)[:, done], in_=out_codes[:, done].bitcast(I32)
                 )
 
-        for s in range(chunks + 8):
+        for s in range(chunks + 2):
 
             if s < chunks:
                 layer1(s)
-            if 1 <= s < chunks + 1:
-                layer2(s - 1)
-            if s >= 8:
-                hand_on(s - 8)
+            if 0 <= s < chunks + 0:
+                layer2(s - 0)
+            if s >= 2:
+                hand_on(s - 2)
         for q in range(4):
             nc.sync.dma_start(
                 out=out_2[0, q : 16 : 4, :].bitcast(I32), in_=out_scales[q : P : 32, :].bitcast(I32)

@@ -94,9 +94,10 @@ def tile_picked_yddpm_silu_po_kernel(
         coef = keep.tile([P, S // P, 2], F32, name="coef")
         minus_cn = keep.tile([P, S // P], F32, name="minus_cn")
         xs = keep.tile([P, S], U8, name="xs", align_bytes=64)
+        xw_first = keep.tile([P, S], U32, name="xw_first", align_bytes=64)
         xw = [
-            [keep.tile([P, HALF], U32, name="xw%d_%d" % (o, h), align_bytes=64) for h in range(halves)]
-            for o in range(passes)
+            [xw_first[:, h * HALF : (h + 1) * HALF] for h in range(halves)],
+            [keep.tile([P, HALF], U32, name="xw1_%d" % h, align_bytes=64) for h in range(halves)],
         ]
 
         def gather_temb(h):
@@ -135,7 +136,10 @@ def tile_picked_yddpm_silu_po_kernel(
 
         def signal(g):
             c, c0 = divmod(g * P, LAT)
-            turned = psum.tile([P, PACK, P], F32, name="turn", bufs=1)
+            if g * P < LAT:
+                turned = psum.tile([P, PACK, P], F32, name="back", bufs=2)
+            else:
+                turned = psum.tile([P, PACK, P], F32, name="turn", bufs=1)
             for t in range(PACK):
                 nc.tensor.transpose(turned[:, t, :], lat_rows[c][:, t, c0 : c0 + P], ident[:])
             signals[g] = ring.tile([P, N], F32, name="signal", bufs=8)
@@ -143,8 +147,6 @@ def tile_picked_yddpm_silu_po_kernel(
                 signals[g][:], turned[:].rearrange("p t m -> p (t m)"), ACT.Copy, scale=coef[:, g, 0:1]
             )
 
-        warm = keep.tile([P, 1], F32, name="warm")
-        nc.scalar.activation(warm[:], ident[:, 0:1], ACT.Silu)
 
         picked = keep.tile([P, S], U8, name="picked", align_bytes=64)
         nc.gpsimd.memset(xs[:].bitcast(I32), 0)
@@ -157,13 +159,16 @@ def tile_picked_yddpm_silu_po_kernel(
                 )
         gather_coef(0)
         gather_coef(1)
-        gather_temb(0)
         w1_dealt = [deal(w1_raw[o], "w1_dealt%d" % o) for o in range(passes)]
         load_rows(w2_raw[:], w2)
         load_lat(1)
         w2_dealt = deal(w2_raw, "w2_dealt")
-        gather_words(0, 0)
-        gather_words(0, 1)
+        signal(0)
+        signal(1)
+        signal(2)
+        signal(3)
+        gather_temb(0)
+        nc.vector.tensor_copy(xw_first[:], xw_all[0][:].indirect(offs_list[:]))
         w1_q = [quantise(w1_dealt[o][:], H, "w1_%d" % o, keep) for o in range(passes)]
         gather_temb(1)
         w2_codes, w2_scales = quantise(w2_dealt[:], N, "w2", keep)

@@ -18,25 +18,24 @@ ACT = mybir.ActivationFunctionType
 
 P = 128
 PACK = 4
+K_PASS = P * PACK
+PASSES = K // K_PASS
+QUADRANT = 32
+SCALE_ROWS = K_PASS // 32
 BANK = 512
-HALF = 512
-TEMB = 512
+HALF = S // 2
+LINE = 4
 TEMB_WINDOW = 704
 COEF_WINDOW = 528
-WIDTHS = [256,256,256,128,128]
-STORE_AFTER = {1: 0, 2: 512, 4: 768}
-FINAL_ON_VECTOR = []
-LAT = 512
-ON_TENSOR = []
-ROUND_ON_VECTOR = [0,1,2,3,4,5]
-ROUND_ON_GPSIMD = []
+WIDTHS = [256, 256, 256, 128, 128]
+STORE_FROM = {1: 0, 2: 512, 4: 768}
+HAND_ON_LAG = 2
 
 
 def tile_picked_yddpm_silu_po_kernel(
     tc, x_words, x_scales, w1, w2, temb, lat, csig, cnoise, offs, step, out_0, out_1, out_2
 ):
     nc = tc.nc
-    passes = K // (P * PACK)
     halves = S // HALF
     chunks = len(WIDTHS)
     starts = [sum(WIDTHS[:c]) for c in range(chunks)]
@@ -51,14 +50,18 @@ def tile_picked_yddpm_silu_po_kernel(
         temb_rows = keep.tile([P, (PACK - 1) * R + TEMB_WINDOW], F32, name="temb_rows")
         coef_rows = keep.tile([P, COEF_WINDOW], F32, name="coef_rows")
         xs_all = keep.tile([P, T], U8, name="xs_all", align_bytes=64)
-        xw_all = [keep.tile([P, T], U32, name="xw_all%d" % o, align_bytes=64) for o in range(passes)]
-        w1_raw = [ring.tile([P, PACK, H], F32, name="w1_raw%d" % o, tag="raw") for o in range(passes)]
+        xw_all = [keep.tile([P, T], U32, name="xw_all%d" % o, align_bytes=64) for o in range(PASSES)]
+        w1_raw = [ring.tile([P, PACK, H], F32, name="w1_raw%d" % o, tag="raw") for o in range(PASSES)]
         w2_raw = ring.tile([P, PACK, N], F32, name="w2_raw", tag="raw")
-        lat_rows = [keep.tile([P, PACK, LAT], F32, name="lat_rows0"), ring.tile([P, PACK, LAT], F32, name="lat_rows1", tag="raw")]
+        lat_rows = [
+            keep.tile([P, PACK, HALF], F32, name="lat_rows0"),
+            ring.tile([P, PACK, HALF], F32, name="lat_rows1", tag="raw"),
+        ]
         ident = keep.tile([P, P], F32, name="ident")
 
-        nc.gpsimd.memset(xs_all[32:64, :].bitcast(I32), 0)
-        nc.vector.memset(xs_all[64:, :].bitcast(I32), 0)
+        scale_rows = PASSES * SCALE_ROWS
+        nc.gpsimd.memset(xs_all[scale_rows : P // 2, :].bitcast(I32), 0)
+        nc.vector.memset(xs_all[P // 2 :, :].bitcast(I32), 0)
         nc.vector.memset(coef_rows[:, R:], 0.0)
         nc.vector.memset(temb_rows[:, PACK * R :], 0.0)
         make_identity(nc, ident[:])
@@ -68,31 +71,29 @@ def tile_picked_yddpm_silu_po_kernel(
                 out=xw_all[o][:].bitcast(I32), in_=x_words[o].rearrange("p c r -> p (c r)").bitcast(I32)
             )
 
-        def load_rows(raw, rows):
-            nc.sync.dma_start(out=raw, in_=rows.rearrange("(p j) c -> p j c", j=PACK))
-
-        def load_lat(c):
-            load_rows(lat_rows[c][:], lat[:, c * LAT : (c + 1) * LAT])
+        def load_slots(tile, rows):
+            nc.sync.dma_start(out=tile[:], in_=rows.rearrange("(p t) c -> p t c", t=PACK))
 
         nc.sync.dma_start(offs_list[:], offs)
-        nc.sync.dma_start(out=xs_all[:32, :].bitcast(I32), in_=x_scales.rearrange("o q c -> (o q) c").bitcast(I32))
+        nc.sync.dma_start(
+            out=xs_all[:scale_rows, :].bitcast(I32), in_=x_scales.rearrange("o q c -> (o q) c").bitcast(I32)
+        )
         nc.sync.dma_start(step_list[:], step)
         nc.sync.dma_start(out=coef_rows[: P // 2, :R], in_=csig[: P // 2, :])
         nc.sync.dma_start(out=coef_rows[P // 2 :, :R], in_=cnoise[P // 2 :, :])
         nc.sync.dma_start(out=temb_rows[:, : PACK * R], in_=temb.rearrange("(p t) r -> p (t r)", t=PACK))
-        load_lat(0)
+        load_slots(lat_rows[0], lat[:, :HALF])
         load_words(0)
-        load_rows(w1_raw[0][:], w1[:512, :])
-        load_rows(w1_raw[1][:], w1[512:, :])
+        for o in range(PASSES):
+            load_slots(w1_raw[o], w1[o * K_PASS : (o + 1) * K_PASS, :])
         load_words(1)
 
-        def entries(lst, first, count):
-            return lst[:, first // 16 : (first + count) // 16]
+        def half_of(offsets, h):
+            return offsets[:, h * HALF // 16 : (h + 1) * HALF // 16]
 
         temb_of = {}
         coef_of = [keep.tile([P, HALF], F32, name="coef_of%d" % h) for h in range(halves)]
         coef = keep.tile([P, S // P, 2], F32, name="coef")
-        minus_cn = keep.tile([P, S // P], F32, name="minus_cn")
         xs = keep.tile([P, S], U8, name="xs", align_bytes=64)
         xw_first = keep.tile([P, S], U32, name="xw_first", align_bytes=64)
         xw = [
@@ -101,80 +102,72 @@ def tile_picked_yddpm_silu_po_kernel(
         ]
 
         def gather_temb(h):
-            temb_of[h] = ring.tile([P, PACK, TEMB], F32, name="temb_of", bufs=2)
+            temb_of[h] = ring.tile([P, PACK, HALF], F32, name="temb_of")
             for t in range(PACK):
-                nc.vector.tensor_copy(
-                    temb_of[h][:, t, :],
-                    temb_rows[:, t * R : t * R + TEMB_WINDOW].indirect(entries(step_list, h * TEMB, TEMB)),
-                )
+                window = temb_rows[:, t * R : t * R + TEMB_WINDOW]
+                nc.vector.tensor_copy(temb_of[h][:, t, :], window.indirect(half_of(step_list, h)))
 
         def gather_coef(h):
-            nc.vector.tensor_copy(coef_of[h][:], coef_rows[:].indirect(entries(step_list, h * HALF, HALF)))
-            bank = psum.tile([P, HALF // P, P], F32, name="turn", bufs=1)
-            for b in range(HALF // P):
+            groups = HALF // P
+            nc.vector.tensor_copy(coef_of[h][:], coef_rows[:].indirect(half_of(step_list, h)))
+            bank = psum.tile([P, groups, P], F32, name="turn")
+            for b in range(groups):
                 nc.tensor.transpose(bank[:, b, :], coef_of[h][:, b * P : (b + 1) * P], ident[:])
-            nc.scalar.copy(coef[:, h * (HALF // P) : (h + 1) * (HALF // P), :], bank[:, :, 0 : P : P // 2])
-
-        def gather_words(o, h):
-            nc.vector.tensor_copy(xw[o][h][:], xw_all[o][:].indirect(entries(offs_list, h * HALF, HALF)))
+            nc.scalar.copy(coef[:, h * groups : (h + 1) * groups, :], bank[:, :, 0 : P : P // 2])
 
         def deal(raw, name):
-            dealt = keep.tile([P, PACK * 512], BF16, name=name, align_bytes=64)
+            dealt = keep.tile([P, PACK * K_PASS], BF16, name=name, align_bytes=64)
             nc.scalar.copy(
                 dealt[:].rearrange("p (t m j) -> p m t j", t=PACK, j=PACK),
                 raw[:].rearrange("p j (m t) -> p m t j", t=PACK),
             )
             return dealt
 
-        def quantise(values, width, name, pool):
-            codes = pool.tile([P, width], U32, name=name + "_codes", align_bytes=64)
-            scales = pool.tile([P, width], U8, name=name + "_scales", align_bytes=64)
+        def quantise(values, width, name):
+            codes = keep.tile([P, width], U32, name=name + "_codes", align_bytes=64)
+            scales = keep.tile([P, width], U8, name=name + "_scales", align_bytes=64)
             nc.vector.quantize_mx(out=codes[:].bitcast(FP8X4), scales=scales[:], in_=values)
             return codes, scales
 
         signals = {}
 
-        def signal(g):
-            c, c0 = divmod(g * P, LAT)
-            if g * P < LAT:
-                turned = psum.tile([P, PACK, P], F32, name="back", bufs=2)
-            else:
-                turned = psum.tile([P, PACK, P], F32, name="turn", bufs=1)
+        def scale_lat(g, bank_tag, banks):
+            h, c0 = divmod(g * P, HALF)
+            turned = psum.tile([P, PACK, P], F32, name=bank_tag, bufs=banks)
             for t in range(PACK):
-                nc.tensor.transpose(turned[:, t, :], lat_rows[c][:, t, c0 : c0 + P], ident[:])
-            signals[g] = ring.tile([P, N], F32, name="signal", bufs=8)
+                nc.tensor.transpose(turned[:, t, :], lat_rows[h][:, t, c0 : c0 + P], ident[:])
+            signals[g] = ring.tile([P, N], F32, name="signal", bufs=S // P)
             nc.scalar.activation(
                 signals[g][:], turned[:].rearrange("p t m -> p (t m)"), ACT.Copy, scale=coef[:, g, 0:1]
             )
 
+        warm = keep.tile([P, 1], F32, name="warm")
+        nc.scalar.activation(warm[:], ident[:, 0:1], ACT.Silu)
 
         picked = keep.tile([P, S], U8, name="picked", align_bytes=64)
         nc.gpsimd.memset(xs[:].bitcast(I32), 0)
         nc.vector.tensor_copy(picked[:], xs_all[:].indirect(offs_list[:]))
-        for o in range(passes):
-            for q in range(4):
+        for o in range(PASSES):
+            for q in range(P // QUADRANT):
+                to_row, from_row = QUADRANT * q + 4 * o, SCALE_ROWS * o + 4 * q
                 nc.gpsimd.dma_start(
-                    out=xs[32 * q + 4 * o : 32 * q + 4 * o + 4, :].bitcast(I32),
-                    in_=picked[16 * o + 4 * q : 16 * o + 4 * q + 4, :].bitcast(I32),
+                    out=xs[to_row : to_row + 4, :].bitcast(I32), in_=picked[from_row : from_row + 4, :].bitcast(I32)
                 )
-        gather_coef(0)
-        gather_coef(1)
-        w1_dealt = [deal(w1_raw[o], "w1_dealt%d" % o) for o in range(passes)]
-        load_rows(w2_raw[:], w2)
-        load_lat(1)
+        for h in range(halves):
+            gather_coef(h)
+        w1_dealt = [deal(w1_raw[o], "w1_dealt%d" % o) for o in range(PASSES)]
+        load_slots(w2_raw, w2)
+        load_slots(lat_rows[1], lat[:, HALF:])
         w2_dealt = deal(w2_raw, "w2_dealt")
-        signal(0)
-        signal(1)
-        signal(2)
-        signal(3)
+        for g in range(HALF // P):
+            scale_lat(g, "back", 2)
         gather_temb(0)
         nc.vector.tensor_copy(xw_first[:], xw_all[0][:].indirect(offs_list[:]))
-        w1_q = [quantise(w1_dealt[o][:], H, "w1_%d" % o, keep) for o in range(passes)]
+        w1_q = [quantise(w1_dealt[o][:], H, "w1_%d" % o) for o in range(PASSES)]
         gather_temb(1)
-        w2_codes, w2_scales = quantise(w2_dealt[:], N, "w2", keep)
-        gather_words(1, 0)
-        gather_words(1, 1)
-
+        w2_codes, w2_scales = quantise(w2_dealt[:], N, "w2")
+        for h in range(halves):
+            nc.vector.tensor_copy(xw[1][h][:], xw_all[1][:].indirect(half_of(offs_list, h)))
 
         out_codes = keep.tile([P, S], U32, name="out_codes", align_bytes=64)
         out_scales = keep.tile([P, S], U8, name="out_scales", align_bytes=64)
@@ -182,113 +175,88 @@ def tile_picked_yddpm_silu_po_kernel(
         result = {}
         rounded = {}
 
-        def weave(ap):
-            return ap.rearrange("p (c i t) -> p c t i", i=4, t=PACK)
+        def words_order(ap):
+            return ap.rearrange("p (c i t) -> p c t i", i=LINE, t=PACK)
 
-        def planes(ap):
-            return ap.rearrange("p t (c i) -> p c t i", i=4)
+        def slots_order(ap):
+            return ap.rearrange("p t (c i) -> p c t i", i=LINE)
 
         def layer1(c):
             width = WIDTHS[c]
             h, c0 = divmod(starts[c], HALF)
-            e, e0 = divmod(starts[c], TEMB)
+            cols = slice(c0, c0 + width)
             per_bank = BANK // width
-            pre = ring.tile([P, PACK, width], F32, name="pre", bufs=2)
+            pre = ring.tile([P, PACK, width], F32, name="pre")
             for t0 in range(0, PACK, per_bank):
                 acc = psum.tile([P, per_bank, width], F32, name="acc", bufs=3)
                 for t in range(t0, t0 + per_bank):
-                    for o in reversed(range(passes)):
+                    for o in reversed(range(PASSES)):
                         codes, scales = w1_q[o]
                         nc.tensor.matmul_mx(
                             out=acc[:, t - t0, :],
                             lhsT=codes[:, t * P : (t + 1) * P].bitcast(FP8X4),
                             lhsT_scale=scales[:, t * P : (t + 1) * P],
-                            rhs=xw[o][h][:, c0 : c0 + width].bitcast(FP8X4),
+                            rhs=xw[o][h][:, cols].bitcast(FP8X4),
                             rhs_scale=xs[4 * o :, starts[c] : starts[c] + width],
-                            start=(o == passes - 1),
+                            start=(o == PASSES - 1),
                             stop=(o == 0),
                         )
-                nc.vector.tensor_tensor(
-                    pre[:, t0 : t0 + per_bank, :], acc[:], temb_of[e][:, t0 : t0 + per_bank, e0 : e0 + width], ALU.add
-                )
+                slots = slice(t0, t0 + per_bank)
+                nc.vector.tensor_tensor(pre[:, slots, :], acc[:], temb_of[h][:, slots, cols], ALU.add)
             hidden[c] = ring.tile([P, width * PACK], BF16, name="hidden", bufs=3, align_bytes=64)
-            nc.scalar.activation(weave(hidden[c][:]), planes(pre[:]), ACT.Silu)
+            nc.scalar.activation(words_order(hidden[c][:]), slots_order(pre[:]), ACT.Silu)
 
         def layer2(c):
             width = WIDTHS[c]
-            h_codes, h_scales = quantise(hidden[c][:], width, "h%d" % c, keep)
-            final = ring.tile([P, PACK, width], F32, name="final", bufs=5)
-            rounded[c] = ring.tile([P, width * PACK], BF16, name="rounded", bufs=4, align_bytes=64)
+            h_codes, h_scales = quantise(hidden[c][:], width, "h%d" % c)
+            result[c] = ring.tile([P, PACK, width], F32, name="result", bufs=chunks)
+            rounded[c] = ring.tile([P, width * PACK], BF16, name="rounded", bufs=chunks - 1, align_bytes=64)
             for b in range(width // P):
                 g = starts[c] // P + b
-                toks = slice(b * P, (b + 1) * P)
+                latents = slice(b * P, (b + 1) * P)
                 if g not in signals:
-                    signal(g)
+                    scale_lat(g, "turn", 1)
                 noise = psum.tile([P, N], F32, name="noise", bufs=2)
                 nc.tensor.matmul_mx(
                     out=noise[:],
-                    lhsT=h_codes[:, toks].bitcast(FP8X4),
-                    lhsT_scale=h_scales[:, toks],
+                    lhsT=h_codes[:, latents].bitcast(FP8X4),
+                    lhsT_scale=h_scales[:, latents],
                     rhs=w2_codes[:].bitcast(FP8X4),
                     rhs_scale=w2_scales[:],
                     start=True,
                     stop=True,
                 )
-                minus = ring.tile([P, N], F32, name="minus", bufs=4)
+                negative = ring.tile([P, N], F32, name="negative", bufs=4)
                 back = psum.tile([P, PACK, P], F32, name="back", bufs=2)
-                if g in ON_TENSOR:
-                    sign = 1.0
-                    nc.scalar.activation(minus[:], noise[:], ACT.Copy, scale=minus_cn[:, g : g + 1])
-                    for t in range(PACK):
-                        for part, first in ((minus, True), (signals[g], False)):
-                            nc.tensor.matmul(
-                                back[:, t, :], part[:, t * P : (t + 1) * P], ident[:],
-                                start=first, stop=not first, is_transpose=True,
-                            )
-                else:
-                    sign = -1.0
-                    nc.vector.scalar_tensor_tensor(
-                        minus[:], noise[:], coef[:, g, 1:2], signals[g][:], ALU.mult, ALU.subtract
-                    )
-                    for t in range(PACK):
-                        nc.tensor.transpose(back[:, t, :], minus[:, t * P : (t + 1) * P], ident[:])
-                if g in FINAL_ON_VECTOR:
-                    nc.vector.tensor_scalar(final[:, :, toks], back[:], sign, None, ALU.mult)
-                else:
-                    nc.scalar.activation(final[:, :, toks], back[:], ACT.Copy, scale=sign)
-                if c not in ROUND_ON_VECTOR and c not in ROUND_ON_GPSIMD:
-                    nc.scalar.activation(
-                        weave(rounded[c][:, b * P * PACK : (b + 1) * P * PACK]), planes(back[:]), ACT.Copy, scale=sign
-                    )
-                if c in ROUND_ON_GPSIMD:
-                    nc.gpsimd.tensor_scalar(
-                        weave(rounded[c][:, b * P * PACK : (b + 1) * P * PACK]), planes(final[:, :, toks]), 1.0, 0.0, ALU.mult, ALU.add
-                    )
-            (nc.scalar if c >= chunks - 1 else nc.sync).dma_start(
-                out=out_0[:, starts[c] : starts[c] + width].rearrange("(p t) s -> p t s", t=PACK), in_=final[:]
+                nc.vector.scalar_tensor_tensor(
+                    negative[:], noise[:], coef[:, g, 1:2], signals[g][:], ALU.mult, ALU.subtract
+                )
+                for t in range(PACK):
+                    nc.tensor.transpose(back[:, t, :], negative[:, t * P : (t + 1) * P], ident[:])
+                nc.scalar.activation(result[c][:, :, latents], back[:], ACT.Copy, scale=-1.0)
+            queue = nc.scalar if c == chunks - 1 else nc.sync
+            queue.dma_start(
+                out=out_0[:, starts[c] : starts[c] + width].rearrange("(p t) s -> p t s", t=PACK), in_=result[c][:]
             )
-            result[c] = final
 
         def hand_on(c):
             cols = slice(starts[c], starts[c] + WIDTHS[c])
-            if c in ROUND_ON_VECTOR:
-                nc.vector.tensor_copy(weave(rounded[c][:]), planes(result[c][:]))
+            nc.vector.tensor_copy(words_order(rounded[c][:]), slots_order(result[c][:]))
             nc.vector.quantize_mx(out=out_codes[:, cols].bitcast(FP8X4), scales=out_scales[:, cols], in_=rounded[c][:])
-            if c in STORE_AFTER:
-                done = slice(STORE_AFTER[c], cols.stop)
+            if c in STORE_FROM:
+                done = slice(STORE_FROM[c], cols.stop)
                 nc.sync.dma_start(
-                    out=out_1[0].rearrange("p c r -> p (c r)").bitcast(I32)[:, done], in_=out_codes[:, done].bitcast(I32)
+                    out=out_1[0].rearrange("p c r -> p (c r)").bitcast(I32)[:, done],
+                    in_=out_codes[:, done].bitcast(I32),
                 )
 
-        for s in range(chunks + 2):
-
-            if s < chunks:
-                layer1(s)
-            if 0 <= s < chunks + 0:
-                layer2(s - 0)
-            if s >= 2:
-                hand_on(s - 2)
-        for q in range(4):
+        for c in range(chunks + HAND_ON_LAG):
+            if c < chunks:
+                layer1(c)
+                layer2(c)
+            if c >= HAND_ON_LAG:
+                hand_on(c - HAND_ON_LAG)
+        for r in range(4):
             nc.sync.dma_start(
-                out=out_2[0, q : 16 : 4, :].bitcast(I32), in_=out_scales[q : P : 32, :].bitcast(I32)
+                out=out_2[0, r:SCALE_ROWS:4, :].bitcast(I32), in_=out_scales[r:P:QUADRANT, :].bitcast(I32)
             )

@@ -22,14 +22,22 @@ K_PASS = P * PACK
 PASSES = K // K_PASS
 QUADRANT = 32
 SCALE_ROWS = K_PASS // 32
-BANK = 512
 HALF = S // 2
 LINE = 4
+GROUPS = S // P
 TEMB_WINDOW = 704
 COEF_WINDOW = 528
-WIDTHS = [256, 256, 256, 128, 128]
-STORE_FROM = {1: 0, 2: 512, 4: 768}
-HAND_ON_LAG = 2
+LOAD_ORDER = ["x0", "w1a", "w1b", "w2"]
+LAT_PIECES = 4
+LAT_WIDTH = S // LAT_PIECES
+LAG_B, LAG_C, LAG_D = 1, 2, 8
+ACC_BANKS, TURN_BANKS, BACK_BANKS = 3, 1, 3
+LAG_SIGNAL = 0
+ROUND_ON_VECTOR = (0, 1, 7)
+STORE_FROM = {1: 0, 3: 256, 5: 512, 7: 768}
+TEMB_WIDTH = 512
+TEMB_BUFS = 2
+OUT_WIDTH = 256
 
 
 def tile_picked_yddpm_silu_po_kernel(
@@ -37,8 +45,6 @@ def tile_picked_yddpm_silu_po_kernel(
 ):
     nc = tc.nc
     halves = S // HALF
-    chunks = len(WIDTHS)
-    starts = [sum(WIDTHS[:c]) for c in range(chunks)]
 
     with ExitStack() as ctx:
         keep = ctx.enter_context(tc.tile_pool(name="keep", bufs=1))
@@ -49,14 +55,15 @@ def tile_picked_yddpm_silu_po_kernel(
         offs_list = keep.tile([P, S // 16], U16, name="offs_list")
         temb_rows = keep.tile([P, (PACK - 1) * R + TEMB_WINDOW], F32, name="temb_rows")
         coef_rows = keep.tile([P, COEF_WINDOW], F32, name="coef_rows")
-        xs_all = keep.tile([P, T], U8, name="xs_all", align_bytes=64)
-        xw_all = [keep.tile([P, T], U32, name="xw_all%d" % o, align_bytes=64) for o in range(PASSES)]
-        w1_raw = [ring.tile([P, PACK, H], F32, name="w1_raw%d" % o, tag="raw") for o in range(PASSES)]
-        w2_raw = ring.tile([P, PACK, N], F32, name="w2_raw", tag="raw")
-        lat_rows = [
-            keep.tile([P, PACK, HALF], F32, name="lat_rows0"),
-            ring.tile([P, PACK, HALF], F32, name="lat_rows1", tag="raw"),
+        xs_all = keep.tile([P, T], U8, name="xs_all", tag="late", align_bytes=64)
+        xw_all = [
+            keep.tile([P, T], U32, name="xw_all0", align_bytes=64),
+            keep.tile([P, T], U32, name="xw_all1", tag="late", align_bytes=64),
         ]
+        w1_raw = [ring.tile([P, PACK, H], F32, name="w1_raw%d" % o, tag="raw") for o in range(PASSES)]
+        w2_raw = keep.tile([P, PACK, N], F32, name="w2_raw")
+        lat_halves = [ring.tile([P, LAT_PIECES // 2, PACK, LAT_WIDTH], F32, name="lat_rows%d" % q, tag="raw") for q in range(2)]
+        lat_rows = [lat_halves[q // (LAT_PIECES // 2)][:, q % (LAT_PIECES // 2)] for q in range(LAT_PIECES)]
         ident = keep.tile([P, P], F32, name="ident")
 
         scale_rows = PASSES * SCALE_ROWS
@@ -82,38 +89,52 @@ def tile_picked_yddpm_silu_po_kernel(
         nc.sync.dma_start(out=coef_rows[: P // 2, :R], in_=csig[: P // 2, :])
         nc.sync.dma_start(out=coef_rows[P // 2 :, :R], in_=cnoise[P // 2 :, :])
         nc.sync.dma_start(out=temb_rows[:, : PACK * R], in_=temb.rearrange("(p t) r -> p (t r)", t=PACK))
-        load_slots(lat_rows[0], lat[:, :HALF])
-        load_words(0)
-        for o in range(PASSES):
-            load_slots(w1_raw[o], w1[o * K_PASS : (o + 1) * K_PASS, :])
-        load_words(1)
+        for what in LOAD_ORDER:
+            if what[0] == "x":
+                load_words(int(what[1]))
+            elif what == "w1a":
+                load_slots(w1_raw[0], w1[:K_PASS, :])
+            elif what == "w1b":
+                load_slots(w1_raw[1], w1[K_PASS:, :])
+            else:
+                load_slots(w2_raw, w2)
 
-        def half_of(offsets, h):
-            return offsets[:, h * HALF // 16 : (h + 1) * HALF // 16]
+        def entries(offsets, first, count):
+            return offsets[:, first // 16 : (first + count) // 16]
 
         temb_of = {}
-        coef_of = [keep.tile([P, HALF], F32, name="coef_of%d" % h) for h in range(halves)]
-        coef = keep.tile([P, S // P, 2], F32, name="coef")
-        xs = keep.tile([P, S], U8, name="xs", align_bytes=64)
+        coef_of = keep.tile([P, S], F32, name="coef_of")
+        coef = keep.tile([P, GROUPS, 2], F32, name="coef")
+        xs = [keep.tile([P, S], U8, name="xs%d" % o, align_bytes=64) for o in range(PASSES)]
         xw_first = keep.tile([P, S], U32, name="xw_first", align_bytes=64)
         xw = [
             [xw_first[:, h * HALF : (h + 1) * HALF] for h in range(halves)],
             [keep.tile([P, HALF], U32, name="xw1_%d" % h, align_bytes=64) for h in range(halves)],
         ]
 
-        def gather_temb(h):
-            temb_of[h] = ring.tile([P, PACK, HALF], F32, name="temb_of")
+        def gather_temb(c):
+            temb_of[c] = ring.tile([P, PACK, TEMB_WIDTH], F32, name="temb_of", bufs=TEMB_BUFS)
             for t in range(PACK):
                 window = temb_rows[:, t * R : t * R + TEMB_WINDOW]
-                nc.vector.tensor_copy(temb_of[h][:, t, :], window.indirect(half_of(step_list, h)))
+                nc.vector.tensor_copy(temb_of[c][:, t, :], window.indirect(entries(step_list, c * TEMB_WIDTH, TEMB_WIDTH)))
 
         def gather_coef(h):
             groups = HALF // P
-            nc.vector.tensor_copy(coef_of[h][:], coef_rows[:].indirect(half_of(step_list, h)))
-            bank = psum.tile([P, groups, P], F32, name="turn")
+            nc.vector.tensor_copy(coef_of[:, h * HALF : (h + 1) * HALF], coef_rows[:].indirect(entries(step_list, h * HALF, HALF)))
+            bank = psum.tile([P, groups, P], F32, name="back", bufs=BACK_BANKS)
             for b in range(groups):
-                nc.tensor.transpose(bank[:, b, :], coef_of[h][:, b * P : (b + 1) * P], ident[:])
+                g = h * groups + b
+                nc.tensor.transpose(bank[:, b, :], coef_of[:, g * P : (g + 1) * P], ident[:])
             nc.scalar.copy(coef[:, h * groups : (h + 1) * groups, :], bank[:, :, 0 : P : P // 2])
+
+        csig_of = keep.tile([P, S], F32, name="csig_of")
+
+        def spread_csig(h):
+            groups = HALF // P
+            bank = psum.tile([P, groups, P], F32, name="back", bufs=BACK_BANKS)
+            for b in range(groups):
+                nc.tensor.transpose(bank[:, b, :], coef[:, h * groups + b, 0:1].to_broadcast([P, P]), ident[:])
+            nc.scalar.copy(csig_of[:, h * HALF : (h + 1) * HALF], bank[:].rearrange("p b j -> p (b j)"))
 
         def deal(raw, name):
             dealt = keep.tile([P, PACK * K_PASS], BF16, name=name, align_bytes=64)
@@ -129,51 +150,39 @@ def tile_picked_yddpm_silu_po_kernel(
             nc.vector.quantize_mx(out=codes[:].bitcast(FP8X4), scales=scales[:], in_=values)
             return codes, scales
 
-        signals = {}
-
-        def scale_lat(g, bank_tag, banks):
-            h, c0 = divmod(g * P, HALF)
-            turned = psum.tile([P, PACK, P], F32, name=bank_tag, bufs=banks)
-            for t in range(PACK):
-                nc.tensor.transpose(turned[:, t, :], lat_rows[h][:, t, c0 : c0 + P], ident[:])
-            signals[g] = ring.tile([P, N], F32, name="signal", bufs=S // P)
-            nc.scalar.activation(
-                signals[g][:], turned[:].rearrange("p t m -> p (t m)"), ACT.Copy, scale=coef[:, g, 0:1]
-            )
-
         warm = keep.tile([P, 1], F32, name="warm")
         nc.scalar.activation(warm[:], ident[:, 0:1], ACT.Silu)
 
         picked = keep.tile([P, S], U8, name="picked", align_bytes=64)
-        nc.gpsimd.memset(xs[:].bitcast(I32), 0)
+        for o in range(PASSES):
+            nc.gpsimd.memset(xs[o][:].bitcast(I32), 0)
         nc.vector.tensor_copy(picked[:], xs_all[:].indirect(offs_list[:]))
         for o in range(PASSES):
+            if o == PASSES - 1:
+                load_words(o)
             for q in range(P // QUADRANT):
-                to_row, from_row = QUADRANT * q + 4 * o, SCALE_ROWS * o + 4 * q
-                nc.gpsimd.dma_start(
-                    out=xs[to_row : to_row + 4, :].bitcast(I32), in_=picked[from_row : from_row + 4, :].bitcast(I32)
+                to_row, from_row = QUADRANT * q, SCALE_ROWS * o + 4 * q
+                nc.sync.dma_start(
+                    out=xs[o][to_row : to_row + 4, :].bitcast(I32), in_=picked[from_row : from_row + 4, :].bitcast(I32)
                 )
         for h in range(halves):
             gather_coef(h)
+        for h in range(halves):
+            spread_csig(h)
         w1_dealt = [deal(w1_raw[o], "w1_dealt%d" % o) for o in range(PASSES)]
-        load_slots(w2_raw, w2)
-        load_slots(lat_rows[1], lat[:, HALF:])
+        for q in range(LAT_PIECES):
+            load_slots(lat_rows[q], lat[:, q * LAT_WIDTH : (q + 1) * LAT_WIDTH])
         w2_dealt = deal(w2_raw, "w2_dealt")
-        for g in range(HALF // P):
-            scale_lat(g, "back", 2)
-        gather_temb(0)
+        for c in range(min(TEMB_BUFS, S // TEMB_WIDTH)):
+            gather_temb(c)
         nc.vector.tensor_copy(xw_first[:], xw_all[0][:].indirect(offs_list[:]))
         w1_q = [quantise(w1_dealt[o][:], H, "w1_%d" % o) for o in range(PASSES)]
-        gather_temb(1)
         w2_codes, w2_scales = quantise(w2_dealt[:], N, "w2")
-        for h in range(halves):
-            nc.vector.tensor_copy(xw[1][h][:], xw_all[1][:].indirect(half_of(offs_list, h)))
+        nc.vector.tensor_copy(xw[1][0][:], xw_all[1][:].indirect(entries(offs_list, 0, HALF)))
 
         out_codes = keep.tile([P, S], U32, name="out_codes", align_bytes=64)
         out_scales = keep.tile([P, S], U8, name="out_scales", align_bytes=64)
-        hidden = {}
-        result = {}
-        rounded = {}
+        hidden, noise, signal, result, rounded = {}, {}, {}, {}, {}
 
         def words_order(ap):
             return ap.rearrange("p (c i t) -> p c t i", i=LINE, t=PACK)
@@ -181,82 +190,95 @@ def tile_picked_yddpm_silu_po_kernel(
         def slots_order(ap):
             return ap.rearrange("p t (c i) -> p c t i", i=LINE)
 
-        def layer1(c):
-            width = WIDTHS[c]
-            h, c0 = divmod(starts[c], HALF)
-            cols = slice(c0, c0 + width)
-            per_bank = BANK // width
-            pre = ring.tile([P, PACK, width], F32, name="pre")
-            for t0 in range(0, PACK, per_bank):
-                acc = psum.tile([P, per_bank, width], F32, name="acc", bufs=3)
-                for t in range(t0, t0 + per_bank):
-                    for o in reversed(range(PASSES)):
-                        codes, scales = w1_q[o]
-                        nc.tensor.matmul_mx(
-                            out=acc[:, t - t0, :],
-                            lhsT=codes[:, t * P : (t + 1) * P].bitcast(FP8X4),
-                            lhsT_scale=scales[:, t * P : (t + 1) * P],
-                            rhs=xw[o][h][:, cols].bitcast(FP8X4),
-                            rhs_scale=xs[4 * o :, starts[c] : starts[c] + width],
-                            start=(o == PASSES - 1),
-                            stop=(o == 0),
-                        )
-                slots = slice(t0, t0 + per_bank)
-                nc.vector.tensor_tensor(pre[:, slots, :], acc[:], temb_of[h][:, slots, cols], ALU.add)
-            hidden[c] = ring.tile([P, width * PACK], BF16, name="hidden", bufs=3, align_bytes=64)
-            nc.scalar.activation(words_order(hidden[c][:]), slots_order(pre[:]), ACT.Silu)
-
-        def layer2(c):
-            width = WIDTHS[c]
-            h_codes, h_scales = quantise(hidden[c][:], width, "h%d" % c)
-            result[c] = ring.tile([P, PACK, width], F32, name="result", bufs=chunks)
-            rounded[c] = ring.tile([P, width * PACK], BF16, name="rounded", bufs=chunks - 1, align_bytes=64)
-            for b in range(width // P):
-                g = starts[c] // P + b
-                latents = slice(b * P, (b + 1) * P)
-                if g not in signals:
-                    scale_lat(g, "turn", 1)
-                noise = psum.tile([P, N], F32, name="noise", bufs=2)
-                nc.tensor.matmul_mx(
-                    out=noise[:],
-                    lhsT=h_codes[:, latents].bitcast(FP8X4),
-                    lhsT_scale=h_scales[:, latents],
-                    rhs=w2_codes[:].bitcast(FP8X4),
-                    rhs_scale=w2_scales[:],
-                    start=True,
-                    stop=True,
-                )
-                negative = ring.tile([P, N], F32, name="negative", bufs=4)
-                back = psum.tile([P, PACK, P], F32, name="back", bufs=2)
-                nc.vector.scalar_tensor_tensor(
-                    negative[:], noise[:], coef[:, g, 1:2], signals[g][:], ALU.mult, ALU.subtract
-                )
+        def stage_a(g):
+            h, c0 = divmod(g * P, HALF)
+            c, e0 = divmod(g * P, TEMB_WIDTH)
+            acc = psum.tile([P, PACK, P], F32, name="acc", bufs=ACC_BANKS)
+            for o in range(PASSES):
+                codes, scales = w1_q[o]
                 for t in range(PACK):
-                    nc.tensor.transpose(back[:, t, :], negative[:, t * P : (t + 1) * P], ident[:])
-                nc.scalar.activation(result[c][:, :, latents], back[:], ACT.Copy, scale=-1.0)
-            queue = nc.scalar if c == chunks - 1 else nc.sync
-            queue.dma_start(
-                out=out_0[:, starts[c] : starts[c] + width].rearrange("(p t) s -> p t s", t=PACK), in_=result[c][:]
+                    nc.tensor.matmul_mx(
+                        out=acc[:, t, :],
+                        lhsT=codes[:, t * P : (t + 1) * P].bitcast(FP8X4),
+                        lhsT_scale=scales[:, t * P : (t + 1) * P],
+                        rhs=xw[o][h][:, c0 : c0 + P].bitcast(FP8X4),
+                        rhs_scale=xs[o][:, g * P : (g + 1) * P],
+                        start=(o == 0 and t == 0),
+                        stop=(o == PASSES - 1 and t == PACK - 1),
+                    )
+            pre = ring.tile([P, PACK, P], F32, name="pre", bufs=3)
+            nc.vector.tensor_tensor(pre[:], acc[:], temb_of[c][:, :, e0 : e0 + P], ALU.add)
+            hidden[g] = ring.tile([P, P * PACK], BF16, name="hidden", bufs=GROUPS, align_bytes=64)
+            nc.scalar.activation(words_order(hidden[g][:]), slots_order(pre[:]), ACT.Silu)
+            if g == 0:
+                nc.vector.tensor_copy(xw[1][1][:], xw_all[1][:].indirect(entries(offs_list, HALF, HALF)))
+            if e0 + P == TEMB_WIDTH and (c + TEMB_BUFS) * TEMB_WIDTH < S:
+                gather_temb(c + TEMB_BUFS)
+
+        def scale_lat(g):
+            q, c0 = divmod(g * P, LAT_WIDTH)
+            signal[g] = ring.tile([P, PACK, P], F32, name="signal", bufs=GROUPS)
+            for t0 in range(0, PACK, 2):
+                slots = slice(t0, t0 + 2)
+                factor = csig_of[:, g * P : (g + 1) * P].unsqueeze(1).to_broadcast([P, 2, P])
+                nc.gpsimd.tensor_tensor(signal[g][:, slots, :], lat_rows[q][:, slots, c0 : c0 + P], factor, ALU.mult)
+
+        def stage_b(g):
+            h_codes, h_scales = quantise(hidden[g][:], P, "h%d" % g)
+            scale_lat(g)
+            noise[g] = psum.tile([P, N], F32, name="noise", bufs=2)
+            nc.tensor.matmul_mx(
+                out=noise[g][:],
+                lhsT=h_codes[:].bitcast(FP8X4),
+                lhsT_scale=h_scales[:],
+                rhs=w2_codes[:].bitcast(FP8X4),
+                rhs_scale=w2_scales[:],
+                start=True,
+                stop=True,
             )
 
-        def hand_on(c):
-            cols = slice(starts[c], starts[c] + WIDTHS[c])
-            nc.vector.tensor_copy(words_order(rounded[c][:]), slots_order(result[c][:]))
-            nc.vector.quantize_mx(out=out_codes[:, cols].bitcast(FP8X4), scales=out_scales[:, cols], in_=rounded[c][:])
-            if c in STORE_FROM:
-                done = slice(STORE_FROM[c], cols.stop)
+        backs = {}
+
+        def stage_c(g):
+            c, c0 = divmod(g * P, OUT_WIDTH)
+            negative = ring.tile([P, N], F32, name="negative", bufs=3)
+            back = psum.tile([P, PACK, P], F32, name="back", bufs=BACK_BANKS)
+            nc.scalar.activation(negative[:], noise[g][:], ACT.Copy, scale=coef[:, g, 1:2])
+            for t in range(PACK):
+                nc.tensor.transpose(back[:, t, :], negative[:, t * P : (t + 1) * P], ident[:])
+            if c0 == 0:
+                result[c] = ring.tile([P, PACK, OUT_WIDTH], F32, name="result", bufs=S // OUT_WIDTH)
+            rounded[g] = ring.tile([P, P * PACK], BF16, name="rounded", bufs=GROUPS, align_bytes=64)
+            nc.vector.tensor_tensor(result[c][:, :, c0 : c0 + P], signal[g][:], back[:], ALU.subtract)
+            last = g >= GROUPS - 2
+            if last or c0 + P == OUT_WIDTH:
+                cols = slice(c0, c0 + P) if last else slice(0, OUT_WIDTH)
+                nc.sync.dma_start(
+                    out=out_0[:, c * OUT_WIDTH + cols.start : c * OUT_WIDTH + cols.stop].rearrange("(p t) s -> p t s", t=PACK),
+                    in_=result[c][:, :, cols],
+                )
+
+        def stage_d(g):
+            c, c0 = divmod(g * P, OUT_WIDTH)
+            cols = slice(g * P, (g + 1) * P)
+            if g not in ROUND_ON_VECTOR:
+                nc.scalar.copy(words_order(rounded[g][:]), slots_order(result[c][:, :, c0 : c0 + P]))
+            else:
+                nc.vector.tensor_copy(words_order(rounded[g][:]), slots_order(result[c][:, :, c0 : c0 + P]))
+            nc.vector.quantize_mx(out=out_codes[:, cols].bitcast(FP8X4), scales=out_scales[:, cols], in_=rounded[g][:])
+            if g in STORE_FROM:
+                done = slice(STORE_FROM[g], cols.stop)
                 nc.sync.dma_start(
                     out=out_1[0].rearrange("p c r -> p (c r)").bitcast(I32)[:, done],
                     in_=out_codes[:, done].bitcast(I32),
                 )
 
-        for c in range(chunks + HAND_ON_LAG):
-            if c < chunks:
-                layer1(c)
-                layer2(c)
-            if c >= HAND_ON_LAG:
-                hand_on(c - HAND_ON_LAG)
+        for s in range(GROUPS + LAG_D):
+            for stage, lag in ((stage_a, 0), (stage_b, LAG_B), (stage_c, LAG_C), (stage_d, LAG_D)):
+                if 0 <= s - lag < GROUPS:
+                    stage(s - lag)
         for r in range(4):
-            nc.sync.dma_start(
+            queue = nc.scalar
+            queue.dma_start(
                 out=out_2[0, r:SCALE_ROWS:4, :].bitcast(I32), in_=out_scales[r:P:QUADRANT, :].bitcast(I32)
             )

@@ -66,12 +66,11 @@ def tile_picked_yddpm_silu_po_kernel(
         lat_rows = [lat_halves[q // (LAT_PIECES // 2)][:, q % (LAT_PIECES // 2)] for q in range(LAT_PIECES)]
         ident = keep.tile([P, P], F32, name="ident")
 
-        scale_rows = PASSES * SCALE_ROWS
-        nc.gpsimd.memset(xs_all[scale_rows : P // 2, :].bitcast(I32), 0)
-        nc.vector.memset(xs_all[P // 2 :, :].bitcast(I32), 0)
+        first_row = P - PASSES * SCALE_ROWS
+        make_identity(nc, ident[:])
+        nc.vector.memset(xs_all[:first_row, :].bitcast(I32), 0)
         nc.vector.memset(coef_rows[:, R:], 0.0)
         nc.vector.memset(temb_rows[:, PACK * R :], 0.0)
-        make_identity(nc, ident[:])
 
         def load_words(o):
             nc.sync.dma_start(
@@ -83,7 +82,7 @@ def tile_picked_yddpm_silu_po_kernel(
 
         nc.sync.dma_start(offs_list[:], offs)
         nc.sync.dma_start(
-            out=xs_all[:scale_rows, :].bitcast(I32), in_=x_scales.rearrange("o q c -> (o q) c").bitcast(I32)
+            out=xs_all[first_row:, :].bitcast(I32), in_=x_scales.rearrange("o q c -> (o q) c").bitcast(I32)
         )
         nc.sync.dma_start(step_list[:], step)
         nc.sync.dma_start(out=coef_rows[: P // 2, :R], in_=csig[: P // 2, :])
@@ -155,13 +154,13 @@ def tile_picked_yddpm_silu_po_kernel(
 
         picked = keep.tile([P, S], U8, name="picked", align_bytes=64)
         for o in range(PASSES):
-            nc.gpsimd.memset(xs[o][:].bitcast(I32), 0)
+            nc.vector.memset(xs[o][:].bitcast(I32), 0)
         nc.vector.tensor_copy(picked[:], xs_all[:].indirect(offs_list[:]))
         for o in range(PASSES):
             if o == PASSES - 1:
                 load_words(o)
             for q in range(P // QUADRANT):
-                to_row, from_row = QUADRANT * q, SCALE_ROWS * o + 4 * q
+                to_row, from_row = QUADRANT * q, first_row + SCALE_ROWS * o + 4 * q
                 nc.sync.dma_start(
                     out=xs[o][to_row : to_row + 4, :].bitcast(I32), in_=picked[from_row : from_row + 4, :].bitcast(I32)
                 )

@@ -28,13 +28,13 @@ GROUPS = S // P
 TEMB_WINDOW = 704
 COEF_WINDOW = 528
 LOAD_ORDER = ["x0", "w1a", "w1b", "w2"]
-LAT_PIECES = 4
+LAT_PIECES = 2
 LAT_WIDTH = S // LAT_PIECES
 LAG_B, LAG_C, LAG_D = 1, 2, 8
 ACC_BANKS, TURN_BANKS, BACK_BANKS = 3, 1, 3
 LAG_SIGNAL = 0
 ROUND_ON_VECTOR = (0, 1, 7)
-STORE_FROM = {1: 0, 3: 256, 5: 512, 7: 768}
+STORE_FROM = {3: 0, 5: 512, 7: 768}
 TEMB_WIDTH = 512
 TEMB_BUFS = 2
 OUT_WIDTH = 256
@@ -206,7 +206,7 @@ def tile_picked_yddpm_silu_po_kernel(
                         stop=(o == PASSES - 1 and t == PACK - 1),
                     )
             pre = ring.tile([P, PACK, P], F32, name="pre", bufs=3)
-            nc.vector.tensor_tensor(pre[:], acc[:], temb_of[c][:, :, e0 : e0 + P], ALU.add)
+            nc.vector.tensor_tensor(pre[:], temb_of[c][:, :, e0 : e0 + P], acc[:], ALU.add)
             hidden[g] = ring.tile([P, P * PACK], BF16, name="hidden", bufs=GROUPS, align_bytes=64)
             nc.scalar.activation(words_order(hidden[g][:]), slots_order(pre[:]), ACT.Silu)
             if g == 0:
@@ -277,7 +277,6 @@ def tile_picked_yddpm_silu_po_kernel(
                 if 0 <= s - lag < GROUPS:
                     stage(s - lag)
         for r in range(4):
-            queue = nc.scalar
-            queue.dma_start(
+            nc.sync.dma_start(
                 out=out_2[0, r:SCALE_ROWS:4, :].bitcast(I32), in_=out_scales[r:P:QUADRANT, :].bitcast(I32)
             )

@@ -25,19 +25,20 @@ SCALE_ROWS = K_PASS // 32
 HALF = S // 2
 LINE = 4
 GROUPS = S // P
-TEMB_WINDOW = 704
+TEMB_WINDOW = 1376
 COEF_WINDOW = 528
-LOAD_ORDER = ["x0", "w1a", "w1b", "w2"]
-LAT_PIECES = 2
+W2_HALF = N // 2
+LAT_PIECES = 4
 LAT_WIDTH = S // LAT_PIECES
-LAG_B, LAG_C, LAG_D = 1, 2, 8
-ACC_BANKS, TURN_BANKS, BACK_BANKS = 3, 1, 3
-LAG_SIGNAL = 0
-ROUND_ON_VECTOR = (0, 1, 7)
-STORE_FROM = {3: 0, 5: 512, 7: 768}
-TEMB_WIDTH = 512
-TEMB_BUFS = 2
 OUT_WIDTH = 256
+LAG_SECOND, LAG_COMBINE, LAG_HAND_ON = 1, 2, 8
+ACC_BANKS, BACK_BANKS = 3, 3
+ROUND_ON_VECTOR = (1, 7)
+STORE_FROM = {3: 0, 5: 512, 7: 768}
+EARLY_LAT = 1
+EARLY_W2 = 1
+TURNED = (0, 1)
+POOL_SLOTS = 2
 
 
 def tile_picked_yddpm_silu_po_kernel(
@@ -54,107 +55,63 @@ def tile_picked_yddpm_silu_po_kernel(
         step_list = keep.tile([P, S // 16], U16, name="step_list")
         offs_list = keep.tile([P, S // 16], U16, name="offs_list")
         temb_rows = keep.tile([P, (PACK - 1) * R + TEMB_WINDOW], F32, name="temb_rows")
-        coef_rows = keep.tile([P, COEF_WINDOW], F32, name="coef_rows")
-        xs_all = keep.tile([P, T], U8, name="xs_all", tag="late", align_bytes=64)
+        coef_rows = keep.tile([P, COEF_WINDOW], F32, name="coef_rows", tag="w2", align_bytes=64)
+        xs_all = keep.tile([P, T], U8, name="xs_all", tag="late_words", align_bytes=64)
         xw_all = [
             keep.tile([P, T], U32, name="xw_all0", align_bytes=64),
-            keep.tile([P, T], U32, name="xw_all1", tag="late", align_bytes=64),
+            keep.tile([P, T], U32, name="xw_all1", tag="late_words", align_bytes=64),
         ]
         w1_raw = [ring.tile([P, PACK, H], F32, name="w1_raw%d" % o, tag="raw") for o in range(PASSES)]
-        w2_raw = keep.tile([P, PACK, N], F32, name="w2_raw")
-        lat_halves = [ring.tile([P, LAT_PIECES // 2, PACK, LAT_WIDTH], F32, name="lat_rows%d" % q, tag="raw") for q in range(2)]
-        lat_rows = [lat_halves[q // (LAT_PIECES // 2)][:, q % (LAT_PIECES // 2)] for q in range(LAT_PIECES)]
+        w2_raw = [keep.tile([P, PACK, W2_HALF], F32, name="w2_raw%d" % u)[:] for u in range(EARLY_W2)]
+        w2_late = keep.tile([P, 2 - EARLY_W2, PACK, W2_HALF], F32, name="w2_late", tag="w2", align_bytes=64)
+        w2_raw = w2_raw + [w2_late[:, u] for u in range(2 - EARLY_W2)]
+        late = LAT_PIECES - EARLY_LAT
+        lat_late = [ring.tile([P, (late + 1) // 2, PACK, LAT_WIDTH], F32, name="lat_late%d" % h, tag="raw") for h in range(2)]
+        lat_rows = [keep.tile([P, PACK, LAT_WIDTH], F32, name="lat_rows%d" % q)[:] for q in range(EARLY_LAT)]
+        lat_rows = lat_rows + [lat_late[q % 2][:, q // 2] for q in range(late)]
         ident = keep.tile([P, P], F32, name="ident")
+        xs_both = keep.tile([P, PASSES * S], U8, name="xs_both", align_bytes=64)
+        xs = [xs_both[:, o * S : (o + 1) * S] for o in range(PASSES)]
 
         first_row = P - PASSES * SCALE_ROWS
         make_identity(nc, ident[:])
         nc.vector.memset(xs_all[:first_row, :].bitcast(I32), 0)
-        nc.vector.memset(coef_rows[:, R:], 0.0)
-        nc.vector.memset(temb_rows[:, PACK * R :], 0.0)
+        nc.gpsimd.memset(coef_rows[:first_row, :R], 0.0)
+        nc.gpsimd.memset(coef_rows[:, R:], 0.0)
+        nc.gpsimd.memset(temb_rows[:, PACK * R :], 0.0)
+        nc.vector.memset(xs_both[:].bitcast(I32), 0)
 
         def load_words(o):
             nc.sync.dma_start(
                 out=xw_all[o][:].bitcast(I32), in_=x_words[o].rearrange("p c r -> p (c r)").bitcast(I32)
             )
 
-        def load_slots(tile, rows):
-            nc.sync.dma_start(out=tile[:], in_=rows.rearrange("(p t) c -> p t c", t=PACK))
+        def load_slots(slots, rows):
+            nc.sync.dma_start(out=slots, in_=rows.rearrange("(p t) c -> p t c", t=PACK))
 
         nc.sync.dma_start(offs_list[:], offs)
         nc.sync.dma_start(
             out=xs_all[first_row:, :].bitcast(I32), in_=x_scales.rearrange("o q c -> (o q) c").bitcast(I32)
         )
         nc.sync.dma_start(step_list[:], step)
-        nc.sync.dma_start(out=coef_rows[: P // 2, :R], in_=csig[: P // 2, :])
-        nc.sync.dma_start(out=coef_rows[P // 2 :, :R], in_=cnoise[P // 2 :, :])
+        nc.sync.dma_start(out=coef_rows[first_row : first_row + 16, :R], in_=csig[:16, :])
+        nc.sync.dma_start(out=coef_rows[first_row + 16 :, :R], in_=cnoise[:16, :])
         nc.sync.dma_start(out=temb_rows[:, : PACK * R], in_=temb.rearrange("(p t) r -> p (t r)", t=PACK))
-        for what in LOAD_ORDER:
-            if what[0] == "x":
-                load_words(int(what[1]))
-            elif what == "w1a":
-                load_slots(w1_raw[0], w1[:K_PASS, :])
-            elif what == "w1b":
-                load_slots(w1_raw[1], w1[K_PASS:, :])
-            else:
-                load_slots(w2_raw, w2)
+        for q in range(EARLY_LAT):
+            load_slots(lat_rows[q], lat[:, q * LAT_WIDTH : (q + 1) * LAT_WIDTH])
+        load_words(0)
+        for o in range(PASSES):
+            load_slots(w1_raw[o][:], w1[o * K_PASS : (o + 1) * K_PASS, :])
+        for u in range(EARLY_W2):
+            load_slots(w2_raw[u], w2[:, u * W2_HALF : (u + 1) * W2_HALF])
 
-        def entries(offsets, first, count):
-            return offsets[:, first // 16 : (first + count) // 16]
-
-        temb_of = {}
-        coef_of = keep.tile([P, S], F32, name="coef_of")
-        coef = keep.tile([P, GROUPS, 2], F32, name="coef")
-        xs = [keep.tile([P, S], U8, name="xs%d" % o, align_bytes=64) for o in range(PASSES)]
-        xw_first = keep.tile([P, S], U32, name="xw_first", align_bytes=64)
-        xw = [
-            [xw_first[:, h * HALF : (h + 1) * HALF] for h in range(halves)],
-            [keep.tile([P, HALF], U32, name="xw1_%d" % h, align_bytes=64) for h in range(halves)],
-        ]
-
-        def gather_temb(c):
-            temb_of[c] = ring.tile([P, PACK, TEMB_WIDTH], F32, name="temb_of", bufs=TEMB_BUFS)
-            for t in range(PACK):
-                window = temb_rows[:, t * R : t * R + TEMB_WINDOW]
-                nc.vector.tensor_copy(temb_of[c][:, t, :], window.indirect(entries(step_list, c * TEMB_WIDTH, TEMB_WIDTH)))
-
-        def gather_coef(h):
-            groups = HALF // P
-            nc.vector.tensor_copy(coef_of[:, h * HALF : (h + 1) * HALF], coef_rows[:].indirect(entries(step_list, h * HALF, HALF)))
-            bank = psum.tile([P, groups, P], F32, name="back", bufs=BACK_BANKS)
-            for b in range(groups):
-                g = h * groups + b
-                nc.tensor.transpose(bank[:, b, :], coef_of[:, g * P : (g + 1) * P], ident[:])
-            nc.scalar.copy(coef[:, h * groups : (h + 1) * groups, :], bank[:, :, 0 : P : P // 2])
-
-        csig_of = keep.tile([P, S], F32, name="csig_of")
-
-        def spread_csig(h):
-            groups = HALF // P
-            bank = psum.tile([P, groups, P], F32, name="back", bufs=BACK_BANKS)
-            for b in range(groups):
-                nc.tensor.transpose(bank[:, b, :], coef[:, h * groups + b, 0:1].to_broadcast([P, P]), ident[:])
-            nc.scalar.copy(csig_of[:, h * HALF : (h + 1) * HALF], bank[:].rearrange("p b j -> p (b j)"))
-
-        def deal(raw, name):
-            dealt = keep.tile([P, PACK * K_PASS], BF16, name=name, align_bytes=64)
-            nc.scalar.copy(
-                dealt[:].rearrange("p (t m j) -> p m t j", t=PACK, j=PACK),
-                raw[:].rearrange("p j (m t) -> p m t j", t=PACK),
-            )
-            return dealt
-
-        def quantise(values, width, name):
-            codes = keep.tile([P, width], U32, name=name + "_codes", align_bytes=64)
-            scales = keep.tile([P, width], U8, name=name + "_scales", align_bytes=64)
-            nc.vector.quantize_mx(out=codes[:].bitcast(FP8X4), scales=scales[:], in_=values)
-            return codes, scales
+        def half_of(offsets, h):
+            return offsets[:, h * HALF // 16 : (h + 1) * HALF // 16]
 
         warm = keep.tile([P, 1], F32, name="warm")
         nc.scalar.activation(warm[:], ident[:, 0:1], ACT.Silu)
 
         picked = keep.tile([P, S], U8, name="picked", align_bytes=64)
-        for o in range(PASSES):
-            nc.vector.memset(xs[o][:].bitcast(I32), 0)
         nc.vector.tensor_copy(picked[:], xs_all[:].indirect(offs_list[:]))
         for o in range(PASSES):
             if o == PASSES - 1:
@@ -164,24 +121,70 @@ def tile_picked_yddpm_silu_po_kernel(
                 nc.sync.dma_start(
                     out=xs[o][to_row : to_row + 4, :].bitcast(I32), in_=picked[from_row : from_row + 4, :].bitcast(I32)
                 )
-        for h in range(halves):
-            gather_coef(h)
-        for h in range(halves):
-            spread_csig(h)
-        w1_dealt = [deal(w1_raw[o], "w1_dealt%d" % o) for o in range(PASSES)]
-        for q in range(LAT_PIECES):
-            load_slots(lat_rows[q], lat[:, q * LAT_WIDTH : (q + 1) * LAT_WIDTH])
-        w2_dealt = deal(w2_raw, "w2_dealt")
-        for c in range(min(TEMB_BUFS, S // TEMB_WIDTH)):
-            gather_temb(c)
-        nc.vector.tensor_copy(xw_first[:], xw_all[0][:].indirect(offs_list[:]))
-        w1_q = [quantise(w1_dealt[o][:], H, "w1_%d" % o) for o in range(PASSES)]
-        w2_codes, w2_scales = quantise(w2_dealt[:], N, "w2")
-        nc.vector.tensor_copy(xw[1][0][:], xw_all[1][:].indirect(entries(offs_list, 0, HALF)))
 
-        out_codes = keep.tile([P, S], U32, name="out_codes", align_bytes=64)
-        out_scales = keep.tile([P, S], U8, name="out_scales", align_bytes=64)
-        hidden, noise, signal, result, rounded = {}, {}, {}, {}, {}
+        coef_of = keep.tile([P, S], F32, name="coef_of")
+        coef = keep.tile([P, GROUPS, 2], F32, name="coef")
+        csig_of = keep.tile([P, S], F32, name="csig_of")
+        per_half = HALF // P
+        for h in range(halves):
+            nc.vector.tensor_copy(coef_of[:, h * HALF : (h + 1) * HALF], coef_rows[:].indirect(half_of(step_list, h)))
+            bank = psum.tile([P, per_half, P], F32, name="back", bufs=BACK_BANKS)
+            for b in range(per_half):
+                g = h * per_half + b
+                nc.tensor.transpose(bank[:, b, :], coef_of[:, g * P : (g + 1) * P], ident[:])
+            nc.scalar.copy(coef[:, h * per_half : (h + 1) * per_half, :], bank[:, :, first_row : P : 16])
+        for h in range(halves):
+            bank = psum.tile([P, per_half, P], F32, name="back", bufs=BACK_BANKS)
+            for b in range(per_half):
+                nc.tensor.transpose(bank[:, b, :], coef[:, h * per_half + b, 0:1].to_broadcast([P, P]), ident[:])
+            nc.scalar.copy(csig_of[:, h * HALF : (h + 1) * HALF], bank[:].rearrange("p b j -> p (b j)"))
+
+        def deal(raw, width, name):
+            dealt = keep.tile([P, PACK * width], BF16, name=name, align_bytes=64)
+            nc.scalar.copy(
+                dealt[:].rearrange("p (t m j) -> p m t j", t=PACK, j=PACK),
+                raw.rearrange("p j (m t) -> p m t j", t=PACK),
+            )
+            return dealt
+
+        def planes(width, name):
+            codes = keep.tile([P, width], U32, name=name + "_codes", align_bytes=64)
+            scales = keep.tile([P, width], U8, name=name + "_scales", align_bytes=64)
+            return codes, scales
+
+        def quantise(codes, scales, values):
+            nc.vector.quantize_mx(out=codes.bitcast(FP8X4), scales=scales, in_=values)
+
+        w1_dealt = [deal(w1_raw[o][:], H, "w1_dealt%d" % o) for o in range(PASSES)]
+        for u in range(EARLY_W2, 2):
+            load_slots(w2_raw[u], w2[:, u * W2_HALF : (u + 1) * W2_HALF])
+        for q in range(EARLY_LAT, LAT_PIECES):
+            load_slots(lat_rows[q], lat[:, q * LAT_WIDTH : (q + 1) * LAT_WIDTH])
+        w2_dealt = [deal(w2_raw[u], W2_HALF, "w2_dealt%d" % u) for u in range(2)]
+
+        temb_of = keep.tile([P, PACK, S], F32, name="temb_of")
+        for t in range(PACK):
+            window = temb_rows[:, t * R : t * R + TEMB_WINDOW]
+            nc.vector.tensor_copy(temb_of[:, t, :], window.indirect(step_list[:]))
+        xw_first = keep.tile([P, S], U32, name="xw_first", align_bytes=64)
+        nc.vector.tensor_copy(xw_first[:], xw_all[0][:].indirect(offs_list[:]))
+        w1_q = [planes(H, "w1_%d" % o) for o in range(PASSES)]
+        for o in range(PASSES):
+            quantise(w1_q[o][0][:], w1_q[o][1][:], w1_dealt[o][:])
+        xw_last = {}
+
+        def gather_last_words(h, tag):
+            xw_last[h] = keep.tile([P, HALF], U32, name="xw_last%d" % h, tag=tag, align_bytes=64)
+            nc.vector.tensor_copy(xw_last[h][:], xw_all[PASSES - 1][:].indirect(half_of(offs_list, h)))
+
+        gather_last_words(0, "first_half")
+        w2_codes, w2_scales = planes(N, "w2")
+        for u in range(2):
+            cols = slice(u * W2_HALF, (u + 1) * W2_HALF)
+            quantise(w2_codes[:, cols], w2_scales[:, cols], w2_dealt[u][:])
+
+        out_codes, out_scales = planes(S, "out")
+        hidden, noise, signal, result = {}, {}, {}, {}
 
         def words_order(ap):
             return ap.rearrange("p (c i t) -> p c t i", i=LINE, t=PACK)
@@ -189,9 +192,9 @@ def tile_picked_yddpm_silu_po_kernel(
         def slots_order(ap):
             return ap.rearrange("p t (c i) -> p c t i", i=LINE)
 
-        def stage_a(g):
+        def first_layer(g):
             h, c0 = divmod(g * P, HALF)
-            c, e0 = divmod(g * P, TEMB_WIDTH)
+            words = [xw_first[:, g * P : (g + 1) * P], xw_last[h][:, c0 : c0 + P]]
             acc = psum.tile([P, PACK, P], F32, name="acc", bufs=ACC_BANKS)
             for o in range(PASSES):
                 codes, scales = w1_q[o]
@@ -200,31 +203,41 @@ def tile_picked_yddpm_silu_po_kernel(
                         out=acc[:, t, :],
                         lhsT=codes[:, t * P : (t + 1) * P].bitcast(FP8X4),
                         lhsT_scale=scales[:, t * P : (t + 1) * P],
-                        rhs=xw[o][h][:, c0 : c0 + P].bitcast(FP8X4),
+                        rhs=words[o].bitcast(FP8X4),
                         rhs_scale=xs[o][:, g * P : (g + 1) * P],
                         start=(o == 0 and t == 0),
                         stop=(o == PASSES - 1 and t == PACK - 1),
                     )
-            pre = ring.tile([P, PACK, P], F32, name="pre", bufs=3)
-            nc.vector.tensor_tensor(pre[:], temb_of[c][:, :, e0 : e0 + P], acc[:], ALU.add)
-            hidden[g] = ring.tile([P, P * PACK], BF16, name="hidden", bufs=GROUPS, align_bytes=64)
+            if g == -1:
+                pre = keep.tile([P, PACK, P], F32, name="pre_first", tag="second_half", align_bytes=64)
+            else:
+                pre = ring.tile([P, PACK, P], F32, name="pre", bufs=3)
+            nc.vector.tensor_tensor(pre[:], temb_of[:, :, g * P : (g + 1) * P], acc[:], ALU.add)
+            tag = "w2" if g == 0 else "hidden%d" % g
+            hidden[g] = keep.tile([P, P * PACK], BF16, name="hidden%d" % g, tag=tag, align_bytes=64)
             nc.scalar.activation(words_order(hidden[g][:]), slots_order(pre[:]), ACT.Silu)
             if g == 0:
-                nc.vector.tensor_copy(xw[1][1][:], xw_all[1][:].indirect(entries(offs_list, HALF, HALF)))
-            if e0 + P == TEMB_WIDTH and (c + TEMB_BUFS) * TEMB_WIDTH < S:
-                gather_temb(c + TEMB_BUFS)
+                gather_last_words(1, "second_half")
 
         def scale_lat(g):
             q, c0 = divmod(g * P, LAT_WIDTH)
-            signal[g] = ring.tile([P, PACK, P], F32, name="signal", bufs=GROUPS)
-            for t0 in range(0, PACK, 2):
-                slots = slice(t0, t0 + 2)
-                factor = csig_of[:, g * P : (g + 1) * P].unsqueeze(1).to_broadcast([P, 2, P])
+            signal[g] = keep.tile([P, PACK, P], F32, name="signal%d" % g)
+            if g in TURNED:
+                turned = psum.tile([P, PACK, P], F32, name="back", bufs=BACK_BANKS)
+                for t in range(PACK):
+                    nc.tensor.transpose(turned[:, t, :], lat_rows[q][:, t, c0 : c0 + P], ident[:])
+                nc.scalar.activation(signal[g][:], turned[:], ACT.Copy, scale=coef[:, g, 0:1])
+                return
+            factor = csig_of[:, g * P : (g + 1) * P].unsqueeze(1).to_broadcast([P, POOL_SLOTS, P])
+            for t0 in range(0, PACK, POOL_SLOTS):
+                slots = slice(t0, t0 + POOL_SLOTS)
                 nc.gpsimd.tensor_tensor(signal[g][:, slots, :], lat_rows[q][:, slots, c0 : c0 + P], factor, ALU.mult)
 
-        def stage_b(g):
-            h_codes, h_scales = quantise(hidden[g][:], P, "h%d" % g)
-            scale_lat(g)
+        def second_layer(g):
+            if g not in signal:
+                scale_lat(g)
+            h_codes, h_scales = planes(P, "h%d" % g)
+            quantise(h_codes[:], h_scales[:], hidden[g][:])
             noise[g] = psum.tile([P, N], F32, name="noise", bufs=2)
             nc.tensor.matmul_mx(
                 out=noise[g][:],
@@ -236,35 +249,48 @@ def tile_picked_yddpm_silu_po_kernel(
                 stop=True,
             )
 
-        backs = {}
-
-        def stage_c(g):
+        def combine(g):
             c, c0 = divmod(g * P, OUT_WIDTH)
-            negative = ring.tile([P, N], F32, name="negative", bufs=3)
-            back = psum.tile([P, PACK, P], F32, name="back", bufs=BACK_BANKS)
-            nc.scalar.activation(negative[:], noise[g][:], ACT.Copy, scale=coef[:, g, 1:2])
-            for t in range(PACK):
-                nc.tensor.transpose(back[:, t, :], negative[:, t * P : (t + 1) * P], ident[:])
-            if c0 == 0:
-                result[c] = ring.tile([P, PACK, OUT_WIDTH], F32, name="result", bufs=S // OUT_WIDTH)
-            rounded[g] = ring.tile([P, P * PACK], BF16, name="rounded", bufs=GROUPS, align_bytes=64)
-            nc.vector.tensor_tensor(result[c][:, :, c0 : c0 + P], signal[g][:], back[:], ALU.subtract)
-            last = g >= GROUPS - 2
-            if last or c0 + P == OUT_WIDTH:
-                cols = slice(c0, c0 + P) if last else slice(0, OUT_WIDTH)
-                nc.sync.dma_start(
-                    out=out_0[:, c * OUT_WIDTH + cols.start : c * OUT_WIDTH + cols.stop].rearrange("(p t) s -> p t s", t=PACK),
-                    in_=result[c][:, :, cols],
-                )
-
-        def stage_d(g):
-            c, c0 = divmod(g * P, OUT_WIDTH)
-            cols = slice(g * P, (g + 1) * P)
-            if g not in ROUND_ON_VECTOR:
-                nc.scalar.copy(words_order(rounded[g][:]), slots_order(result[c][:, :, c0 : c0 + P]))
+            scaled = ring.tile([P, PACK, P], F32, name="scaled", bufs=3)
+            in_slots = noise[g][:].rearrange("p (u t m) -> p t u m", u=2, t=PACK)
+            halves_of = lambda ap: ap.rearrange("p t (u m) -> p t u m", u=2)
+            if g in TURNED:
+                for u in range(2):
+                    nc.vector.scalar_tensor_tensor(
+                        halves_of(scaled[:])[:, :, u], in_slots[:, :, u], coef[:, g, 1:2], halves_of(signal[g][:])[:, :, u],
+                        ALU.mult, ALU.subtract,
+                    )
             else:
-                nc.vector.tensor_copy(words_order(rounded[g][:]), slots_order(result[c][:, :, c0 : c0 + P]))
-            nc.vector.quantize_mx(out=out_codes[:, cols].bitcast(FP8X4), scales=out_scales[:, cols], in_=rounded[g][:])
+                nc.scalar.activation(halves_of(scaled[:]), in_slots, ACT.Copy, scale=coef[:, g, 1:2])
+            back = psum.tile([P, PACK, P], F32, name="back", bufs=BACK_BANKS)
+            for t in range(PACK):
+                nc.tensor.transpose(back[:, t, :], scaled[:, t, :], ident[:])
+            if c0 == 0:
+                result[c] = keep.tile([P, PACK, OUT_WIDTH], F32, name="result%d" % c)
+            if g in TURNED:
+                nc.scalar.activation(result[c][:, :, c0 : c0 + P], back[:], ACT.Copy, scale=-1.0)
+            else:
+                nc.vector.tensor_tensor(result[c][:, :, c0 : c0 + P], signal[g][:], back[:], ALU.subtract)
+            alone = g >= GROUPS - 2
+            if alone or c0 + P == OUT_WIDTH:
+                first = c0 if alone else 0
+                rows = out_0[:, c * OUT_WIDTH + first : (g + 1) * P].rearrange("(p t) s -> p t s", t=PACK)
+                nc.sync.dma_start(out=rows, in_=result[c][:, :, first : c0 + P])
+
+        def hand_on(g):
+            c, c0 = divmod(g * P, OUT_WIDTH)
+            alone = g >= GROUPS - 2
+            if not alone and c0 + P < OUT_WIDTH:
+                return
+            first = c0 if alone else 0
+            cols = slice(c * OUT_WIDTH + first, (g + 1) * P)
+            rounded = keep.tile([P, (c0 + P - first) * PACK], BF16, name="rounded%d" % g, align_bytes=64)
+            values = slots_order(result[c][:, :, first : c0 + P])
+            if g in ROUND_ON_VECTOR:
+                nc.vector.tensor_copy(words_order(rounded[:]), values)
+            else:
+                nc.scalar.copy(words_order(rounded[:]), values)
+            quantise(out_codes[:, cols], out_scales[:, cols], rounded[:])
             if g in STORE_FROM:
                 done = slice(STORE_FROM[g], cols.stop)
                 nc.sync.dma_start(
@@ -272,8 +298,11 @@ def tile_picked_yddpm_silu_po_kernel(
                     in_=out_codes[:, done].bitcast(I32),
                 )
 
-        for s in range(GROUPS + LAG_D):
-            for stage, lag in ((stage_a, 0), (stage_b, LAG_B), (stage_c, LAG_C), (stage_d, LAG_D)):
+        for g in range(GROUPS):
+            if g not in TURNED or g * P < EARLY_LAT * LAT_WIDTH:
+                scale_lat(g)
+        for s in range(GROUPS + LAG_HAND_ON):
+            for stage, lag in ((first_layer, 0), (second_layer, LAG_SECOND), (combine, LAG_COMBINE), (hand_on, LAG_HAND_ON)):
                 if 0 <= s - lag < GROUPS:
                     stage(s - lag)
         for r in range(4):

@@ -33,7 +33,7 @@ LAT_WIDTH = S // LAT_PIECES
 OUT_WIDTH = 256
 LAG_SECOND, LAG_COMBINE, LAG_HAND_ON = 1, 2, 8
 ACC_BANKS, BACK_BANKS = 3, 3
-ROUND_ON_VECTOR = (1, 7)
+ROUND_ON_VECTOR = (1, 3, 7)
 STORE_FROM = {3: 0, 5: 512, 7: 768}
 EARLY_LAT = 1
 EARLY_W2 = 1
@@ -54,8 +54,8 @@ def tile_picked_yddpm_silu_po_kernel(
 
         step_list = keep.tile([P, S // 16], U16, name="step_list")
         offs_list = keep.tile([P, S // 16], U16, name="offs_list")
-        temb_rows = keep.tile([P, (PACK - 1) * R + TEMB_WINDOW], F32, name="temb_rows")
-        coef_rows = keep.tile([P, COEF_WINDOW], F32, name="coef_rows", tag="w2", align_bytes=64)
+        temb_rows = keep.tile([P, (PACK - 1) * R + TEMB_WINDOW], F32, name="temb_rows", tag="w2", align_bytes=64)
+        coef_rows = keep.tile([P, COEF_WINDOW], F32, name="coef_rows")
         xs_all = keep.tile([P, T], U8, name="xs_all", tag="late_words", align_bytes=64)
         xw_all = [
             keep.tile([P, T], U32, name="xw_all0", align_bytes=64),
@@ -75,11 +75,11 @@ def tile_picked_yddpm_silu_po_kernel(
 
         first_row = P - PASSES * SCALE_ROWS
         make_identity(nc, ident[:])
-        nc.vector.memset(xs_all[:first_row, :].bitcast(I32), 0)
-        nc.gpsimd.memset(coef_rows[:first_row, :R], 0.0)
-        nc.gpsimd.memset(coef_rows[:, R:], 0.0)
-        nc.gpsimd.memset(temb_rows[:, PACK * R :], 0.0)
+        nc.vector.memset(coef_rows[:first_row, :R], 0.0)
+        nc.vector.memset(coef_rows[:, R:], 0.0)
         nc.vector.memset(xs_both[:].bitcast(I32), 0)
+        nc.gpsimd.memset(xs_all[:first_row, :].bitcast(I32), 0)
+        nc.gpsimd.memset(temb_rows[:, PACK * R :], 0.0)
 
         def load_words(o):
             nc.sync.dma_start(
@@ -89,13 +89,13 @@ def tile_picked_yddpm_silu_po_kernel(
         def load_slots(slots, rows):
             nc.sync.dma_start(out=slots, in_=rows.rearrange("(p t) c -> p t c", t=PACK))
 
+        nc.sync.dma_start(step_list[:], step)
+        nc.sync.dma_start(out=coef_rows[first_row : first_row + 16, :R], in_=csig[:16, :])
+        nc.sync.dma_start(out=coef_rows[first_row + 16 :, :R], in_=cnoise[:16, :])
         nc.sync.dma_start(offs_list[:], offs)
         nc.sync.dma_start(
             out=xs_all[first_row:, :].bitcast(I32), in_=x_scales.rearrange("o q c -> (o q) c").bitcast(I32)
         )
-        nc.sync.dma_start(step_list[:], step)
-        nc.sync.dma_start(out=coef_rows[first_row : first_row + 16, :R], in_=csig[:16, :])
-        nc.sync.dma_start(out=coef_rows[first_row + 16 :, :R], in_=cnoise[:16, :])
         nc.sync.dma_start(out=temb_rows[:, : PACK * R], in_=temb.rearrange("(p t) r -> p (t r)", t=PACK))
         for q in range(EARLY_LAT):
             load_slots(lat_rows[q], lat[:, q * LAT_WIDTH : (q + 1) * LAT_WIDTH])
@@ -110,17 +110,6 @@ def tile_picked_yddpm_silu_po_kernel(
 
         warm = keep.tile([P, 1], F32, name="warm")
         nc.scalar.activation(warm[:], ident[:, 0:1], ACT.Silu)
-
-        picked = keep.tile([P, S], U8, name="picked", align_bytes=64)
-        nc.vector.tensor_copy(picked[:], xs_all[:].indirect(offs_list[:]))
-        for o in range(PASSES):
-            if o == PASSES - 1:
-                load_words(o)
-            for q in range(P // QUADRANT):
-                to_row, from_row = QUADRANT * q, first_row + SCALE_ROWS * o + 4 * q
-                nc.sync.dma_start(
-                    out=xs[o][to_row : to_row + 4, :].bitcast(I32), in_=picked[from_row : from_row + 4, :].bitcast(I32)
-                )
 
         coef_of = keep.tile([P, S], F32, name="coef_of")
         coef = keep.tile([P, GROUPS, 2], F32, name="coef")
@@ -138,6 +127,17 @@ def tile_picked_yddpm_silu_po_kernel(
             for b in range(per_half):
                 nc.tensor.transpose(bank[:, b, :], coef[:, h * per_half + b, 0:1].to_broadcast([P, P]), ident[:])
             nc.scalar.copy(csig_of[:, h * HALF : (h + 1) * HALF], bank[:].rearrange("p b j -> p (b j)"))
+
+        picked = keep.tile([P, S], U8, name="picked", align_bytes=64)
+        nc.vector.tensor_copy(picked[:], xs_all[:].indirect(offs_list[:]))
+        for o in range(PASSES):
+            if o == PASSES - 1:
+                load_words(o)
+            for q in range(P // QUADRANT):
+                to_row, from_row = QUADRANT * q, first_row + SCALE_ROWS * o + 4 * q
+                nc.sync.dma_start(
+                    out=xs[o][to_row : to_row + 4, :].bitcast(I32), in_=picked[from_row : from_row + 4, :].bitcast(I32)
+                )
 
         def deal(raw, width, name):
             dealt = keep.tile([P, PACK * width], BF16, name=name, align_bytes=64)
@@ -192,6 +192,8 @@ def tile_picked_yddpm_silu_po_kernel(
         def slots_order(ap):
             return ap.rearrange("p t (c i) -> p c t i", i=LINE)
 
+        first_sums = []
+
         def first_layer(g):
             h, c0 = divmod(g * P, HALF)
             words = [xw_first[:, g * P : (g + 1) * P], xw_last[h][:, c0 : c0 + P]]
@@ -208,13 +210,14 @@ def tile_picked_yddpm_silu_po_kernel(
                         start=(o == 0 and t == 0),
                         stop=(o == PASSES - 1 and t == PACK - 1),
                     )
-            if g == -1:
-                pre = keep.tile([P, PACK, P], F32, name="pre_first", tag="second_half", align_bytes=64)
+            if g == 0:
+                first_sums.append(keep.tile([P, ACC_BANKS, PACK, P], F32, name="first_sums", tag="w2", align_bytes=64))
+            if g < ACC_BANKS:
+                pre = first_sums[0][:, g]
             else:
                 pre = ring.tile([P, PACK, P], F32, name="pre", bufs=3)
             nc.vector.tensor_tensor(pre[:], temb_of[:, :, g * P : (g + 1) * P], acc[:], ALU.add)
-            tag = "w2" if g == 0 else "hidden%d" % g
-            hidden[g] = keep.tile([P, P * PACK], BF16, name="hidden%d" % g, tag=tag, align_bytes=64)
+            hidden[g] = keep.tile([P, P * PACK], BF16, name="hidden%d" % g, align_bytes=64)
             nc.scalar.activation(words_order(hidden[g][:]), slots_order(pre[:]), ACT.Silu)
             if g == 0:
                 gather_last_words(1, "second_half")

@@ -36,7 +36,6 @@ ACC_BANKS, BACK_BANKS = 3, 3
 ROUND_ON_VECTOR = (1, 3, 7)
 STORE_FROM = {3: 0, 5: 512, 7: 768}
 EARLY_LAT = 1
-EARLY_W2 = 1
 TURNED = (0, 1)
 POOL_SLOTS = 2
 
@@ -62,9 +61,11 @@ def tile_picked_yddpm_silu_po_kernel(
             keep.tile([P, T], U32, name="xw_all1", tag="late_words", align_bytes=64),
         ]
         w1_raw = [ring.tile([P, PACK, H], F32, name="w1_raw%d" % o, tag="raw") for o in range(PASSES)]
-        w2_raw = [keep.tile([P, PACK, W2_HALF], F32, name="w2_raw%d" % u)[:] for u in range(EARLY_W2)]
-        w2_late = keep.tile([P, 2 - EARLY_W2, PACK, W2_HALF], F32, name="w2_late", tag="w2", align_bytes=64)
-        w2_raw = w2_raw + [w2_late[:, u] for u in range(2 - EARLY_W2)]
+        coef_of = keep.tile([P, S], F32, name="coef_of", tag="w2_last", align_bytes=64)
+        w2_raw = [
+            keep.tile([P, PACK, W2_HALF], F32, name="w2_raw0", tag="w2", align_bytes=64)[:],
+            keep.tile([P, PACK, W2_HALF], F32, name="w2_raw1", tag="w2_last", align_bytes=64)[:],
+        ]
         late = LAT_PIECES - EARLY_LAT
         lat_late = [ring.tile([P, (late + 1) // 2, PACK, LAT_WIDTH], F32, name="lat_late%d" % h, tag="raw") for h in range(2)]
         lat_rows = [keep.tile([P, PACK, LAT_WIDTH], F32, name="lat_rows%d" % q)[:] for q in range(EARLY_LAT)]
@@ -102,8 +103,6 @@ def tile_picked_yddpm_silu_po_kernel(
         load_words(0)
         for o in range(PASSES):
             load_slots(w1_raw[o][:], w1[o * K_PASS : (o + 1) * K_PASS, :])
-        for u in range(EARLY_W2):
-            load_slots(w2_raw[u], w2[:, u * W2_HALF : (u + 1) * W2_HALF])
 
         def half_of(offsets, h):
             return offsets[:, h * HALF // 16 : (h + 1) * HALF // 16]
@@ -111,7 +110,6 @@ def tile_picked_yddpm_silu_po_kernel(
         warm = keep.tile([P, 1], F32, name="warm")
         nc.scalar.activation(warm[:], ident[:, 0:1], ACT.Silu)
 
-        coef_of = keep.tile([P, S], F32, name="coef_of")
         coef = keep.tile([P, GROUPS, 2], F32, name="coef")
         csig_of = keep.tile([P, S], F32, name="csig_of")
         per_half = HALF // P
@@ -156,7 +154,7 @@ def tile_picked_yddpm_silu_po_kernel(
             nc.vector.quantize_mx(out=codes.bitcast(FP8X4), scales=scales, in_=values)
 
         w1_dealt = [deal(w1_raw[o][:], H, "w1_dealt%d" % o) for o in range(PASSES)]
-        for u in range(EARLY_W2, 2):
+        for u in range(2):
             load_slots(w2_raw[u], w2[:, u * W2_HALF : (u + 1) * W2_HALF])
         for q in range(EARLY_LAT, LAT_PIECES):
             load_slots(lat_rows[q], lat[:, q * LAT_WIDTH : (q + 1) * LAT_WIDTH])

@@ -33,7 +33,7 @@ LAT_WIDTH = S // LAT_PIECES
 OUT_WIDTH = 256
 LAG_SECOND, LAG_COMBINE, LAG_HAND_ON = 1, 2, 8
 ACC_BANKS, BACK_BANKS = 3, 3
-ROUND_ON_VECTOR = (1, 3, 7)
+ROUND_ON_VECTOR = (7,)
 STORE_FROM = {3: 0, 5: 512, 7: 768}
 EARLY_LAT = 1
 TURNED = (0, 1)

@@ -22,22 +22,22 @@ K_PASS = P * PACK
 PASSES = K // K_PASS
 QUADRANT = 32
 SCALE_ROWS = K_PASS // 32
+GROUPS = S // P
 HALF = S // 2
 LINE = 4
-GROUPS = S // P
 TEMB_WINDOW = 1376
 COEF_WINDOW = 528
+COEF_ROWS = QUADRANT // 2
 W2_HALF = N // 2
-LAT_PIECES = 4
-LAT_WIDTH = S // LAT_PIECES
-OUT_WIDTH = 256
-LAG_SECOND, LAG_COMBINE, LAG_HAND_ON = 1, 2, 8
-ACC_BANKS, BACK_BANKS = 3, 3
-ROUND_ON_VECTOR = (7,)
-STORE_FROM = {3: 0, 5: 512, 7: 768}
-EARLY_LAT = 1
-TURNED = (0, 1)
+LAT_WIDTH = 256
+LAT_PIECES = S // LAT_WIDTH
+TURNED = LAT_WIDTH // P
 POOL_SLOTS = 2
+PAIR = 2 * P
+SINGLE_FROM = GROUPS - 2
+LAG_SECOND, LAG_COMBINE, LAG_HAND_ON = 1, 2, GROUPS
+ACC_BANKS, NOISE_BANKS, BACK_BANKS = 3, 2, 3
+STORE_FROM = {3: 0, 5: 512, 7: 768}
 
 
 def tile_picked_yddpm_silu_po_kernel(
@@ -45,6 +45,7 @@ def tile_picked_yddpm_silu_po_kernel(
 ):
     nc = tc.nc
     halves = S // HALF
+    per_half = HALF // P
 
     with ExitStack() as ctx:
         keep = ctx.enter_context(tc.tile_pool(name="keep", bufs=1))
@@ -53,7 +54,9 @@ def tile_picked_yddpm_silu_po_kernel(
 
         step_list = keep.tile([P, S // 16], U16, name="step_list")
         offs_list = keep.tile([P, S // 16], U16, name="offs_list")
-        temb_rows = keep.tile([P, (PACK - 1) * R + TEMB_WINDOW], F32, name="temb_rows", tag="w2", align_bytes=64)
+        temb_rows = keep.tile(
+            [P, (PACK - 1) * R + TEMB_WINDOW], F32, name="temb_rows", tag="w2_second", align_bytes=64
+        )
         coef_rows = keep.tile([P, COEF_WINDOW], F32, name="coef_rows")
         xs_all = keep.tile([P, T], U8, name="xs_all", tag="late_words", align_bytes=64)
         xw_all = [
@@ -61,25 +64,24 @@ def tile_picked_yddpm_silu_po_kernel(
             keep.tile([P, T], U32, name="xw_all1", tag="late_words", align_bytes=64),
         ]
         w1_raw = [ring.tile([P, PACK, H], F32, name="w1_raw%d" % o, tag="raw") for o in range(PASSES)]
-        coef_of = keep.tile([P, S], F32, name="coef_of", tag="w2_last", align_bytes=64)
+        coef_of = keep.tile([P, S], F32, name="coef_of", tag="w2_first", align_bytes=64)
         w2_raw = [
-            keep.tile([P, PACK, W2_HALF], F32, name="w2_raw0", tag="w2", align_bytes=64)[:],
-            keep.tile([P, PACK, W2_HALF], F32, name="w2_raw1", tag="w2_last", align_bytes=64)[:],
+            keep.tile([P, PACK, W2_HALF], F32, name="w2_raw0", tag="w2_first", align_bytes=64),
+            keep.tile([P, PACK, W2_HALF], F32, name="w2_raw1", tag="w2_second", align_bytes=64),
         ]
-        late = LAT_PIECES - EARLY_LAT
-        lat_late = [ring.tile([P, (late + 1) // 2, PACK, LAT_WIDTH], F32, name="lat_late%d" % h, tag="raw") for h in range(2)]
-        lat_rows = [keep.tile([P, PACK, LAT_WIDTH], F32, name="lat_rows%d" % q)[:] for q in range(EARLY_LAT)]
-        lat_rows = lat_rows + [lat_late[q % 2][:, q // 2] for q in range(late)]
+        lat_late = [ring.tile([P, 2, PACK, LAT_WIDTH], F32, name="lat_late%d" % b, tag="raw") for b in range(2)]
+        lat_first = keep.tile([P, PACK, LAT_WIDTH], F32, name="lat_rows0")
+        lat_rows = [lat_first[:], lat_late[0][:, 0], lat_late[1][:, 0], lat_late[0][:, 1]]
         ident = keep.tile([P, P], F32, name="ident")
         xs_both = keep.tile([P, PASSES * S], U8, name="xs_both", align_bytes=64)
         xs = [xs_both[:, o * S : (o + 1) * S] for o in range(PASSES)]
 
-        first_row = P - PASSES * SCALE_ROWS
+        last_quadrant = P - QUADRANT
         make_identity(nc, ident[:])
-        nc.vector.memset(coef_rows[:first_row, :R], 0.0)
+        nc.vector.memset(coef_rows[:last_quadrant, :R], 0.0)
         nc.vector.memset(coef_rows[:, R:], 0.0)
         nc.vector.memset(xs_both[:].bitcast(I32), 0)
-        nc.gpsimd.memset(xs_all[:first_row, :].bitcast(I32), 0)
+        nc.gpsimd.memset(xs_all[:last_quadrant, :].bitcast(I32), 0)
         nc.gpsimd.memset(temb_rows[:, PACK * R :], 0.0)
 
         def load_words(o):
@@ -90,16 +92,18 @@ def tile_picked_yddpm_silu_po_kernel(
         def load_slots(slots, rows):
             nc.sync.dma_start(out=slots, in_=rows.rearrange("(p t) c -> p t c", t=PACK))
 
+        def load_lat(q):
+            load_slots(lat_rows[q], lat[:, q * LAT_WIDTH : (q + 1) * LAT_WIDTH])
+
         nc.sync.dma_start(step_list[:], step)
-        nc.sync.dma_start(out=coef_rows[first_row : first_row + 16, :R], in_=csig[:16, :])
-        nc.sync.dma_start(out=coef_rows[first_row + 16 :, :R], in_=cnoise[:16, :])
+        nc.sync.dma_start(out=coef_rows[last_quadrant : P - COEF_ROWS, :R], in_=csig[:COEF_ROWS, :])
+        nc.sync.dma_start(out=coef_rows[P - COEF_ROWS :, :R], in_=cnoise[:COEF_ROWS, :])
         nc.sync.dma_start(offs_list[:], offs)
         nc.sync.dma_start(
-            out=xs_all[first_row:, :].bitcast(I32), in_=x_scales.rearrange("o q c -> (o q) c").bitcast(I32)
+            out=xs_all[last_quadrant:, :].bitcast(I32), in_=x_scales.rearrange("o q c -> (o q) c").bitcast(I32)
         )
         nc.sync.dma_start(out=temb_rows[:, : PACK * R], in_=temb.rearrange("(p t) r -> p (t r)", t=PACK))
-        for q in range(EARLY_LAT):
-            load_slots(lat_rows[q], lat[:, q * LAT_WIDTH : (q + 1) * LAT_WIDTH])
+        load_lat(0)
         load_words(0)
         for o in range(PASSES):
             load_slots(w1_raw[o][:], w1[o * K_PASS : (o + 1) * K_PASS, :])
@@ -112,19 +116,19 @@ def tile_picked_yddpm_silu_po_kernel(
 
         coef = keep.tile([P, GROUPS, 2], F32, name="coef")
         csig_of = keep.tile([P, S], F32, name="csig_of")
-        per_half = HALF // P
         for h in range(halves):
             nc.vector.tensor_copy(coef_of[:, h * HALF : (h + 1) * HALF], coef_rows[:].indirect(half_of(step_list, h)))
             bank = psum.tile([P, per_half, P], F32, name="back", bufs=BACK_BANKS)
             for b in range(per_half):
                 g = h * per_half + b
                 nc.tensor.transpose(bank[:, b, :], coef_of[:, g * P : (g + 1) * P], ident[:])
-            nc.scalar.copy(coef[:, h * per_half : (h + 1) * per_half, :], bank[:, :, first_row : P : 16])
+            nc.scalar.copy(coef[:, h * per_half : (h + 1) * per_half, :], bank[:, :, last_quadrant:P:COEF_ROWS])
         for h in range(halves):
-            bank = psum.tile([P, per_half, P], F32, name="back", bufs=BACK_BANKS)
-            for b in range(per_half):
-                nc.tensor.transpose(bank[:, b, :], coef[:, h * per_half + b, 0:1].to_broadcast([P, P]), ident[:])
-            nc.scalar.copy(csig_of[:, h * HALF : (h + 1) * HALF], bank[:].rearrange("p b j -> p (b j)"))
+            first, end = max(h * per_half, TURNED), (h + 1) * per_half
+            bank = psum.tile([P, end - first, P], F32, name="back", bufs=BACK_BANKS)
+            for g in range(first, end):
+                nc.tensor.transpose(bank[:, g - first, :], coef[:, g, 0:1].to_broadcast([P, P]), ident[:])
+            nc.scalar.copy(csig_of[:, first * P : end * P], bank[:].rearrange("p b j -> p (b j)"))
 
         picked = keep.tile([P, S], U8, name="picked", align_bytes=64)
         nc.vector.tensor_copy(picked[:], xs_all[:].indirect(offs_list[:]))
@@ -132,7 +136,7 @@ def tile_picked_yddpm_silu_po_kernel(
             if o == PASSES - 1:
                 load_words(o)
             for q in range(P // QUADRANT):
-                to_row, from_row = QUADRANT * q, first_row + SCALE_ROWS * o + 4 * q
+                to_row, from_row = QUADRANT * q, last_quadrant + SCALE_ROWS * o + 4 * q
                 nc.sync.dma_start(
                     out=xs[o][to_row : to_row + 4, :].bitcast(I32), in_=picked[from_row : from_row + 4, :].bitcast(I32)
                 )
@@ -141,7 +145,7 @@ def tile_picked_yddpm_silu_po_kernel(
             dealt = keep.tile([P, PACK * width], BF16, name=name, align_bytes=64)
             nc.scalar.copy(
                 dealt[:].rearrange("p (t m j) -> p m t j", t=PACK, j=PACK),
-                raw.rearrange("p j (m t) -> p m t j", t=PACK),
+                raw[:].rearrange("p j (m t) -> p m t j", t=PACK),
             )
             return dealt
 
@@ -153,11 +157,11 @@ def tile_picked_yddpm_silu_po_kernel(
         def quantise(codes, scales, values):
             nc.vector.quantize_mx(out=codes.bitcast(FP8X4), scales=scales, in_=values)
 
-        w1_dealt = [deal(w1_raw[o][:], H, "w1_dealt%d" % o) for o in range(PASSES)]
+        w1_dealt = [deal(w1_raw[o], H, "w1_dealt%d" % o) for o in range(PASSES)]
         for u in range(2):
-            load_slots(w2_raw[u], w2[:, u * W2_HALF : (u + 1) * W2_HALF])
-        for q in range(EARLY_LAT, LAT_PIECES):
-            load_slots(lat_rows[q], lat[:, q * LAT_WIDTH : (q + 1) * LAT_WIDTH])
+            load_slots(w2_raw[u][:], w2[:, u * W2_HALF : (u + 1) * W2_HALF])
+        for q in range(1, LAT_PIECES):
+            load_lat(q)
         w2_dealt = [deal(w2_raw[u], W2_HALF, "w2_dealt%d" % u) for u in range(2)]
 
         temb_of = keep.tile([P, PACK, S], F32, name="temb_of")
@@ -169,13 +173,14 @@ def tile_picked_yddpm_silu_po_kernel(
         w1_q = [planes(H, "w1_%d" % o) for o in range(PASSES)]
         for o in range(PASSES):
             quantise(w1_q[o][0][:], w1_q[o][1][:], w1_dealt[o][:])
+
         xw_last = {}
 
-        def gather_last_words(h, tag):
-            xw_last[h] = keep.tile([P, HALF], U32, name="xw_last%d" % h, tag=tag, align_bytes=64)
+        def gather_last_words(h):
+            xw_last[h] = keep.tile([P, HALF], U32, name="xw_last%d" % h, align_bytes=64)
             nc.vector.tensor_copy(xw_last[h][:], xw_all[PASSES - 1][:].indirect(half_of(offs_list, h)))
 
-        gather_last_words(0, "first_half")
+        gather_last_words(0)
         w2_codes, w2_scales = planes(N, "w2")
         for u in range(2):
             cols = slice(u * W2_HALF, (u + 1) * W2_HALF)
@@ -183,6 +188,7 @@ def tile_picked_yddpm_silu_po_kernel(
 
         out_codes, out_scales = planes(S, "out")
         hidden, noise, signal, result = {}, {}, {}, {}
+        first_sums = keep.tile([P, ACC_BANKS, PACK, P], F32, name="first_sums", tag="w2_first", align_bytes=64)
 
         def words_order(ap):
             return ap.rearrange("p (c i t) -> p c t i", i=LINE, t=PACK)
@@ -190,11 +196,10 @@ def tile_picked_yddpm_silu_po_kernel(
         def slots_order(ap):
             return ap.rearrange("p t (c i) -> p c t i", i=LINE)
 
-        first_sums = []
-
         def first_layer(g):
             h, c0 = divmod(g * P, HALF)
-            words = [xw_first[:, g * P : (g + 1) * P], xw_last[h][:, c0 : c0 + P]]
+            cols = slice(g * P, (g + 1) * P)
+            words = [xw_first[:, cols], xw_last[h][:, c0 : c0 + P]]
             acc = psum.tile([P, PACK, P], F32, name="acc", bufs=ACC_BANKS)
             for o in range(PASSES):
                 codes, scales = w1_q[o]
@@ -204,42 +209,36 @@ def tile_picked_yddpm_silu_po_kernel(
                         lhsT=codes[:, t * P : (t + 1) * P].bitcast(FP8X4),
                         lhsT_scale=scales[:, t * P : (t + 1) * P],
                         rhs=words[o].bitcast(FP8X4),
-                        rhs_scale=xs[o][:, g * P : (g + 1) * P],
+                        rhs_scale=xs[o][:, cols],
                         start=(o == 0 and t == 0),
                         stop=(o == PASSES - 1 and t == PACK - 1),
                     )
-            if g == 0:
-                first_sums.append(keep.tile([P, ACC_BANKS, PACK, P], F32, name="first_sums", tag="w2", align_bytes=64))
-            if g < ACC_BANKS:
-                pre = first_sums[0][:, g]
-            else:
-                pre = ring.tile([P, PACK, P], F32, name="pre", bufs=3)
-            nc.vector.tensor_tensor(pre[:], temb_of[:, :, g * P : (g + 1) * P], acc[:], ALU.add)
+            pre = first_sums[:, g] if g < ACC_BANKS else keep.tile([P, PACK, P], F32, name="pre%d" % g)[:]
+            nc.vector.tensor_tensor(pre, temb_of[:, :, cols], acc[:], ALU.add)
             hidden[g] = keep.tile([P, P * PACK], BF16, name="hidden%d" % g, align_bytes=64)
-            nc.scalar.activation(words_order(hidden[g][:]), slots_order(pre[:]), ACT.Silu)
+            nc.scalar.activation(words_order(hidden[g][:]), slots_order(pre), ACT.Silu)
             if g == 0:
-                gather_last_words(1, "second_half")
+                gather_last_words(1)
 
         def scale_lat(g):
             q, c0 = divmod(g * P, LAT_WIDTH)
             signal[g] = keep.tile([P, PACK, P], F32, name="signal%d" % g)
-            if g in TURNED:
+            if g < TURNED:
                 turned = psum.tile([P, PACK, P], F32, name="back", bufs=BACK_BANKS)
                 for t in range(PACK):
                     nc.tensor.transpose(turned[:, t, :], lat_rows[q][:, t, c0 : c0 + P], ident[:])
                 nc.scalar.activation(signal[g][:], turned[:], ACT.Copy, scale=coef[:, g, 0:1])
-                return
-            factor = csig_of[:, g * P : (g + 1) * P].unsqueeze(1).to_broadcast([P, POOL_SLOTS, P])
-            for t0 in range(0, PACK, POOL_SLOTS):
-                slots = slice(t0, t0 + POOL_SLOTS)
-                nc.gpsimd.tensor_tensor(signal[g][:, slots, :], lat_rows[q][:, slots, c0 : c0 + P], factor, ALU.mult)
+            else:
+                factor = csig_of[:, g * P : (g + 1) * P].unsqueeze(1).to_broadcast([P, POOL_SLOTS, P])
+                for t0 in range(0, PACK, POOL_SLOTS):
+                    slots = slice(t0, t0 + POOL_SLOTS)
+                    values = lat_rows[q][:, slots, c0 : c0 + P]
+                    nc.gpsimd.tensor_tensor(signal[g][:, slots, :], values, factor, ALU.mult)
 
         def second_layer(g):
-            if g not in signal:
-                scale_lat(g)
             h_codes, h_scales = planes(P, "h%d" % g)
             quantise(h_codes[:], h_scales[:], hidden[g][:])
-            noise[g] = psum.tile([P, N], F32, name="noise", bufs=2)
+            noise[g] = psum.tile([P, N], F32, name="noise", bufs=NOISE_BANKS)
             nc.tensor.matmul_mx(
                 out=noise[g][:],
                 lhsT=h_codes[:].bitcast(FP8X4),
@@ -250,44 +249,57 @@ def tile_picked_yddpm_silu_po_kernel(
                 stop=True,
             )
 
+        def by_halves(ap):
+            return ap.rearrange("p t (u m) -> p t u m", u=2)
+
+        def leaving(g):
+            c0 = g * P % PAIR
+            if g >= SINGLE_FROM:
+                return c0
+            return 0 if c0 + P == PAIR else None
+
         def combine(g):
-            c, c0 = divmod(g * P, OUT_WIDTH)
-            scaled = ring.tile([P, PACK, P], F32, name="scaled", bufs=3)
-            in_slots = noise[g][:].rearrange("p (u t m) -> p t u m", u=2, t=PACK)
-            halves_of = lambda ap: ap.rearrange("p t (u m) -> p t u m", u=2)
-            if g in TURNED:
+            c, c0 = divmod(g * P, PAIR)
+            scaled = keep.tile([P, PACK, P], F32, name="scaled%d" % g)
+            ee = noise[g][:].rearrange("p (u t m) -> p t u m", u=2, t=PACK)
+            if g < TURNED:
                 for u in range(2):
                     nc.vector.scalar_tensor_tensor(
-                        halves_of(scaled[:])[:, :, u], in_slots[:, :, u], coef[:, g, 1:2], halves_of(signal[g][:])[:, :, u],
-                        ALU.mult, ALU.subtract,
+                        by_halves(scaled[:])[:, :, u],
+                        ee[:, :, u],
+                        coef[:, g, 1:2],
+                        by_halves(signal[g][:])[:, :, u],
+                        ALU.mult,
+                        ALU.subtract,
                     )
             else:
-                nc.scalar.activation(halves_of(scaled[:]), in_slots, ACT.Copy, scale=coef[:, g, 1:2])
-            back = psum.tile([P, PACK, P], F32, name="back", bufs=BACK_BANKS)
+                nc.scalar.activation(by_halves(scaled[:]), ee, ACT.Copy, scale=coef[:, g, 1:2])
+            if g >= GROUPS - ACC_BANKS:
+                back = psum.tile([P, PACK, P], F32, name="acc", bufs=ACC_BANKS)
+            else:
+                back = psum.tile([P, PACK, P], F32, name="back", bufs=BACK_BANKS)
             for t in range(PACK):
                 nc.tensor.transpose(back[:, t, :], scaled[:, t, :], ident[:])
             if c0 == 0:
-                result[c] = keep.tile([P, PACK, OUT_WIDTH], F32, name="result%d" % c)
-            if g in TURNED:
+                result[c] = keep.tile([P, PACK, PAIR], F32, name="result%d" % c)
+            if g < TURNED:
                 nc.scalar.activation(result[c][:, :, c0 : c0 + P], back[:], ACT.Copy, scale=-1.0)
             else:
                 nc.vector.tensor_tensor(result[c][:, :, c0 : c0 + P], signal[g][:], back[:], ALU.subtract)
-            alone = g >= GROUPS - 2
-            if alone or c0 + P == OUT_WIDTH:
-                first = c0 if alone else 0
-                rows = out_0[:, c * OUT_WIDTH + first : (g + 1) * P].rearrange("(p t) s -> p t s", t=PACK)
+            first = leaving(g)
+            if first is not None:
+                rows = out_0[:, c * PAIR + first : (g + 1) * P].rearrange("(p t) s -> p t s", t=PACK)
                 nc.sync.dma_start(out=rows, in_=result[c][:, :, first : c0 + P])
 
         def hand_on(g):
-            c, c0 = divmod(g * P, OUT_WIDTH)
-            alone = g >= GROUPS - 2
-            if not alone and c0 + P < OUT_WIDTH:
+            c, c0 = divmod(g * P, PAIR)
+            first = leaving(g)
+            if first is None:
                 return
-            first = c0 if alone else 0
-            cols = slice(c * OUT_WIDTH + first, (g + 1) * P)
+            cols = slice(c * PAIR + first, (g + 1) * P)
             rounded = keep.tile([P, (c0 + P - first) * PACK], BF16, name="rounded%d" % g, align_bytes=64)
             values = slots_order(result[c][:, :, first : c0 + P])
-            if g in ROUND_ON_VECTOR:
+            if g == GROUPS - 1:
                 nc.vector.tensor_copy(words_order(rounded[:]), values)
             else:
                 nc.scalar.copy(words_order(rounded[:]), values)
@@ -300,10 +312,10 @@ def tile_picked_yddpm_silu_po_kernel(
                 )
 
         for g in range(GROUPS):
-            if g not in TURNED or g * P < EARLY_LAT * LAT_WIDTH:
-                scale_lat(g)
+            scale_lat(g)
+        stages = ((first_layer, 0), (second_layer, LAG_SECOND), (combine, LAG_COMBINE), (hand_on, LAG_HAND_ON))
         for s in range(GROUPS + LAG_HAND_ON):
-            for stage, lag in ((first_layer, 0), (second_layer, LAG_SECOND), (combine, LAG_COMBINE), (hand_on, LAG_HAND_ON)):
+            for stage, lag in stages:
                 if 0 <= s - lag < GROUPS:
                     stage(s - lag)
         for r in range(4):

@@ -25,19 +25,43 @@ SCALE_ROWS = K_PASS // 32
 GROUPS = S // P
 HALF = S // 2
 LINE = 4
-TEMB_WINDOW = 1376
-COEF_WINDOW = 528
+WINDOW = HALF + 16
 COEF_ROWS = QUADRANT // 2
-W2_HALF = N // 2
-LAT_WIDTH = 256
+W_HALF = 256
+M_HALF = W_HALF // PACK
+LAT_WIDTH = 512
 LAT_PIECES = S // LAT_WIDTH
-TURNED = LAT_WIDTH // P
 POOL_SLOTS = 2
 PAIR = 2 * P
 SINGLE_FROM = GROUPS - 2
-LAG_SECOND, LAG_COMBINE, LAG_HAND_ON = 1, 2, GROUPS
-ACC_BANKS, NOISE_BANKS, BACK_BANKS = 3, 2, 3
-STORE_FROM = {3: 0, 5: 512, 7: 768}
+LATE_ORDER = "abA"
+TIE = 0
+ROUND_ON = "sssssssv"
+W2_DEAL = "sg"
+MULT_ON = "vvggggvv"
+STAGES = "f0 q1 s1 l2 c2 r8 h8"
+WORDS_FIRST = 0
+EARLY_V = 0
+W1_WHOLE = 0
+STORE_AFTER = "13567"
+SCALE_ON = "ssssssss"
+UNITS = "22211"
+SPLIT_ROUND = 1
+HOLD_TAG = "temb2"
+MOVES_ON = "ss"
+TURN_TAG = "back"
+COPY_ON = "ssssssss"
+ACC_BANKS = 3
+NOISE_BANKS = 2
+BACK_BANKS = 3
+W2_STEP = "00"
+NOISE_ACC = 9
+BACK_ACC = 5
+HOLD_ROUND = 0
+CODES_AFTER = "357"
+LATE_V = 2
+
+BANKS = {"back": BACK_BANKS, "noise": NOISE_BANKS, "acc": ACC_BANKS, "turn": 1}
 
 
 def tile_picked_yddpm_silu_po_kernel(
@@ -49,40 +73,39 @@ def tile_picked_yddpm_silu_po_kernel(
 
     with ExitStack() as ctx:
         keep = ctx.enter_context(tc.tile_pool(name="keep", bufs=1))
-        ring = ctx.enter_context(tc.tile_pool(name="ring", bufs=2))
         psum = ctx.enter_context(tc.psum_pool(name="psum", bufs=1))
+
+        def held(shape, dtype, name, tag):
+            return keep.tile(shape, dtype, name=name, tag=tag, align_bytes=64)
 
         step_list = keep.tile([P, S // 16], U16, name="step_list")
         offs_list = keep.tile([P, S // 16], U16, name="offs_list")
-        temb_rows = keep.tile(
-            [P, (PACK - 1) * R + TEMB_WINDOW], F32, name="temb_rows", tag="w2_second", align_bytes=64
-        )
-        coef_rows = keep.tile([P, COEF_WINDOW], F32, name="coef_rows")
-        xs_all = keep.tile([P, T], U8, name="xs_all", tag="late_words", align_bytes=64)
-        xw_all = [
-            keep.tile([P, T], U32, name="xw_all0", align_bytes=64),
-            keep.tile([P, T], U32, name="xw_all1", tag="late_words", align_bytes=64),
-        ]
-        w1_raw = [ring.tile([P, PACK, H], F32, name="w1_raw%d" % o, tag="raw") for o in range(PASSES)]
-        coef_of = keep.tile([P, S], F32, name="coef_of", tag="w2_first", align_bytes=64)
-        w2_raw = [
-            keep.tile([P, PACK, W2_HALF], F32, name="w2_raw0", tag="w2_first", align_bytes=64),
-            keep.tile([P, PACK, W2_HALF], F32, name="w2_raw1", tag="w2_second", align_bytes=64),
-        ]
-        lat_late = [ring.tile([P, 2, PACK, LAT_WIDTH], F32, name="lat_late%d" % b, tag="raw") for b in range(2)]
-        lat_first = keep.tile([P, PACK, LAT_WIDTH], F32, name="lat_rows0")
-        lat_rows = [lat_first[:], lat_late[0][:, 0], lat_late[1][:, 0], lat_late[0][:, 1]]
+        temb_rows = [keep.tile([P, PACK * R], F32, name="temb_rows0")]
+        temb_rows = temb_rows + [held([P, WINDOW], F32, "temb_rows%d" % t, "temb%d" % t) for t in range(1, PACK)]
+        coef_rows = keep.tile([P, WINDOW], F32, name="coef_rows")
+        xs_all = held([P, T], U8, "xs_all", "first_w1" if WORDS_FIRST else "last_words")
+        xw_all = [held([P, T], U32, "xw_all0", "first_words"), held([P, T], U32, "xw_all1", "last_words")]
+        w1_first = held([P, PACK, H], F32, "w1_first", "first_w1")
+        w1_last = held([P, 2, PACK, W_HALF], F32, "w1_last", "first_words")
+        w2_raw = [held([P, PACK, W_HALF], F32, "w2_raw%d" % u, "temb%d" % (u + 1)) for u in range(2)]
+        lat_first = held([P, PACK, LAT_WIDTH], F32, "lat_first", "temb3")
+        lat_late = held([P, LAT_PIECES - 1, PACK, LAT_WIDTH], F32, "lat_late", "last_words" if WORDS_FIRST else "first_w1")
+        lat_rows = [lat_first[:]] + [lat_late[:, q] for q in range(LAT_PIECES - 1)]
         ident = keep.tile([P, P], F32, name="ident")
         xs_both = keep.tile([P, PASSES * S], U8, name="xs_both", align_bytes=64)
         xs = [xs_both[:, o * S : (o + 1) * S] for o in range(PASSES)]
 
         last_quadrant = P - QUADRANT
+        nc.gpsimd.memset(xs_all[:last_quadrant, :].bitcast(I32), 0)
         make_identity(nc, ident[:])
+        warm = keep.tile([P, 2], F32, name="warm")
+        nc.vector.memset(warm[:, 0:1], 0.0)
+        nc.scalar.activation(warm[:, 1:2], warm[:, 0:1], ACT.Silu)
         nc.vector.memset(coef_rows[:last_quadrant, :R], 0.0)
         nc.vector.memset(coef_rows[:, R:], 0.0)
+        for t in range(1, PACK):
+            nc.vector.memset(temb_rows[t][:, R:], 0.0)
         nc.vector.memset(xs_both[:].bitcast(I32), 0)
-        nc.gpsimd.memset(xs_all[:last_quadrant, :].bitcast(I32), 0)
-        nc.gpsimd.memset(temb_rows[:, PACK * R :], 0.0)
 
         def load_words(o):
             nc.sync.dma_start(
@@ -92,28 +115,64 @@ def tile_picked_yddpm_silu_po_kernel(
         def load_slots(slots, rows):
             nc.sync.dma_start(out=slots, in_=rows.rearrange("(p t) c -> p t c", t=PACK))
 
-        def load_lat(q):
-            load_slots(lat_rows[q], lat[:, q * LAT_WIDTH : (q + 1) * LAT_WIDTH])
-
         nc.sync.dma_start(step_list[:], step)
         nc.sync.dma_start(out=coef_rows[last_quadrant : P - COEF_ROWS, :R], in_=csig[:COEF_ROWS, :])
         nc.sync.dma_start(out=coef_rows[P - COEF_ROWS :, :R], in_=cnoise[:COEF_ROWS, :])
+        nc.sync.dma_start(out=temb_rows[0][:], in_=temb.rearrange("(p t) r -> p (t r)", t=PACK))
         nc.sync.dma_start(offs_list[:], offs)
         nc.sync.dma_start(
             out=xs_all[last_quadrant:, :].bitcast(I32), in_=x_scales.rearrange("o q c -> (o q) c").bitcast(I32)
         )
-        nc.sync.dma_start(out=temb_rows[:, : PACK * R], in_=temb.rearrange("(p t) r -> p (t r)", t=PACK))
-        load_lat(0)
         load_words(0)
-        for o in range(PASSES):
-            load_slots(w1_raw[o][:], w1[o * K_PASS : (o + 1) * K_PASS, :])
+        if not WORDS_FIRST:
+            load_slots(w1_first[:], w1[:K_PASS, :])
+        else:
+            load_words(1)
 
         def half_of(offsets, h):
             return offsets[:, h * HALF // 16 : (h + 1) * HALF // 16]
 
-        warm = keep.tile([P, 1], F32, name="warm")
-        nc.scalar.activation(warm[:], ident[:, 0:1], ACT.Silu)
+        for t in range(1, PACK):
+            nc.vector.tensor_copy(temb_rows[t][:, :R], temb_rows[0][:, t * R : (t + 1) * R])
 
+        picked = keep.tile([P, S], U8, name="picked", align_bytes=64)
+        nc.vector.tensor_copy(picked[:], xs_all[:].indirect(offs_list[:]))
+        for o in range(PASSES):
+            if o == PASSES - 1:
+                if WORDS_FIRST:
+                    load_slots(w1_first[:], w1[:K_PASS, :])
+                else:
+                    load_words(o)
+            for r in range(4):
+                first = last_quadrant + SCALE_ROWS * o + r
+                (nc.sync if MOVES_ON[o] == "s" else nc.gpsimd).dma_start(
+                    out=xs[o][r:P:QUADRANT, :].bitcast(I32), in_=picked[first : first + SCALE_ROWS - r : 4, :].bitcast(I32)
+                )
+        w1_whole = w1_last[:].rearrange("p u j c -> p (u j c)").rearrange("p (j c) -> p j c", j=PACK)
+        if W1_WHOLE:
+            load_slots(w1_whole, w1[K_PASS:, :])
+        else:
+            for u in range(2):
+                load_slots(w1_last[:, u], w1[K_PASS:, u * W_HALF : (u + 1) * W_HALF])
+        for name in LATE_ORDER + "".join(c for c in "ABCD"[:LAT_PIECES] if c not in LATE_ORDER):
+            if name in "ab":
+                u = "ab".index(name)
+                load_slots(w2_raw[u][:], w2[:, u * W_HALF : (u + 1) * W_HALF])
+            else:
+                q = "ABCD".index(name)
+                load_slots(lat_rows[q], lat[:, q * LAT_WIDTH : (q + 1) * LAT_WIDTH])
+
+        temb_of = keep.tile([P, PACK, S], F32, name="temb_of")
+
+        def gather_temb(t):
+            for h in range(halves):
+                nc.scalar.activation(
+                    temb_of[:, t, h * HALF : (h + 1) * HALF], temb_rows[t][:].indirect(half_of(step_list, h)), ACT.Copy
+                )
+
+        gather_temb(0)
+        gather_temb(1)
+        coef_of = keep.tile([P, S], F32, name="coef_of")
         coef = keep.tile([P, GROUPS, 2], F32, name="coef")
         csig_of = keep.tile([P, S], F32, name="csig_of")
         for h in range(halves):
@@ -122,32 +181,30 @@ def tile_picked_yddpm_silu_po_kernel(
             for b in range(per_half):
                 g = h * per_half + b
                 nc.tensor.transpose(bank[:, b, :], coef_of[:, g * P : (g + 1) * P], ident[:])
-            nc.scalar.copy(coef[:, h * per_half : (h + 1) * per_half, :], bank[:, :, last_quadrant:P:COEF_ROWS])
+            nc.vector.tensor_copy(coef[:, h * per_half : (h + 1) * per_half, :], bank[:, :, last_quadrant:P:COEF_ROWS])
+        gather_temb(2)
+        gather_temb(3)
         for h in range(halves):
-            first, end = max(h * per_half, TURNED), (h + 1) * per_half
-            bank = psum.tile([P, end - first, P], F32, name="back", bufs=BACK_BANKS)
-            for g in range(first, end):
-                nc.tensor.transpose(bank[:, g - first, :], coef[:, g, 0:1].to_broadcast([P, P]), ident[:])
-            nc.scalar.copy(csig_of[:, first * P : end * P], bank[:].rearrange("p b j -> p (b j)"))
+            bank = psum.tile([P, per_half, P], F32, name="noise", bufs=NOISE_BANKS)
+            for b in range(per_half):
+                g = h * per_half + b
+                nc.tensor.transpose(bank[:, b, :], coef[:, g, 0:1].to_broadcast([P, P]), ident[:])
+            nc.vector.tensor_copy(csig_of[:, h * HALF : (h + 1) * HALF], bank[:].rearrange("p b j -> p (b j)"))
 
-        picked = keep.tile([P, S], U8, name="picked", align_bytes=64)
-        nc.vector.tensor_copy(picked[:], xs_all[:].indirect(offs_list[:]))
-        for o in range(PASSES):
-            if o == PASSES - 1:
-                load_words(o)
-            for q in range(P // QUADRANT):
-                to_row, from_row = QUADRANT * q, last_quadrant + SCALE_ROWS * o + 4 * q
-                nc.sync.dma_start(
-                    out=xs[o][to_row : to_row + 4, :].bitcast(I32), in_=picked[from_row : from_row + 4, :].bitcast(I32)
-                )
-
-        def deal(raw, width, name):
+        def deal(copy, raw, name):
+            slots = raw.shape[3]
+            width = raw.shape[2] * slots
             dealt = keep.tile([P, PACK * width], BF16, name=name, align_bytes=64)
-            nc.scalar.copy(
-                dealt[:].rearrange("p (t m j) -> p m t j", t=PACK, j=PACK),
-                raw[:].rearrange("p j (m t) -> p m t j", t=PACK),
-            )
+            copy(dealt[:].rearrange("p (t m j) -> p m t j", t=slots, j=PACK), raw.rearrange("p j m t -> p m t j"))
             return dealt
+
+        def pool_copy(out, in_):
+            nc.gpsimd.tensor_scalar(out, in_, 1.0, 0.0, ALU.mult, ALU.add)
+
+        copier = {"s": nc.scalar.copy, "v": nc.vector.tensor_copy, "g": pool_copy}
+
+        def by_slot(raw):
+            return raw.rearrange("p j (m t) -> p j m t", t=PACK)
 
         def planes(width, name):
             codes = keep.tile([P, width], U32, name=name + "_codes", align_bytes=64)
@@ -157,38 +214,53 @@ def tile_picked_yddpm_silu_po_kernel(
         def quantise(codes, scales, values):
             nc.vector.quantize_mx(out=codes.bitcast(FP8X4), scales=scales, in_=values)
 
-        w1_dealt = [deal(w1_raw[o], H, "w1_dealt%d" % o) for o in range(PASSES)]
-        for u in range(2):
-            load_slots(w2_raw[u][:], w2[:, u * W2_HALF : (u + 1) * W2_HALF])
-        for q in range(1, LAT_PIECES):
-            load_lat(q)
-        w2_dealt = [deal(w2_raw[u], W2_HALF, "w2_dealt%d" % u) for u in range(2)]
-
-        temb_of = keep.tile([P, PACK, S], F32, name="temb_of")
-        for t in range(PACK):
-            window = temb_rows[:, t * R : t * R + TEMB_WINDOW]
-            nc.vector.tensor_copy(temb_of[:, t, :], window.indirect(step_list[:]))
-        xw_first = keep.tile([P, S], U32, name="xw_first", align_bytes=64)
-        nc.vector.tensor_copy(xw_first[:], xw_all[0][:].indirect(offs_list[:]))
+        xw = [keep.tile([P, S], U32, name="xw%d" % o, align_bytes=64) for o in range(PASSES)]
         w1_q = [planes(H, "w1_%d" % o) for o in range(PASSES)]
-        for o in range(PASSES):
-            quantise(w1_q[o][0][:], w1_q[o][1][:], w1_dealt[o][:])
+        nc.vector.tensor_copy(xw[0][:], xw_all[0][:].indirect(offs_list[:]))
+        if WORDS_FIRST:
+            nc.vector.tensor_copy(xw[1][:], xw_all[1][:].indirect(offs_list[:]))
+            for u in range(2):
+                dealt = deal(copier["sv"[u]], by_slot(w1_first[:])[:, :, :, 2 * u : 2 * u + 2], "w1_first%d" % u)
+                cols = slice(u * W_HALF, (u + 1) * W_HALF)
+                quantise(w1_q[0][0][:, cols], w1_q[0][1][:, cols], dealt[:])
+        else:
+            dealt = deal(nc.vector.tensor_copy, by_slot(w1_first[:]), "w1_first_dealt")
+            quantise(w1_q[0][0][:], w1_q[0][1][:], dealt[:])
+            nc.vector.tensor_copy(xw[1][:], xw_all[1][:].indirect(offs_list[:]))
 
-        xw_last = {}
+        def quantise_slots(dealt, first, count, u):
+            for t in range(count):
+                cols = slice((first + t) * P + u * M_HALF, (first + t) * P + (u + 1) * M_HALF)
+                quantise(w1_q[1][0][:, cols], w1_q[1][1][:, cols], dealt[:, t * W_HALF : (t + 1) * W_HALF])
 
-        def gather_last_words(h):
-            xw_last[h] = keep.tile([P, HALF], U32, name="xw_last%d" % h, align_bytes=64)
-            nc.vector.tensor_copy(xw_last[h][:], xw_all[PASSES - 1][:].indirect(half_of(offs_list, h)))
+        shares = []
+        if W1_WHOLE:
+            parts = []
+            for copy, first, end in ((nc.scalar.copy, LATE_V, PACK), (nc.vector.tensor_copy, 0, LATE_V)):
+                parts.append((deal(copy, by_slot(w1_whole)[:, :, :, first:end], "w1_whole%d" % end), first, end))
+            for dealt, first, end in parts:
+                quantise(w1_q[1][0][:, first * P : end * P], w1_q[1][1][:, first * P : end * P], dealt[:])
+        for u, split in enumerate(() if W1_WHOLE else (EARLY_V, LATE_V)):
+            raw = by_slot(w1_last[:, u])
+            for copy, first, end in ((nc.scalar.copy, split, PACK), (nc.vector.tensor_copy, 0, split)):
+                if end > first:
+                    shares.append((deal(copy, raw[:, :, :, first:end], "w1_last%d%d" % (u, end)), first, end - first, u))
+        for share in shares:
+            quantise_slots(*share)
 
-        gather_last_words(0)
         w2_codes, w2_scales = planes(N, "w2")
-        for u in range(2):
-            cols = slice(u * W2_HALF, (u + 1) * W2_HALF)
-            quantise(w2_codes[:, cols], w2_scales[:, cols], w2_dealt[u][:])
+
+        w2_dealt = keep.tile([P, PACK * N], BF16, name="w2_dealt", align_bytes=64)
+
+        def prepare_w2(u):
+            place = w2_dealt[:].rearrange("p (t u m j) -> p u m t j", t=PACK, u=2, j=PACK)[:, u]
+            copier[W2_DEAL[u]](place, by_slot(w2_raw[u][:]).rearrange("p j m t -> p m t j"))
+            if u == 1:
+                quantise(w2_codes[:], w2_scales[:], w2_dealt[:])
 
         out_codes, out_scales = planes(S, "out")
-        hidden, noise, signal, result = {}, {}, {}, {}
-        first_sums = keep.tile([P, ACC_BANKS, PACK, P], F32, name="first_sums", tag="w2_first", align_bytes=64)
+        hidden, noise, signal = {}, {}, {}
+        result = keep.tile([P, PACK, S], F32, name="result")
 
         def words_order(ap):
             return ap.rearrange("p (c i t) -> p c t i", i=LINE, t=PACK)
@@ -197,9 +269,7 @@ def tile_picked_yddpm_silu_po_kernel(
             return ap.rearrange("p t (c i) -> p c t i", i=LINE)
 
         def first_layer(g):
-            h, c0 = divmod(g * P, HALF)
             cols = slice(g * P, (g + 1) * P)
-            words = [xw_first[:, cols], xw_last[h][:, c0 : c0 + P]]
             acc = psum.tile([P, PACK, P], F32, name="acc", bufs=ACC_BANKS)
             for o in range(PASSES):
                 codes, scales = w1_q[o]
@@ -208,113 +278,123 @@ def tile_picked_yddpm_silu_po_kernel(
                         out=acc[:, t, :],
                         lhsT=codes[:, t * P : (t + 1) * P].bitcast(FP8X4),
                         lhsT_scale=scales[:, t * P : (t + 1) * P],
-                        rhs=words[o].bitcast(FP8X4),
+                        rhs=xw[o][:, cols].bitcast(FP8X4),
                         rhs_scale=xs[o][:, cols],
                         start=(o == 0 and t == 0),
                         stop=(o == PASSES - 1 and t == PACK - 1),
                     )
-            pre = first_sums[:, g] if g < ACC_BANKS else keep.tile([P, PACK, P], F32, name="pre%d" % g)[:]
-            nc.vector.tensor_tensor(pre, temb_of[:, :, cols], acc[:], ALU.add)
+            pre = keep.tile([P, PACK, P], F32, name="pre%d" % g)
+            nc.vector.tensor_tensor(pre[:], temb_of[:, :, cols], acc[:], ALU.add)
             hidden[g] = keep.tile([P, P * PACK], BF16, name="hidden%d" % g, align_bytes=64)
-            nc.scalar.activation(words_order(hidden[g][:]), slots_order(pre), ACT.Silu)
-            if g == 0:
-                gather_last_words(1)
+            nc.scalar.activation(words_order(hidden[g][:]), slots_order(pre[:]), ACT.Silu)
 
         def scale_lat(g):
             q, c0 = divmod(g * P, LAT_WIDTH)
-            signal[g] = keep.tile([P, PACK, P], F32, name="signal%d" % g)
-            if g < TURNED:
-                turned = psum.tile([P, PACK, P], F32, name="back", bufs=BACK_BANKS)
+            tag = "hidden%d" % (g - TIE) if 0 <= g - TIE and MULT_ON[g] == "g" else "signal%d" % g
+            signal[g] = held([P, PACK, P], F32, "signal%d" % g, tag)
+            if MULT_ON[g] == "t":
+                turned = psum.tile([P, PACK, P], F32, name=TURN_TAG, bufs=BANKS[TURN_TAG])
                 for t in range(PACK):
                     nc.tensor.transpose(turned[:, t, :], lat_rows[q][:, t, c0 : c0 + P], ident[:])
                 nc.scalar.activation(signal[g][:], turned[:], ACT.Copy, scale=coef[:, g, 0:1])
-            else:
-                factor = csig_of[:, g * P : (g + 1) * P].unsqueeze(1).to_broadcast([P, POOL_SLOTS, P])
-                for t0 in range(0, PACK, POOL_SLOTS):
-                    slots = slice(t0, t0 + POOL_SLOTS)
-                    values = lat_rows[q][:, slots, c0 : c0 + P]
-                    nc.gpsimd.tensor_tensor(signal[g][:, slots, :], values, factor, ALU.mult)
+                return
+            width = POOL_SLOTS if MULT_ON[g] == "g" else PACK
+            engine = nc.gpsimd if MULT_ON[g] == "g" else nc.vector
+            factor = csig_of[:, g * P : (g + 1) * P].unsqueeze(1).to_broadcast([P, width, P])
+            for t0 in range(0, PACK, width):
+                slots = slice(t0, t0 + width)
+                engine.tensor_tensor(signal[g][:, slots, :], lat_rows[q][:, slots, c0 : c0 + P], factor, ALU.mult)
+
+        h_q = {}
+        h_codes_all = held([P, S], U32, "h_codes", HOLD_TAG)
+        h_scales_all = keep.tile([P, S], U8, name="h_scales", align_bytes=64)
+
+        def quantise_hidden(g):
+            h_q[g] = (h_codes_all[:, g * P : (g + 1) * P], h_scales_all[:, g * P : (g + 1) * P])
+            quantise(h_q[g][0], h_q[g][1], hidden[g][:])
 
         def second_layer(g):
-            h_codes, h_scales = planes(P, "h%d" % g)
-            quantise(h_codes[:], h_scales[:], hidden[g][:])
-            noise[g] = psum.tile([P, N], F32, name="noise", bufs=NOISE_BANKS)
+            h_codes, h_scales = h_q[g]
+            if g >= NOISE_ACC:
+                noise[g] = psum.tile([P, N], F32, name="acc", bufs=ACC_BANKS)
+            else:
+                noise[g] = psum.tile([P, N], F32, name="noise", bufs=NOISE_BANKS)
             nc.tensor.matmul_mx(
                 out=noise[g][:],
-                lhsT=h_codes[:].bitcast(FP8X4),
-                lhsT_scale=h_scales[:],
+                lhsT=h_codes.bitcast(FP8X4),
+                lhsT_scale=h_scales,
                 rhs=w2_codes[:].bitcast(FP8X4),
                 rhs_scale=w2_scales[:],
                 start=True,
                 stop=True,
             )
 
-        def by_halves(ap):
-            return ap.rearrange("p t (u m) -> p t u m", u=2)
-
-        def leaving(g):
-            c0 = g * P % PAIR
-            if g >= SINGLE_FROM:
-                return c0
-            return 0 if c0 + P == PAIR else None
-
         def combine(g):
-            c, c0 = divmod(g * P, PAIR)
+            cols = slice(g * P, (g + 1) * P)
             scaled = keep.tile([P, PACK, P], F32, name="scaled%d" % g)
-            ee = noise[g][:].rearrange("p (u t m) -> p t u m", u=2, t=PACK)
-            if g < TURNED:
-                for u in range(2):
-                    nc.vector.scalar_tensor_tensor(
-                        by_halves(scaled[:])[:, :, u],
-                        ee[:, :, u],
-                        coef[:, g, 1:2],
-                        by_halves(signal[g][:])[:, :, u],
-                        ALU.mult,
-                        ALU.subtract,
-                    )
+            flat = scaled[:].rearrange("p t m -> p (t m)")
+            if MULT_ON[g] == "t":
+                nc.vector.scalar_tensor_tensor(
+                    flat, noise[g][:], coef[:, g, 1:2], signal[g][:].rearrange("p t m -> p (t m)"), ALU.mult, ALU.subtract
+                )
+            elif SCALE_ON[g] == "v":
+                nc.vector.tensor_scalar(flat, noise[g][:], coef[:, g, 1:2], None, ALU.mult)
             else:
-                nc.scalar.activation(by_halves(scaled[:]), ee, ACT.Copy, scale=coef[:, g, 1:2])
-            if g >= GROUPS - ACC_BANKS:
+                nc.scalar.activation(flat, noise[g][:], ACT.Copy, scale=coef[:, g, 1:2])
+            if g >= BACK_ACC:
                 back = psum.tile([P, PACK, P], F32, name="acc", bufs=ACC_BANKS)
             else:
                 back = psum.tile([P, PACK, P], F32, name="back", bufs=BACK_BANKS)
             for t in range(PACK):
                 nc.tensor.transpose(back[:, t, :], scaled[:, t, :], ident[:])
-            if c0 == 0:
-                result[c] = keep.tile([P, PACK, PAIR], F32, name="result%d" % c)
-            if g < TURNED:
-                nc.scalar.activation(result[c][:, :, c0 : c0 + P], back[:], ACT.Copy, scale=-1.0)
+            if MULT_ON[g] != "t":
+                nc.vector.tensor_tensor(result[:, :, cols], signal[g][:], back[:], ALU.subtract)
+            elif COPY_ON[g] == "s":
+                nc.scalar.activation(result[:, :, cols], back[:], ACT.Copy, scale=-1.0)
             else:
-                nc.vector.tensor_tensor(result[c][:, :, c0 : c0 + P], signal[g][:], back[:], ALU.subtract)
-            first = leaving(g)
-            if first is not None:
-                rows = out_0[:, c * PAIR + first : (g + 1) * P].rearrange("(p t) s -> p t s", t=PACK)
-                nc.sync.dma_start(out=rows, in_=result[c][:, :, first : c0 + P])
+                nc.vector.tensor_scalar(result[:, :, cols], back[:], -1.0, None, ALU.mult)
+            if str(g) in STORE_AFTER:
+                place = STORE_AFTER.index(str(g))
+                done = slice((int(STORE_AFTER[place - 1]) + 1) * P if place else 0, cols.stop)
+                nc.sync.dma_start(out=out_0[:, done].rearrange("(p t) s -> p t s", t=PACK), in_=result[:, :, done])
+
+        rounded = {}
+
+        unit_first, place = {}, 0
+        for width in UNITS:
+            for g in range(place, place + int(width)):
+                unit_first[g] = (place, place + int(width) - 1)
+            place = place + int(width)
+
+        def round_result(g):
+            first, last = unit_first[g]
+            if g == first:
+                rounded[last] = keep.tile([P, (last - first + 1) * P * PACK], BF16, name="rounded%d" % g, align_bytes=64)
+            if SPLIT_ROUND or g == last:
+                begin = g if SPLIT_ROUND else first
+                into = rounded[last][:, (begin - first) * P * PACK : (g - first + 1) * P * PACK]
+                copier[ROUND_ON[g]](words_order(into), slots_order(result[:, :, begin * P : (g + 1) * P]))
 
         def hand_on(g):
-            c, c0 = divmod(g * P, PAIR)
-            first = leaving(g)
-            if first is None:
+            first, last = unit_first[g]
+            if g != last:
                 return
-            cols = slice(c * PAIR + first, (g + 1) * P)
-            rounded = keep.tile([P, (c0 + P - first) * PACK], BF16, name="rounded%d" % g, align_bytes=64)
-            values = slots_order(result[c][:, :, first : c0 + P])
-            if g == GROUPS - 1:
-                nc.vector.tensor_copy(words_order(rounded[:]), values)
-            else:
-                nc.scalar.copy(words_order(rounded[:]), values)
-            quantise(out_codes[:, cols], out_scales[:, cols], rounded[:])
-            if g in STORE_FROM:
-                done = slice(STORE_FROM[g], cols.stop)
+            cols = slice(first * P, (g + 1) * P)
+            quantise(out_codes[:, cols], out_scales[:, cols], rounded[g][:])
+            if str(g) in CODES_AFTER:
+                place = CODES_AFTER.index(str(g))
+                done = slice((int(CODES_AFTER[place - 1]) + 1) * P if place else 0, cols.stop)
                 nc.sync.dma_start(
                     out=out_1[0].rearrange("p c r -> p (c r)").bitcast(I32)[:, done],
                     in_=out_codes[:, done].bitcast(I32),
                 )
 
-        for g in range(GROUPS):
-            scale_lat(g)
-        stages = ((first_layer, 0), (second_layer, LAG_SECOND), (combine, LAG_COMBINE), (hand_on, LAG_HAND_ON))
-        for s in range(GROUPS + LAG_HAND_ON):
+        named = {"f": first_layer, "s": second_layer, "l": scale_lat, "c": combine, "h": hand_on, "q": quantise_hidden, "r": round_result}
+        stages = [(named[word[0]], int(word[1:])) for word in STAGES.split()]
+        for s in range(2 * GROUPS + 1):
+            for u in range(2):
+                if int(W2_STEP[u]) == s:
+                    prepare_w2(u)
             for stage, lag in stages:
                 if 0 <= s - lag < GROUPS:
                     stage(s - lag)

@@ -42,6 +42,23 @@ MULT_ON = "vvggggvv"
 STAGES = "f0 q1 s1 l2 c2 r8 h8"
 WORDS_FIRST = 0
 EARLY_V = 0
+LAST_TAG = "coef_rows"
+CSIG_ON = "s"
+TEMB_ON = "ssssssvv"
+FIRST_ON = "g"
+W2_WHOLE = 0
+XW_TAIL = 0
+PAIR_M = 0
+Q_UNITS = "11111111"
+JOIN_W1 = 0
+MOVES_REV = 0
+EXTRA_ACC = 0
+CLOCKS = ""
+FIRST_V = 2
+BYTES_FIRST = 1
+CHAIN = 9
+TIE_V = 9
+OUT_TAG = "out_codes"
 W1_WHOLE = 0
 STORE_AFTER = "13567"
 SCALE_ON = "ssssssss"
@@ -82,12 +99,16 @@ def tile_picked_yddpm_silu_po_kernel(
         offs_list = keep.tile([P, S // 16], U16, name="offs_list")
         temb_rows = [keep.tile([P, PACK * R], F32, name="temb_rows0")]
         temb_rows = temb_rows + [held([P, WINDOW], F32, "temb_rows%d" % t, "temb%d" % t) for t in range(1, PACK)]
-        coef_rows = keep.tile([P, WINDOW], F32, name="coef_rows")
-        xs_all = held([P, T], U8, "xs_all", "first_w1" if WORDS_FIRST else "last_words")
+        coef_rows = held([P, WINDOW], F32, "coef_rows", "first_w1" if WORDS_FIRST == 2 else "coef_rows")
+        xs_all = held([P, T], U8, "xs_all", "first_w1" if WORDS_FIRST == 1 else "last_words")
         xw_all = [held([P, T], U32, "xw_all0", "first_words"), held([P, T], U32, "xw_all1", "last_words")]
         w1_first = held([P, PACK, H], F32, "w1_first", "first_w1")
-        w1_last = held([P, 2, PACK, W_HALF], F32, "w1_last", "first_words")
-        w2_raw = [held([P, PACK, W_HALF], F32, "w2_raw%d" % u, "temb%d" % (u + 1)) for u in range(2)]
+        w1_last = held([P, 2, PACK, W_HALF], F32, "w1_last", LAST_TAG)
+        if W2_WHOLE:
+            w2_whole = held([P, PACK, N], F32, "w2_whole", "temb2")
+            w2_raw = [w2_whole[:, :, u * W_HALF : (u + 1) * W_HALF] for u in range(2)]
+        else:
+            w2_raw = [held([P, PACK, W_HALF], F32, "w2_raw%d" % u, "temb%d" % (u + 1)) for u in range(2)]
         lat_first = held([P, PACK, LAT_WIDTH], F32, "lat_first", "temb3")
         lat_late = held([P, LAT_PIECES - 1, PACK, LAT_WIDTH], F32, "lat_late", "last_words" if WORDS_FIRST else "first_w1")
         lat_rows = [lat_first[:]] + [lat_late[:, q] for q in range(LAT_PIECES - 1)]
@@ -115,18 +136,30 @@ def tile_picked_yddpm_silu_po_kernel(
         def load_slots(slots, rows):
             nc.sync.dma_start(out=slots, in_=rows.rearrange("(p t) c -> p t c", t=PACK))
 
+        def load_bytes():
+            nc.sync.dma_start(offs_list[:], offs)
+            nc.sync.dma_start(
+                out=xs_all[last_quadrant:, :].bitcast(I32), in_=x_scales.rearrange("o q c -> (o q) c").bitcast(I32)
+            )
+
+        def load_coef():
+            nc.sync.dma_start(out=coef_rows[last_quadrant : P - COEF_ROWS, :R], in_=csig[:COEF_ROWS, :])
+            nc.sync.dma_start(out=coef_rows[P - COEF_ROWS :, :R], in_=cnoise[:COEF_ROWS, :])
+
+        if BYTES_FIRST:
+            load_bytes()
         nc.sync.dma_start(step_list[:], step)
-        nc.sync.dma_start(out=coef_rows[last_quadrant : P - COEF_ROWS, :R], in_=csig[:COEF_ROWS, :])
-        nc.sync.dma_start(out=coef_rows[P - COEF_ROWS :, :R], in_=cnoise[:COEF_ROWS, :])
+        if not BYTES_FIRST:
+            load_coef()
         nc.sync.dma_start(out=temb_rows[0][:], in_=temb.rearrange("(p t) r -> p (t r)", t=PACK))
-        nc.sync.dma_start(offs_list[:], offs)
-        nc.sync.dma_start(
-            out=xs_all[last_quadrant:, :].bitcast(I32), in_=x_scales.rearrange("o q c -> (o q) c").bitcast(I32)
-        )
+        if BYTES_FIRST:
+            load_coef()
+        else:
+            load_bytes()
         load_words(0)
         if not WORDS_FIRST:
             load_slots(w1_first[:], w1[:K_PASS, :])
-        else:
+        elif WORDS_FIRST == 1:
             load_words(1)
 
         def half_of(offsets, h):
@@ -137,12 +170,13 @@ def tile_picked_yddpm_silu_po_kernel(
 
         picked = keep.tile([P, S], U8, name="picked", align_bytes=64)
         nc.vector.tensor_copy(picked[:], xs_all[:].indirect(offs_list[:]))
-        for o in range(PASSES):
-            if o == PASSES - 1:
+        for place in range(PASSES):
+            o = PASSES - 1 - place if MOVES_REV else place
+            if place == PASSES - 1:
+                if WORDS_FIRST != 1:
+                    load_words(place)
                 if WORDS_FIRST:
                     load_slots(w1_first[:], w1[:K_PASS, :])
-                else:
-                    load_words(o)
             for r in range(4):
                 first = last_quadrant + SCALE_ROWS * o + r
                 (nc.sync if MOVES_ON[o] == "s" else nc.gpsimd).dma_start(
@@ -157,7 +191,10 @@ def tile_picked_yddpm_silu_po_kernel(
         for name in LATE_ORDER + "".join(c for c in "ABCD"[:LAT_PIECES] if c not in LATE_ORDER):
             if name in "ab":
                 u = "ab".index(name)
-                load_slots(w2_raw[u][:], w2[:, u * W_HALF : (u + 1) * W_HALF])
+                if not W2_WHOLE:
+                    load_slots(w2_raw[u][:], w2[:, u * W_HALF : (u + 1) * W_HALF])
+                elif u == 0:
+                    load_slots(w2_whole[:], w2)
             else:
                 q = "ABCD".index(name)
                 load_slots(lat_rows[q], lat[:, q * LAT_WIDTH : (q + 1) * LAT_WIDTH])
@@ -166,15 +203,19 @@ def tile_picked_yddpm_silu_po_kernel(
 
         def gather_temb(t):
             for h in range(halves):
-                nc.scalar.activation(
-                    temb_of[:, t, h * HALF : (h + 1) * HALF], temb_rows[t][:].indirect(half_of(step_list, h)), ACT.Copy
-                )
+                into, window = temb_of[:, t, h * HALF : (h + 1) * HALF], temb_rows[t][:].indirect(half_of(step_list, h))
+                if TEMB_ON[2 * t + h] == "s":
+                    nc.scalar.activation(into, window, ACT.Copy)
+                else:
+                    nc.vector.tensor_copy(into, window)
 
         gather_temb(0)
         gather_temb(1)
         coef_of = keep.tile([P, S], F32, name="coef_of")
         coef = keep.tile([P, GROUPS, 2], F32, name="coef")
-        csig_of = keep.tile([P, S], F32, name="csig_of")
+        csig_all = keep.tile([P, S], F32, name="csig_all")
+        csig_of = [csig_all[:, g * P : (g + 1) * P] for g in range(GROUPS)]
+        csig_pair = [csig_all[:, c * PAIR : (c + 1) * PAIR] for c in range(GROUPS // 2)]
         for h in range(halves):
             nc.vector.tensor_copy(coef_of[:, h * HALF : (h + 1) * HALF], coef_rows[:].indirect(half_of(step_list, h)))
             bank = psum.tile([P, per_half, P], F32, name="back", bufs=BACK_BANKS)
@@ -189,7 +230,7 @@ def tile_picked_yddpm_silu_po_kernel(
             for b in range(per_half):
                 g = h * per_half + b
                 nc.tensor.transpose(bank[:, b, :], coef[:, g, 0:1].to_broadcast([P, P]), ident[:])
-            nc.vector.tensor_copy(csig_of[:, h * HALF : (h + 1) * HALF], bank[:].rearrange("p b j -> p (b j)"))
+            (nc.vector.tensor_copy if CSIG_ON == "v" else nc.scalar.copy)(csig_all[:, h * HALF : (h + 1) * HALF], bank[:].rearrange("p b j -> p (b j)"))
 
         def deal(copy, raw, name):
             slots = raw.shape[3]
@@ -219,14 +260,15 @@ def tile_picked_yddpm_silu_po_kernel(
         nc.vector.tensor_copy(xw[0][:], xw_all[0][:].indirect(offs_list[:]))
         if WORDS_FIRST:
             nc.vector.tensor_copy(xw[1][:], xw_all[1][:].indirect(offs_list[:]))
-            for u in range(2):
-                dealt = deal(copier["sv"[u]], by_slot(w1_first[:])[:, :, :, 2 * u : 2 * u + 2], "w1_first%d" % u)
-                cols = slice(u * W_HALF, (u + 1) * W_HALF)
-                quantise(w1_q[0][0][:, cols], w1_q[0][1][:, cols], dealt[:])
+            for copy, first, end in ((nc.vector.tensor_copy, 0, FIRST_V), (nc.scalar.copy, FIRST_V, PACK)):
+                if end > first:
+                    dealt = deal(copy, by_slot(w1_first[:])[:, :, :, first:end], "w1_first%d" % end)
+                    quantise(w1_q[0][0][:, first * P : end * P], w1_q[0][1][:, first * P : end * P], dealt[:])
         else:
-            dealt = deal(nc.vector.tensor_copy, by_slot(w1_first[:]), "w1_first_dealt")
+            dealt = deal(copier[FIRST_ON], by_slot(w1_first[:]), "w1_first_dealt")
             quantise(w1_q[0][0][:], w1_q[0][1][:], dealt[:])
-            nc.vector.tensor_copy(xw[1][:], xw_all[1][:].indirect(offs_list[:]))
+            head = S - XW_TAIL
+            nc.vector.tensor_copy(xw[1][:, :head], xw_all[1][:].indirect(offs_list[:, : head // 16]))
 
         def quantise_slots(dealt, first, count, u):
             for t in range(count):
@@ -240,13 +282,30 @@ def tile_picked_yddpm_silu_po_kernel(
                 parts.append((deal(copy, by_slot(w1_whole)[:, :, :, first:end], "w1_whole%d" % end), first, end))
             for dealt, first, end in parts:
                 quantise(w1_q[1][0][:, first * P : end * P], w1_q[1][1][:, first * P : end * P], dealt[:])
-        for u, split in enumerate(() if W1_WHOLE else (EARLY_V, LATE_V)):
+        if JOIN_W1:
+            joined = keep.tile([P, PACK * H], BF16, name="w1_joined", align_bytes=64)
+            view = joined[:].rearrange("p (t u m j) -> p u m t j", t=PACK, u=2, j=PACK)
+            for u, split in enumerate((EARLY_V, LATE_V)):
+                raw = by_slot(w1_last[:, u]).rearrange("p j m t -> p m t j")
+                for copy, first, end in ((nc.scalar.copy, split, PACK), (nc.vector.tensor_copy, 0, split)):
+                    if end > first:
+                        copy(view[:, u, :, first:end, :], raw[:, :, first:end, :])
+            for first, end in ((0, LATE_V), (LATE_V, PACK)):
+                quantise(
+                    w1_q[1][0][:, first * P : end * P],
+                    w1_q[1][1][:, first * P : end * P],
+                    joined[:, first * K_PASS : end * K_PASS],
+                )
+        for u, split in enumerate(() if W1_WHOLE or JOIN_W1 else (EARLY_V, LATE_V)):
             raw = by_slot(w1_last[:, u])
             for copy, first, end in ((nc.scalar.copy, split, PACK), (nc.vector.tensor_copy, 0, split)):
                 if end > first:
                     shares.append((deal(copy, raw[:, :, :, first:end], "w1_last%d%d" % (u, end)), first, end - first, u))
         for share in shares:
             quantise_slots(*share)
+        if XW_TAIL:
+            xw_tail = held([P, XW_TAIL], U32, "xw_tail", "w1_last1%d" % LATE_V)
+            nc.vector.tensor_copy(xw_tail[:], xw_all[1][:].indirect(offs_list[:, (S - XW_TAIL) // 16 :]))
 
         w2_codes, w2_scales = planes(N, "w2")
 
@@ -258,8 +317,9 @@ def tile_picked_yddpm_silu_po_kernel(
             if u == 1:
                 quantise(w2_codes[:], w2_scales[:], w2_dealt[:])
 
-        out_codes, out_scales = planes(S, "out")
-        hidden, noise, signal = {}, {}, {}
+        out_codes = held([P, S], U32, "out_codes", OUT_TAG)
+        out_scales = keep.tile([P, S], U8, name="out_scales", align_bytes=64)
+        hidden, noise, signal, parts = {}, {}, {}, {}
         result = keep.tile([P, PACK, S], F32, name="result")
 
         def words_order(ap):
@@ -268,9 +328,33 @@ def tile_picked_yddpm_silu_po_kernel(
         def slots_order(ap):
             return ap.rearrange("p t (c i) -> p c t i", i=LINE)
 
+        extra = {
+            ACC_BANKS + b: psum.tile([P, PACK, P], F32, name="back", bufs=BACK_BANKS) for b in range(EXTRA_ACC)
+        }
+
+        q_unit, place = {}, 0
+        for width in Q_UNITS:
+            for g in range(place, place + int(width)):
+                q_unit[g] = (place, place + int(width) - 1)
+            place = place + int(width)
+
+        def words_of(o, g):
+            past = g * P - (S - XW_TAIL)
+            if o == 1 and past >= 0:
+                return xw_tail[:, past : past + P]
+            return xw[o][:, g * P : (g + 1) * P]
+
+        def clock(name, ap):
+            if name in CLOCKS.split():
+                tick = keep.tile([P, 1], F32, name="tick_" + name)
+                nc.gpsimd.tensor_copy(tick[:], ap)
+
         def first_layer(g):
             cols = slice(g * P, (g + 1) * P)
-            acc = psum.tile([P, PACK, P], F32, name="acc", bufs=ACC_BANKS)
+            if g in extra:
+                acc = extra[g]
+            else:
+                acc = psum.tile([P, PACK, P], F32, name="acc", bufs=ACC_BANKS)
             for o in range(PASSES):
                 codes, scales = w1_q[o]
                 for t in range(PACK):
@@ -278,20 +362,43 @@ def tile_picked_yddpm_silu_po_kernel(
                         out=acc[:, t, :],
                         lhsT=codes[:, t * P : (t + 1) * P].bitcast(FP8X4),
                         lhsT_scale=scales[:, t * P : (t + 1) * P],
-                        rhs=xw[o][:, cols].bitcast(FP8X4),
+                        rhs=words_of(o, g).bitcast(FP8X4),
                         rhs_scale=xs[o][:, cols],
                         start=(o == 0 and t == 0),
                         stop=(o == PASSES - 1 and t == PACK - 1),
                     )
             pre = keep.tile([P, PACK, P], F32, name="pre%d" % g)
             nc.vector.tensor_tensor(pre[:], temb_of[:, :, cols], acc[:], ALU.add)
-            hidden[g] = keep.tile([P, P * PACK], BF16, name="hidden%d" % g, align_bytes=64)
+            first, last = q_unit[g]
+            if g == first:
+                hidden["unit"] = keep.tile([P, (last - first + 1) * K_PASS], BF16, name="hidden%d" % last, align_bytes=64)
+                hidden["unit", last] = hidden["unit"]
+            hidden[g] = hidden["unit"][:, (g - first) * K_PASS : (g - first + 1) * K_PASS]
             nc.scalar.activation(words_order(hidden[g][:]), slots_order(pre[:]), ACT.Silu)
+            clock("pre%d" % g, pre[:, 0, 0:1])
 
         def scale_lat(g):
             q, c0 = divmod(g * P, LAT_WIDTH)
-            tag = "hidden%d" % (g - TIE) if 0 <= g - TIE and MULT_ON[g] == "g" else "signal%d" % g
-            signal[g] = held([P, PACK, P], F32, "signal%d" % g, tag)
+            tag = "hidden%d" % (g - TIE) if 0 <= g - TIE and (MULT_ON[g] == "g" or g >= TIE_V) else "signal%d" % g
+            if MULT_ON[g] != "h" and g not in signal:
+                signal[g] = held([P, PACK, P], F32, "signal%d" % g, tag)
+            if PAIR_M and MULT_ON[g - g % 2 : g - g % 2 + 2] == "vv":
+                if g % 2 == 0:
+                    both = keep.tile([P, PACK, PAIR], F32, name="both%d" % g)
+                    factor = csig_pair[g // 2][:].unsqueeze(1).to_broadcast([P, PACK, PAIR])
+                    nc.vector.tensor_tensor(both[:], lat_rows[q][:, :, c0 : c0 + PAIR], factor, ALU.mult)
+                    signal[g], signal[g + 1] = both[:, :, :P], both[:, :, P:]
+                return
+            if MULT_ON[g] == "h":
+                for engine, first, end, tag in (
+                    (nc.gpsimd, 0, POOL_SLOTS, "hidden%d" % (g - TIE)),
+                    (nc.vector, POOL_SLOTS, PACK, "own%d" % g),
+                ):
+                    part = held([P, end - first, P], F32, "part%d%d" % (g, first), tag)
+                    factor = csig_of[g][:].unsqueeze(1).to_broadcast([P, end - first, P])
+                    engine.tensor_tensor(part[:], lat_rows[q][:, first:end, c0 : c0 + P], factor, ALU.mult)
+                    parts[g, first] = (part, end)
+                return
             if MULT_ON[g] == "t":
                 turned = psum.tile([P, PACK, P], F32, name=TURN_TAG, bufs=BANKS[TURN_TAG])
                 for t in range(PACK):
@@ -300,17 +407,30 @@ def tile_picked_yddpm_silu_po_kernel(
                 return
             width = POOL_SLOTS if MULT_ON[g] == "g" else PACK
             engine = nc.gpsimd if MULT_ON[g] == "g" else nc.vector
-            factor = csig_of[:, g * P : (g + 1) * P].unsqueeze(1).to_broadcast([P, width, P])
+            factor = csig_of[g][:].unsqueeze(1).to_broadcast([P, width, P])
             for t0 in range(0, PACK, width):
                 slots = slice(t0, t0 + width)
                 engine.tensor_tensor(signal[g][:, slots, :], lat_rows[q][:, slots, c0 : c0 + P], factor, ALU.mult)
 
         h_q = {}
-        h_codes_all = held([P, S], U32, "h_codes", HOLD_TAG)
         h_scales_all = keep.tile([P, S], U8, name="h_scales", align_bytes=64)
 
         def quantise_hidden(g):
-            h_q[g] = (h_codes_all[:, g * P : (g + 1) * P], h_scales_all[:, g * P : (g + 1) * P])
+            before = g - CHAIN
+            if CHAIN == 9:
+                if g == 0:
+                    h_q["all"] = held([P, S], U32, "h_codes", HOLD_TAG)
+                h_q[g] = (h_q["all"][:, g * P : (g + 1) * P], h_scales_all[:, g * P : (g + 1) * P])
+                first, last = q_unit[g]
+                if g == first:
+                    cols = slice(first * P, (last + 1) * P)
+                    quantise(h_q["all"][:, cols], h_scales_all[:, cols], hidden["unit", last][:])
+                return
+            if 0 <= before < GROUPS and MULT_ON[before] == "g":
+                tag = "csig%d" % before
+            else:
+                tag = HOLD_TAG if g == 0 else "h_codes%d" % g
+            h_q[g] = (held([P, P], U32, "h_codes%d" % g, tag)[:], h_scales_all[:, g * P : (g + 1) * P])
             quantise(h_q[g][0], h_q[g][1], hidden[g][:])
 
         def second_layer(g):
@@ -347,7 +467,11 @@ def tile_picked_yddpm_silu_po_kernel(
                 back = psum.tile([P, PACK, P], F32, name="back", bufs=BACK_BANKS)
             for t in range(PACK):
                 nc.tensor.transpose(back[:, t, :], scaled[:, t, :], ident[:])
-            if MULT_ON[g] != "t":
+            if MULT_ON[g] == "h":
+                for first in (POOL_SLOTS, 0):
+                    part, end = parts[g, first]
+                    nc.vector.tensor_tensor(result[:, first:end, cols], part[:], back[:, first:end, :], ALU.subtract)
+            elif MULT_ON[g] != "t":
                 nc.vector.tensor_tensor(result[:, :, cols], signal[g][:], back[:], ALU.subtract)
             elif COPY_ON[g] == "s":
                 nc.scalar.activation(result[:, :, cols], back[:], ACT.Copy, scale=-1.0)

@@ -29,56 +29,15 @@ WINDOW = HALF + 16
 COEF_ROWS = QUADRANT // 2
 W_HALF = 256
 M_HALF = W_HALF // PACK
-LAT_WIDTH = 512
-LAT_PIECES = S // LAT_WIDTH
+SCALAR_SLOTS = 3
+VECTOR_DEALS = 2
+POOL_GROUPS = range(2, 6)
 POOL_SLOTS = 2
-PAIR = 2 * P
-SINGLE_FROM = GROUPS - 2
-LATE_ORDER = "abA"
-TIE = 0
-ROUND_ON = "sssssssv"
-W2_DEAL = "sg"
-MULT_ON = "vvggggvv"
-STAGES = "f0 q1 s1 l2 c2 r8 h8"
-WORDS_FIRST = 0
-EARLY_V = 0
-LAST_TAG = "coef_rows"
-CSIG_ON = "s"
-TEMB_ON = "ssssssvv"
-FIRST_ON = "g"
-W2_WHOLE = 0
-XW_TAIL = 0
-PAIR_M = 0
-Q_UNITS = "11111111"
-JOIN_W1 = 0
-MOVES_REV = 0
-EXTRA_ACC = 0
-CLOCKS = ""
-FIRST_V = 2
-BYTES_FIRST = 1
-CHAIN = 9
-TIE_V = 9
-OUT_TAG = "out_codes"
-W1_WHOLE = 0
-STORE_AFTER = "13567"
-SCALE_ON = "ssssssss"
-UNITS = "22211"
-SPLIT_ROUND = 1
-HOLD_TAG = "temb2"
-MOVES_ON = "ss"
-TURN_TAG = "back"
-COPY_ON = "ssssssss"
-ACC_BANKS = 3
-NOISE_BANKS = 2
-BACK_BANKS = 3
-W2_STEP = "00"
-NOISE_ACC = 9
-BACK_ACC = 5
-HOLD_ROUND = 0
-CODES_AFTER = "357"
-LATE_V = 2
-
-BANKS = {"back": BACK_BANKS, "noise": NOISE_BANKS, "acc": ACC_BANKS, "turn": 1}
+VECTOR_ROUNDS = (4, 5, 7)
+PAIRED = GROUPS - 2
+LAG_SECOND, LAG_COMBINE, LAG_HAND_ON = 1, 2, GROUPS
+ACC_BANKS, NOISE_BANKS, BACK_BANKS = 3, 2, 3
+CODES_FROM = {3: 0, 5: 4, 7: 6}
 
 
 def tile_picked_yddpm_silu_po_kernel(
@@ -92,26 +51,21 @@ def tile_picked_yddpm_silu_po_kernel(
         keep = ctx.enter_context(tc.tile_pool(name="keep", bufs=1))
         psum = ctx.enter_context(tc.psum_pool(name="psum", bufs=1))
 
-        def held(shape, dtype, name, tag):
+        def tagged(shape, dtype, name, tag):
             return keep.tile(shape, dtype, name=name, tag=tag, align_bytes=64)
 
         step_list = keep.tile([P, S // 16], U16, name="step_list")
         offs_list = keep.tile([P, S // 16], U16, name="offs_list")
-        temb_rows = [keep.tile([P, PACK * R], F32, name="temb_rows0")]
-        temb_rows = temb_rows + [held([P, WINDOW], F32, "temb_rows%d" % t, "temb%d" % t) for t in range(1, PACK)]
-        coef_rows = held([P, WINDOW], F32, "coef_rows", "first_w1" if WORDS_FIRST == 2 else "coef_rows")
-        xs_all = held([P, T], U8, "xs_all", "first_w1" if WORDS_FIRST == 1 else "last_words")
-        xw_all = [held([P, T], U32, "xw_all0", "first_words"), held([P, T], U32, "xw_all1", "last_words")]
-        w1_first = held([P, PACK, H], F32, "w1_first", "first_w1")
-        w1_last = held([P, 2, PACK, W_HALF], F32, "w1_last", LAST_TAG)
-        if W2_WHOLE:
-            w2_whole = held([P, PACK, N], F32, "w2_whole", "temb2")
-            w2_raw = [w2_whole[:, :, u * W_HALF : (u + 1) * W_HALF] for u in range(2)]
-        else:
-            w2_raw = [held([P, PACK, W_HALF], F32, "w2_raw%d" % u, "temb%d" % (u + 1)) for u in range(2)]
-        lat_first = held([P, PACK, LAT_WIDTH], F32, "lat_first", "temb3")
-        lat_late = held([P, LAT_PIECES - 1, PACK, LAT_WIDTH], F32, "lat_late", "last_words" if WORDS_FIRST else "first_w1")
-        lat_rows = [lat_first[:]] + [lat_late[:, q] for q in range(LAT_PIECES - 1)]
+        temb_rows = [keep.tile([P, PACK * R], F32, name="temb_rows0")] + [
+            tagged([P, WINDOW], F32, "temb_rows%d" % t, "temb%d" % t) for t in range(1, PACK)
+        ]
+        coef_rows = tagged([P, WINDOW], F32, "coef_rows", "coef_window")
+        xs_all = tagged([P, T], U8, "xs_all", "last_words")
+        xw_all = [keep.tile([P, T], U32, name="xw_all0", align_bytes=64), tagged([P, T], U32, "xw_all1", "last_words")]
+        w1_first = tagged([P, PACK, H], F32, "w1_first", "first_w1")
+        w1_last = tagged([P, 2, PACK, W_HALF], F32, "w1_last", "coef_window")
+        w2_raw = [tagged([P, PACK, W_HALF], F32, "w2_raw%d" % u, "temb%d" % (u + 1)) for u in range(2)]
+        lat_rows = [tagged([P, PACK, HALF], F32, "lat_rows%d" % h, tag) for h, tag in enumerate(("temb3", "first_w1"))]
         ident = keep.tile([P, P], F32, name="ident")
         xs_both = keep.tile([P, PASSES * S], U8, name="xs_both", align_bytes=64)
         xs = [xs_both[:, o * S : (o + 1) * S] for o in range(PASSES)]
@@ -136,116 +90,84 @@ def tile_picked_yddpm_silu_po_kernel(
         def load_slots(slots, rows):
             nc.sync.dma_start(out=slots, in_=rows.rearrange("(p t) c -> p t c", t=PACK))
 
-        def load_bytes():
-            nc.sync.dma_start(offs_list[:], offs)
-            nc.sync.dma_start(
-                out=xs_all[last_quadrant:, :].bitcast(I32), in_=x_scales.rearrange("o q c -> (o q) c").bitcast(I32)
-            )
-
-        def load_coef():
-            nc.sync.dma_start(out=coef_rows[last_quadrant : P - COEF_ROWS, :R], in_=csig[:COEF_ROWS, :])
-            nc.sync.dma_start(out=coef_rows[P - COEF_ROWS :, :R], in_=cnoise[:COEF_ROWS, :])
-
-        if BYTES_FIRST:
-            load_bytes()
+        nc.sync.dma_start(offs_list[:], offs)
+        nc.sync.dma_start(
+            out=xs_all[last_quadrant:, :].bitcast(I32), in_=x_scales.rearrange("o q c -> (o q) c").bitcast(I32)
+        )
         nc.sync.dma_start(step_list[:], step)
-        if not BYTES_FIRST:
-            load_coef()
         nc.sync.dma_start(out=temb_rows[0][:], in_=temb.rearrange("(p t) r -> p (t r)", t=PACK))
-        if BYTES_FIRST:
-            load_coef()
-        else:
-            load_bytes()
+        nc.sync.dma_start(out=coef_rows[last_quadrant : P - COEF_ROWS, :R], in_=csig[:COEF_ROWS, :])
+        nc.sync.dma_start(out=coef_rows[P - COEF_ROWS :, :R], in_=cnoise[:COEF_ROWS, :])
         load_words(0)
-        if not WORDS_FIRST:
-            load_slots(w1_first[:], w1[:K_PASS, :])
-        elif WORDS_FIRST == 1:
-            load_words(1)
+        load_slots(w1_first[:], w1[:K_PASS, :])
 
-        def half_of(offsets, h):
-            return offsets[:, h * HALF // 16 : (h + 1) * HALF // 16]
-
-        for t in range(1, PACK):
-            nc.vector.tensor_copy(temb_rows[t][:, :R], temb_rows[0][:, t * R : (t + 1) * R])
+        for t in list(range(SCALAR_SLOTS, PACK)) + list(range(1, SCALAR_SLOTS)):
+            nc.gpsimd.tensor_copy(temb_rows[t][:, :R], temb_rows[0][:, t * R : (t + 1) * R])
 
         picked = keep.tile([P, S], U8, name="picked", align_bytes=64)
         nc.vector.tensor_copy(picked[:], xs_all[:].indirect(offs_list[:]))
-        for place in range(PASSES):
-            o = PASSES - 1 - place if MOVES_REV else place
-            if place == PASSES - 1:
-                if WORDS_FIRST != 1:
-                    load_words(place)
-                if WORDS_FIRST:
-                    load_slots(w1_first[:], w1[:K_PASS, :])
+
+        def move_scales(o):
             for r in range(4):
                 first = last_quadrant + SCALE_ROWS * o + r
-                (nc.sync if MOVES_ON[o] == "s" else nc.gpsimd).dma_start(
-                    out=xs[o][r:P:QUADRANT, :].bitcast(I32), in_=picked[first : first + SCALE_ROWS - r : 4, :].bitcast(I32)
+                nc.sync.dma_start(
+                    out=xs[o][r:P:QUADRANT, :].bitcast(I32),
+                    in_=picked[first : first + SCALE_ROWS - r : 4, :].bitcast(I32),
                 )
-        w1_whole = w1_last[:].rearrange("p u j c -> p (u j c)").rearrange("p (j c) -> p j c", j=PACK)
-        if W1_WHOLE:
-            load_slots(w1_whole, w1[K_PASS:, :])
-        else:
-            for u in range(2):
-                load_slots(w1_last[:, u], w1[K_PASS:, u * W_HALF : (u + 1) * W_HALF])
-        for name in LATE_ORDER + "".join(c for c in "ABCD"[:LAT_PIECES] if c not in LATE_ORDER):
-            if name in "ab":
-                u = "ab".index(name)
-                if not W2_WHOLE:
-                    load_slots(w2_raw[u][:], w2[:, u * W_HALF : (u + 1) * W_HALF])
-                elif u == 0:
-                    load_slots(w2_whole[:], w2)
-            else:
-                q = "ABCD".index(name)
-                load_slots(lat_rows[q], lat[:, q * LAT_WIDTH : (q + 1) * LAT_WIDTH])
+
+        move_scales(1)
+        load_words(1)
+        move_scales(0)
+        for u in range(2):
+            load_slots(w1_last[:, u], w1[K_PASS:, u * W_HALF : (u + 1) * W_HALF])
+        for u in range(2):
+            load_slots(w2_raw[u][:], w2[:, u * W_HALF : (u + 1) * W_HALF])
+        for h in range(halves):
+            load_slots(lat_rows[h][:], lat[:, h * HALF : (h + 1) * HALF])
+
+        def half_of_step(h):
+            return step_list[:, h * HALF // 16 : (h + 1) * HALF // 16]
 
         temb_of = keep.tile([P, PACK, S], F32, name="temb_of")
 
         def gather_temb(t):
             for h in range(halves):
-                into, window = temb_of[:, t, h * HALF : (h + 1) * HALF], temb_rows[t][:].indirect(half_of(step_list, h))
-                if TEMB_ON[2 * t + h] == "s":
-                    nc.scalar.activation(into, window, ACT.Copy)
+                looked_up = temb_rows[t][:].indirect(half_of_step(h))
+                if t < SCALAR_SLOTS:
+                    nc.scalar.activation(temb_of[:, t, h * HALF : (h + 1) * HALF], looked_up, ACT.Copy)
                 else:
-                    nc.vector.tensor_copy(into, window)
+                    nc.vector.tensor_copy(temb_of[:, t, h * HALF : (h + 1) * HALF], looked_up)
 
         gather_temb(0)
         gather_temb(1)
         coef_of = keep.tile([P, S], F32, name="coef_of")
         coef = keep.tile([P, GROUPS, 2], F32, name="coef")
-        csig_all = keep.tile([P, S], F32, name="csig_all")
-        csig_of = [csig_all[:, g * P : (g + 1) * P] for g in range(GROUPS)]
-        csig_pair = [csig_all[:, c * PAIR : (c + 1) * PAIR] for c in range(GROUPS // 2)]
+        csig_of = keep.tile([P, S], F32, name="csig_of")
         for h in range(halves):
-            nc.vector.tensor_copy(coef_of[:, h * HALF : (h + 1) * HALF], coef_rows[:].indirect(half_of(step_list, h)))
+            nc.vector.tensor_copy(coef_of[:, h * HALF : (h + 1) * HALF], coef_rows[:].indirect(half_of_step(h)))
             bank = psum.tile([P, per_half, P], F32, name="back", bufs=BACK_BANKS)
             for b in range(per_half):
                 g = h * per_half + b
                 nc.tensor.transpose(bank[:, b, :], coef_of[:, g * P : (g + 1) * P], ident[:])
-            nc.vector.tensor_copy(coef[:, h * per_half : (h + 1) * per_half, :], bank[:, :, last_quadrant:P:COEF_ROWS])
+            nc.scalar.copy(coef[:, h * per_half : (h + 1) * per_half, :], bank[:, :, last_quadrant:P:COEF_ROWS])
         gather_temb(2)
         gather_temb(3)
         for h in range(halves):
             bank = psum.tile([P, per_half, P], F32, name="noise", bufs=NOISE_BANKS)
             for b in range(per_half):
-                g = h * per_half + b
-                nc.tensor.transpose(bank[:, b, :], coef[:, g, 0:1].to_broadcast([P, P]), ident[:])
-            (nc.vector.tensor_copy if CSIG_ON == "v" else nc.scalar.copy)(csig_all[:, h * HALF : (h + 1) * HALF], bank[:].rearrange("p b j -> p (b j)"))
-
-        def deal(copy, raw, name):
-            slots = raw.shape[3]
-            width = raw.shape[2] * slots
-            dealt = keep.tile([P, PACK * width], BF16, name=name, align_bytes=64)
-            copy(dealt[:].rearrange("p (t m j) -> p m t j", t=slots, j=PACK), raw.rearrange("p j m t -> p m t j"))
-            return dealt
+                nc.tensor.transpose(bank[:, b, :], coef[:, h * per_half + b, 0:1].to_broadcast([P, P]), ident[:])
+            nc.scalar.copy(csig_of[:, h * HALF : (h + 1) * HALF], bank[:].rearrange("p b j -> p (b j)"))
 
         def pool_copy(out, in_):
             nc.gpsimd.tensor_scalar(out, in_, 1.0, 0.0, ALU.mult, ALU.add)
 
-        copier = {"s": nc.scalar.copy, "v": nc.vector.tensor_copy, "g": pool_copy}
-
         def by_slot(raw):
-            return raw.rearrange("p j (m t) -> p j m t", t=PACK)
+            return raw.rearrange("p j (m t) -> p m t j", t=PACK)
+
+        def deal(copy, values, name):
+            dealt = keep.tile([P, values.shape[1] * values.shape[2] * PACK], BF16, name=name, align_bytes=64)
+            copy(dealt[:].rearrange("p (t m j) -> p m t j", t=values.shape[2], j=PACK), values)
+            return dealt
 
         def planes(width, name):
             codes = keep.tile([P, width], U32, name=name + "_codes", align_bytes=64)
@@ -258,69 +180,35 @@ def tile_picked_yddpm_silu_po_kernel(
         xw = [keep.tile([P, S], U32, name="xw%d" % o, align_bytes=64) for o in range(PASSES)]
         w1_q = [planes(H, "w1_%d" % o) for o in range(PASSES)]
         nc.vector.tensor_copy(xw[0][:], xw_all[0][:].indirect(offs_list[:]))
-        if WORDS_FIRST:
-            nc.vector.tensor_copy(xw[1][:], xw_all[1][:].indirect(offs_list[:]))
-            for copy, first, end in ((nc.vector.tensor_copy, 0, FIRST_V), (nc.scalar.copy, FIRST_V, PACK)):
-                if end > first:
-                    dealt = deal(copy, by_slot(w1_first[:])[:, :, :, first:end], "w1_first%d" % end)
-                    quantise(w1_q[0][0][:, first * P : end * P], w1_q[0][1][:, first * P : end * P], dealt[:])
-        else:
-            dealt = deal(copier[FIRST_ON], by_slot(w1_first[:]), "w1_first_dealt")
-            quantise(w1_q[0][0][:], w1_q[0][1][:], dealt[:])
-            head = S - XW_TAIL
-            nc.vector.tensor_copy(xw[1][:, :head], xw_all[1][:].indirect(offs_list[:, : head // 16]))
+        first_dealt = deal(pool_copy, by_slot(w1_first[:]), "w1_first_dealt")
+        quantise(w1_q[0][0][:], w1_q[0][1][:], first_dealt[:])
+        nc.vector.tensor_copy(xw[1][:], xw_all[1][:].indirect(offs_list[:]))
 
-        def quantise_slots(dealt, first, count, u):
-            for t in range(count):
-                cols = slice((first + t) * P + u * M_HALF, (first + t) * P + (u + 1) * M_HALF)
-                quantise(w1_q[1][0][:, cols], w1_q[1][1][:, cols], dealt[:, t * W_HALF : (t + 1) * W_HALF])
-
-        shares = []
-        if W1_WHOLE:
-            parts = []
-            for copy, first, end in ((nc.scalar.copy, LATE_V, PACK), (nc.vector.tensor_copy, 0, LATE_V)):
-                parts.append((deal(copy, by_slot(w1_whole)[:, :, :, first:end], "w1_whole%d" % end), first, end))
-            for dealt, first, end in parts:
-                quantise(w1_q[1][0][:, first * P : end * P], w1_q[1][1][:, first * P : end * P], dealt[:])
-        if JOIN_W1:
-            joined = keep.tile([P, PACK * H], BF16, name="w1_joined", align_bytes=64)
-            view = joined[:].rearrange("p (t u m j) -> p u m t j", t=PACK, u=2, j=PACK)
-            for u, split in enumerate((EARLY_V, LATE_V)):
-                raw = by_slot(w1_last[:, u]).rearrange("p j m t -> p m t j")
-                for copy, first, end in ((nc.scalar.copy, split, PACK), (nc.vector.tensor_copy, 0, split)):
-                    if end > first:
-                        copy(view[:, u, :, first:end, :], raw[:, :, first:end, :])
-            for first, end in ((0, LATE_V), (LATE_V, PACK)):
-                quantise(
-                    w1_q[1][0][:, first * P : end * P],
-                    w1_q[1][1][:, first * P : end * P],
-                    joined[:, first * K_PASS : end * K_PASS],
-                )
-        for u, split in enumerate(() if W1_WHOLE or JOIN_W1 else (EARLY_V, LATE_V)):
-            raw = by_slot(w1_last[:, u])
-            for copy, first, end in ((nc.scalar.copy, split, PACK), (nc.vector.tensor_copy, 0, split)):
-                if end > first:
-                    shares.append((deal(copy, raw[:, :, :, first:end], "w1_last%d%d" % (u, end)), first, end - first, u))
-        for share in shares:
-            quantise_slots(*share)
-        if XW_TAIL:
-            xw_tail = held([P, XW_TAIL], U32, "xw_tail", "w1_last1%d" % LATE_V)
-            nc.vector.tensor_copy(xw_tail[:], xw_all[1][:].indirect(offs_list[:, (S - XW_TAIL) // 16 :]))
+        shares = (
+            (nc.scalar.copy, 0, 0, PACK),
+            (nc.scalar.copy, 1, VECTOR_DEALS, PACK),
+            (nc.vector.tensor_copy, 1, 0, VECTOR_DEALS),
+        )
+        last_dealt = [
+            deal(copy, by_slot(w1_last[:, u])[:, :, first:end, :], "w1_last_dealt%d" % place)
+            for place, (copy, u, first, end) in enumerate(shares)
+        ]
+        for dealt, (copy, u, first, end) in zip(last_dealt, shares):
+            for t in range(first, end):
+                cols = slice(t * P + u * M_HALF, t * P + (u + 1) * M_HALF)
+                values = dealt[:, (t - first) * W_HALF : (t - first + 1) * W_HALF]
+                quantise(w1_q[1][0][:, cols], w1_q[1][1][:, cols], values)
 
         w2_codes, w2_scales = planes(N, "w2")
-
         w2_dealt = keep.tile([P, PACK * N], BF16, name="w2_dealt", align_bytes=64)
-
-        def prepare_w2(u):
-            place = w2_dealt[:].rearrange("p (t u m j) -> p u m t j", t=PACK, u=2, j=PACK)[:, u]
-            copier[W2_DEAL[u]](place, by_slot(w2_raw[u][:]).rearrange("p j m t -> p m t j"))
-            if u == 1:
-                quantise(w2_codes[:], w2_scales[:], w2_dealt[:])
-
-        out_codes = held([P, S], U32, "out_codes", OUT_TAG)
-        out_scales = keep.tile([P, S], U8, name="out_scales", align_bytes=64)
-        hidden, noise, signal, parts = {}, {}, {}, {}
+        out_codes, out_scales = planes(S, "out")
         result = keep.tile([P, PACK, S], F32, name="result")
+        h_scales = keep.tile([P, S], U8, name="h_scales", align_bytes=64)
+        for u, copy in enumerate((nc.scalar.copy, pool_copy)):
+            copy(w2_dealt[:].rearrange("p (t u m j) -> p u m t j", t=PACK, u=2, j=PACK)[:, u], by_slot(w2_raw[u][:]))
+        quantise(w2_codes[:], w2_scales[:], w2_dealt[:])
+        h_codes = tagged([P, S], U32, "h_codes", "temb2")
+        hidden, noise, signal, rounded = {}, {}, {}, {}
 
         def words_order(ap):
             return ap.rearrange("p (c i t) -> p c t i", i=LINE, t=PACK)
@@ -328,33 +216,15 @@ def tile_picked_yddpm_silu_po_kernel(
         def slots_order(ap):
             return ap.rearrange("p t (c i) -> p c t i", i=LINE)
 
-        extra = {
-            ACC_BANKS + b: psum.tile([P, PACK, P], F32, name="back", bufs=BACK_BANKS) for b in range(EXTRA_ACC)
-        }
+        def columns(first, last):
+            return slice(first * P, (last + 1) * P)
 
-        q_unit, place = {}, 0
-        for width in Q_UNITS:
-            for g in range(place, place + int(width)):
-                q_unit[g] = (place, place + int(width) - 1)
-            place = place + int(width)
-
-        def words_of(o, g):
-            past = g * P - (S - XW_TAIL)
-            if o == 1 and past >= 0:
-                return xw_tail[:, past : past + P]
-            return xw[o][:, g * P : (g + 1) * P]
-
-        def clock(name, ap):
-            if name in CLOCKS.split():
-                tick = keep.tile([P, 1], F32, name="tick_" + name)
-                nc.gpsimd.tensor_copy(tick[:], ap)
+        def leaves_with(g):
+            return (g - g % 2, g - g % 2 + 1) if g < PAIRED else (g, g)
 
         def first_layer(g):
-            cols = slice(g * P, (g + 1) * P)
-            if g in extra:
-                acc = extra[g]
-            else:
-                acc = psum.tile([P, PACK, P], F32, name="acc", bufs=ACC_BANKS)
+            cols = columns(g, g)
+            acc = psum.tile([P, PACK, P], F32, name="acc", bufs=ACC_BANKS)
             for o in range(PASSES):
                 codes, scales = w1_q[o]
                 for t in range(PACK):
@@ -362,163 +232,84 @@ def tile_picked_yddpm_silu_po_kernel(
                         out=acc[:, t, :],
                         lhsT=codes[:, t * P : (t + 1) * P].bitcast(FP8X4),
                         lhsT_scale=scales[:, t * P : (t + 1) * P],
-                        rhs=words_of(o, g).bitcast(FP8X4),
+                        rhs=xw[o][:, cols].bitcast(FP8X4),
                         rhs_scale=xs[o][:, cols],
                         start=(o == 0 and t == 0),
                         stop=(o == PASSES - 1 and t == PACK - 1),
                     )
             pre = keep.tile([P, PACK, P], F32, name="pre%d" % g)
             nc.vector.tensor_tensor(pre[:], temb_of[:, :, cols], acc[:], ALU.add)
-            first, last = q_unit[g]
-            if g == first:
-                hidden["unit"] = keep.tile([P, (last - first + 1) * K_PASS], BF16, name="hidden%d" % last, align_bytes=64)
-                hidden["unit", last] = hidden["unit"]
-            hidden[g] = hidden["unit"][:, (g - first) * K_PASS : (g - first + 1) * K_PASS]
+            hidden[g] = tagged([P, K_PASS], BF16, "hidden%d" % g, "hidden%d" % g)
             nc.scalar.activation(words_order(hidden[g][:]), slots_order(pre[:]), ACT.Silu)
-            clock("pre%d" % g, pre[:, 0, 0:1])
-
-        def scale_lat(g):
-            q, c0 = divmod(g * P, LAT_WIDTH)
-            tag = "hidden%d" % (g - TIE) if 0 <= g - TIE and (MULT_ON[g] == "g" or g >= TIE_V) else "signal%d" % g
-            if MULT_ON[g] != "h" and g not in signal:
-                signal[g] = held([P, PACK, P], F32, "signal%d" % g, tag)
-            if PAIR_M and MULT_ON[g - g % 2 : g - g % 2 + 2] == "vv":
-                if g % 2 == 0:
-                    both = keep.tile([P, PACK, PAIR], F32, name="both%d" % g)
-                    factor = csig_pair[g // 2][:].unsqueeze(1).to_broadcast([P, PACK, PAIR])
-                    nc.vector.tensor_tensor(both[:], lat_rows[q][:, :, c0 : c0 + PAIR], factor, ALU.mult)
-                    signal[g], signal[g + 1] = both[:, :, :P], both[:, :, P:]
-                return
-            if MULT_ON[g] == "h":
-                for engine, first, end, tag in (
-                    (nc.gpsimd, 0, POOL_SLOTS, "hidden%d" % (g - TIE)),
-                    (nc.vector, POOL_SLOTS, PACK, "own%d" % g),
-                ):
-                    part = held([P, end - first, P], F32, "part%d%d" % (g, first), tag)
-                    factor = csig_of[g][:].unsqueeze(1).to_broadcast([P, end - first, P])
-                    engine.tensor_tensor(part[:], lat_rows[q][:, first:end, c0 : c0 + P], factor, ALU.mult)
-                    parts[g, first] = (part, end)
-                return
-            if MULT_ON[g] == "t":
-                turned = psum.tile([P, PACK, P], F32, name=TURN_TAG, bufs=BANKS[TURN_TAG])
-                for t in range(PACK):
-                    nc.tensor.transpose(turned[:, t, :], lat_rows[q][:, t, c0 : c0 + P], ident[:])
-                nc.scalar.activation(signal[g][:], turned[:], ACT.Copy, scale=coef[:, g, 0:1])
-                return
-            width = POOL_SLOTS if MULT_ON[g] == "g" else PACK
-            engine = nc.gpsimd if MULT_ON[g] == "g" else nc.vector
-            factor = csig_of[g][:].unsqueeze(1).to_broadcast([P, width, P])
-            for t0 in range(0, PACK, width):
-                slots = slice(t0, t0 + width)
-                engine.tensor_tensor(signal[g][:, slots, :], lat_rows[q][:, slots, c0 : c0 + P], factor, ALU.mult)
-
-        h_q = {}
-        h_scales_all = keep.tile([P, S], U8, name="h_scales", align_bytes=64)
-
-        def quantise_hidden(g):
-            before = g - CHAIN
-            if CHAIN == 9:
-                if g == 0:
-                    h_q["all"] = held([P, S], U32, "h_codes", HOLD_TAG)
-                h_q[g] = (h_q["all"][:, g * P : (g + 1) * P], h_scales_all[:, g * P : (g + 1) * P])
-                first, last = q_unit[g]
-                if g == first:
-                    cols = slice(first * P, (last + 1) * P)
-                    quantise(h_q["all"][:, cols], h_scales_all[:, cols], hidden["unit", last][:])
-                return
-            if 0 <= before < GROUPS and MULT_ON[before] == "g":
-                tag = "csig%d" % before
-            else:
-                tag = HOLD_TAG if g == 0 else "h_codes%d" % g
-            h_q[g] = (held([P, P], U32, "h_codes%d" % g, tag)[:], h_scales_all[:, g * P : (g + 1) * P])
-            quantise(h_q[g][0], h_q[g][1], hidden[g][:])
 
         def second_layer(g):
-            h_codes, h_scales = h_q[g]
-            if g >= NOISE_ACC:
-                noise[g] = psum.tile([P, N], F32, name="acc", bufs=ACC_BANKS)
-            else:
-                noise[g] = psum.tile([P, N], F32, name="noise", bufs=NOISE_BANKS)
+            cols = columns(g, g)
+            quantise(h_codes[:, cols], h_scales[:, cols], hidden[g][:])
+            noise[g] = psum.tile([P, N], F32, name="noise", bufs=NOISE_BANKS)
             nc.tensor.matmul_mx(
                 out=noise[g][:],
-                lhsT=h_codes.bitcast(FP8X4),
-                lhsT_scale=h_scales,
+                lhsT=h_codes[:, cols].bitcast(FP8X4),
+                lhsT_scale=h_scales[:, cols],
                 rhs=w2_codes[:].bitcast(FP8X4),
                 rhs_scale=w2_scales[:],
                 start=True,
                 stop=True,
             )
 
+        def scale_lat(g):
+            h, c0 = divmod(g * P, HALF)
+            engine, width, tag = (nc.gpsimd, POOL_SLOTS, "hidden") if g in POOL_GROUPS else (nc.vector, PACK, "signal")
+            signal[g] = tagged([P, PACK, P], F32, "signal%d" % g, tag + "%d" % g)
+            factor = csig_of[:, columns(g, g)].unsqueeze(1).to_broadcast([P, width, P])
+            for t0 in range(0, PACK, width):
+                slots = slice(t0, t0 + width)
+                engine.tensor_tensor(signal[g][:, slots, :], lat_rows[h][:, slots, c0 : c0 + P], factor, ALU.mult)
+
         def combine(g):
-            cols = slice(g * P, (g + 1) * P)
             scaled = keep.tile([P, PACK, P], F32, name="scaled%d" % g)
-            flat = scaled[:].rearrange("p t m -> p (t m)")
-            if MULT_ON[g] == "t":
-                nc.vector.scalar_tensor_tensor(
-                    flat, noise[g][:], coef[:, g, 1:2], signal[g][:].rearrange("p t m -> p (t m)"), ALU.mult, ALU.subtract
-                )
-            elif SCALE_ON[g] == "v":
-                nc.vector.tensor_scalar(flat, noise[g][:], coef[:, g, 1:2], None, ALU.mult)
-            else:
-                nc.scalar.activation(flat, noise[g][:], ACT.Copy, scale=coef[:, g, 1:2])
-            if g >= BACK_ACC:
+            nc.scalar.activation(
+                scaled[:].rearrange("p t m -> p (t m)"), noise[g][:], ACT.Copy, scale=coef[:, g, 1:2]
+            )
+            if g >= GROUPS - ACC_BANKS:
                 back = psum.tile([P, PACK, P], F32, name="acc", bufs=ACC_BANKS)
             else:
                 back = psum.tile([P, PACK, P], F32, name="back", bufs=BACK_BANKS)
             for t in range(PACK):
                 nc.tensor.transpose(back[:, t, :], scaled[:, t, :], ident[:])
-            if MULT_ON[g] == "h":
-                for first in (POOL_SLOTS, 0):
-                    part, end = parts[g, first]
-                    nc.vector.tensor_tensor(result[:, first:end, cols], part[:], back[:, first:end, :], ALU.subtract)
-            elif MULT_ON[g] != "t":
-                nc.vector.tensor_tensor(result[:, :, cols], signal[g][:], back[:], ALU.subtract)
-            elif COPY_ON[g] == "s":
-                nc.scalar.activation(result[:, :, cols], back[:], ACT.Copy, scale=-1.0)
-            else:
-                nc.vector.tensor_scalar(result[:, :, cols], back[:], -1.0, None, ALU.mult)
-            if str(g) in STORE_AFTER:
-                place = STORE_AFTER.index(str(g))
-                done = slice((int(STORE_AFTER[place - 1]) + 1) * P if place else 0, cols.stop)
+            nc.vector.tensor_tensor(result[:, :, columns(g, g)], signal[g][:], back[:], ALU.subtract)
+            first, last = leaves_with(g)
+            if g == last:
+                done = columns(first, last)
                 nc.sync.dma_start(out=out_0[:, done].rearrange("(p t) s -> p t s", t=PACK), in_=result[:, :, done])
 
-        rounded = {}
-
-        unit_first, place = {}, 0
-        for width in UNITS:
-            for g in range(place, place + int(width)):
-                unit_first[g] = (place, place + int(width) - 1)
-            place = place + int(width)
-
-        def round_result(g):
-            first, last = unit_first[g]
-            if g == first:
-                rounded[last] = keep.tile([P, (last - first + 1) * P * PACK], BF16, name="rounded%d" % g, align_bytes=64)
-            if SPLIT_ROUND or g == last:
-                begin = g if SPLIT_ROUND else first
-                into = rounded[last][:, (begin - first) * P * PACK : (g - first + 1) * P * PACK]
-                copier[ROUND_ON[g]](words_order(into), slots_order(result[:, :, begin * P : (g + 1) * P]))
+        round_tags = {0: "hidden%d" % (GROUPS - 1), VECTOR_ROUNDS[0]: "first_w1"}
 
         def hand_on(g):
-            first, last = unit_first[g]
-            if g != last:
-                return
-            cols = slice(first * P, (g + 1) * P)
-            quantise(out_codes[:, cols], out_scales[:, cols], rounded[g][:])
-            if str(g) in CODES_AFTER:
-                place = CODES_AFTER.index(str(g))
-                done = slice((int(CODES_AFTER[place - 1]) + 1) * P if place else 0, cols.stop)
+            first, last = leaves_with(g)
+            if g == first:
+                name = "rounded%d" % g
+                rounded[last] = tagged([P, (last - first + 1) * K_PASS], BF16, name, round_tags.get(g, name))
+            copy = nc.vector.tensor_copy if g in VECTOR_ROUNDS else nc.scalar.copy
+            place = rounded[last][:, (g - first) * K_PASS : (g - first + 1) * K_PASS]
+            copy(words_order(place), slots_order(result[:, :, columns(g, g)]))
+            if g == last:
+                cols = columns(first, last)
+                quantise(out_codes[:, cols], out_scales[:, cols], rounded[g][:])
+            if g in CODES_FROM:
+                done = columns(CODES_FROM[g], g)
                 nc.sync.dma_start(
                     out=out_1[0].rearrange("p c r -> p (c r)").bitcast(I32)[:, done],
                     in_=out_codes[:, done].bitcast(I32),
                 )
 
-        named = {"f": first_layer, "s": second_layer, "l": scale_lat, "c": combine, "h": hand_on, "q": quantise_hidden, "r": round_result}
-        stages = [(named[word[0]], int(word[1:])) for word in STAGES.split()]
-        for s in range(2 * GROUPS + 1):
-            for u in range(2):
-                if int(W2_STEP[u]) == s:
-                    prepare_w2(u)
+        stages = (
+            (first_layer, 0),
+            (second_layer, LAG_SECOND),
+            (scale_lat, LAG_COMBINE),
+            (combine, LAG_COMBINE),
+            (hand_on, LAG_HAND_ON),
+        )
+        for s in range(GROUPS + LAG_HAND_ON):
             for stage, lag in stages:
                 if 0 <= s - lag < GROUPS:
                     stage(s - lag)

@@ -31,13 +31,25 @@ W_HALF = 256
 M_HALF = W_HALF // PACK
 SCALAR_SLOTS = 3
 VECTOR_DEALS = 2
-POOL_GROUPS = range(2, 6)
-POOL_SLOTS = 2
-VECTOR_ROUNDS = (4, 5, 7)
-PAIRED = GROUPS - 2
-LAG_SECOND, LAG_COMBINE, LAG_HAND_ON = 1, 2, GROUPS
-ACC_BANKS, NOISE_BANKS, BACK_BANKS = 3, 2, 3
+W2_SCALAR = (4, 0)
+HIDDEN_RUNS = tuple((g, g) for g in range(8))
+SIGNAL_RUNS = tuple((g, g) for g in range(8))
+OUT_RUNS = ((0, 1), (2, 3), (4, 5), (6, 6), (7, 7))
+ROUND_RUNS = ((0, 1), (2, 3), (4, 5), (6, 6), (7, 7))
+STORE_RUNS = ((0, 1), (2, 3), (4, 5), (6, 6), (7, 7))
 CODES_FROM = {3: 0, 5: 4, 7: 6}
+VECTOR_ROUNDS = (5, 7)
+POOL_ROUNDS = ()
+VECTOR_SCALES = ()
+FROM_PSUM = ()
+PRODUCTS = ((False, 0, 0, 0, 4), (False, 1, 1, 0, 4), (True, 2, 2, 0, 2), (True, 2, 2, 2, 4), (True, 3, 3, 0, 2), (True, 3, 3, 2, 4), (True, 4, 4, 0, 2), (True, 4, 4, 2, 4), (False, 5, 5, 0, 4), (False, 6, 6, 0, 4), (False, 7, 7, 0, 4))
+ACC_BANK = (0, 1, 2, 3, 0, 1, 2, 0)
+NOISE_BANK = (6, 7, 6, 7, 6, 7, 6, 7)
+BACK_BANK = (4, 5, 3, 4, 5, 3, 1, 2)
+TAKES = {"h_codes0": "temb2", "signal2": "hidden2", "signal3": "hidden3", "signal4": "hidden4", "rounded0": "hidden7", "rounded4": "first_w1"}
+PROGRAM = "D0 D1 W0 F0 F1 H0 M0 F2 H1 M1 L0 T0 C0 F3 H2 M2 L1 T1 C1 F4 H3 M3 L2 L3 T2 C2 F5 H4 M4 L4 L5 T3 C3 F6 H5 M5 L6 L7 T4 C4 F7 H6 M6 L8 T5 C5 H7 M7 L9 T6 C6 R0 L10 T7 C7 R1 O0 R2 R3 O2 R4 R5 O4 R6 O6 R7 O7"
+FIRST_ORDER = (0, 1, 2, 3)
+LATER_ORDER = (0, 1, 2, 3)
 
 
 def tile_picked_yddpm_silu_po_kernel(
@@ -53,6 +65,9 @@ def tile_picked_yddpm_silu_po_kernel(
 
         def tagged(shape, dtype, name, tag):
             return keep.tile(shape, dtype, name=name, tag=tag, align_bytes=64)
+
+        def in_bank(number):
+            return psum.tile([P, PACK, P], F32, name="bank%d" % number)
 
         step_list = keep.tile([P, S // 16], U16, name="step_list")
         offs_list = keep.tile([P, S // 16], U16, name="offs_list")
@@ -143,9 +158,10 @@ def tile_picked_yddpm_silu_po_kernel(
         coef_of = keep.tile([P, S], F32, name="coef_of")
         coef = keep.tile([P, GROUPS, 2], F32, name="coef")
         csig_of = keep.tile([P, S], F32, name="csig_of")
+        csig_banks = []
         for h in range(halves):
             nc.vector.tensor_copy(coef_of[:, h * HALF : (h + 1) * HALF], coef_rows[:].indirect(half_of_step(h)))
-            bank = psum.tile([P, per_half, P], F32, name="back", bufs=BACK_BANKS)
+            bank = in_bank(4 + h)
             for b in range(per_half):
                 g = h * per_half + b
                 nc.tensor.transpose(bank[:, b, :], coef_of[:, g * P : (g + 1) * P], ident[:])
@@ -153,7 +169,8 @@ def tile_picked_yddpm_silu_po_kernel(
         gather_temb(2)
         gather_temb(3)
         for h in range(halves):
-            bank = psum.tile([P, per_half, P], F32, name="noise", bufs=NOISE_BANKS)
+            bank = in_bank(6 + h)
+            csig_banks.append(bank)
             for b in range(per_half):
                 nc.tensor.transpose(bank[:, b, :], coef[:, h * per_half + b, 0:1].to_broadcast([P, P]), ident[:])
             nc.scalar.copy(csig_of[:, h * HALF : (h + 1) * HALF], bank[:].rearrange("p b j -> p (b j)"))
@@ -203,12 +220,7 @@ def tile_picked_yddpm_silu_po_kernel(
         w2_dealt = keep.tile([P, PACK * N], BF16, name="w2_dealt", align_bytes=64)
         out_codes, out_scales = planes(S, "out")
         result = keep.tile([P, PACK, S], F32, name="result")
-        h_scales = keep.tile([P, S], U8, name="h_scales", align_bytes=64)
-        for u, copy in enumerate((nc.scalar.copy, pool_copy)):
-            copy(w2_dealt[:].rearrange("p (t u m j) -> p u m t j", t=PACK, u=2, j=PACK)[:, u], by_slot(w2_raw[u][:]))
-        quantise(w2_codes[:], w2_scales[:], w2_dealt[:])
-        h_codes = tagged([P, S], U32, "h_codes", "temb2")
-        hidden, noise, signal, rounded = {}, {}, {}, {}
+        hidden, h_codes, h_scales, back, signal, rounded, noises = {}, {}, {}, {}, {}, {}, {}
 
         def words_order(ap):
             return ap.rearrange("p (c i t) -> p c t i", i=LINE, t=PACK)
@@ -219,100 +231,130 @@ def tile_picked_yddpm_silu_po_kernel(
         def columns(first, last):
             return slice(first * P, (last + 1) * P)
 
-        def leaves_with(g):
-            return (g - g % 2, g - g % 2 + 1) if g < PAIRED else (g, g)
+        def deal_w2(u):
+            view = w2_dealt[:].rearrange("p (t u m j) -> p u m t j", t=PACK, u=2, j=PACK)[:, u]
+            split = W2_SCALAR[u]
+            if split:
+                nc.scalar.copy(view[:, :, :split, :], by_slot(w2_raw[u][:])[:, :, :split, :])
+            if split < PACK:
+                pool_copy(view[:, :, split:, :], by_slot(w2_raw[u][:])[:, :, split:, :])
+
+        def run_of(g, runs):
+            return [run for run in runs if run[0] <= g <= run[1]][0]
 
         def first_layer(g):
             cols = columns(g, g)
-            acc = psum.tile([P, PACK, P], F32, name="acc", bufs=ACC_BANKS)
+            acc = in_bank(ACC_BANK[g])
+            order = FIRST_ORDER if g == 0 else LATER_ORDER
             for o in range(PASSES):
                 codes, scales = w1_q[o]
-                for t in range(PACK):
+                for place, t in enumerate(order):
                     nc.tensor.matmul_mx(
                         out=acc[:, t, :],
                         lhsT=codes[:, t * P : (t + 1) * P].bitcast(FP8X4),
                         lhsT_scale=scales[:, t * P : (t + 1) * P],
                         rhs=xw[o][:, cols].bitcast(FP8X4),
                         rhs_scale=xs[o][:, cols],
-                        start=(o == 0 and t == 0),
-                        stop=(o == PASSES - 1 and t == PACK - 1),
+                        start=(o == 0 and place == 0),
+                        stop=(o == PASSES - 1 and place == PACK - 1),
                     )
             pre = keep.tile([P, PACK, P], F32, name="pre%d" % g)
             nc.vector.tensor_tensor(pre[:], temb_of[:, :, cols], acc[:], ALU.add)
-            hidden[g] = tagged([P, K_PASS], BF16, "hidden%d" % g, "hidden%d" % g)
-            nc.scalar.activation(words_order(hidden[g][:]), slots_order(pre[:]), ACT.Silu)
+            first, last = run_of(g, HIDDEN_RUNS)
+            if g == first:
+                hidden[first] = tagged([P, (last - first + 1) * K_PASS], BF16, "hidden%d" % g, "hidden%d" % g)
+            place = hidden[first][:, (g - first) * K_PASS : (g - first + 1) * K_PASS]
+            nc.scalar.activation(words_order(place), slots_order(pre[:]), ACT.Silu)
+
+        def quantise_hidden(first):
+            last = run_of(first, HIDDEN_RUNS)[1]
+            width = (last - first + 1) * P
+            name = "h_codes%d" % first
+            h_codes[first] = tagged([P, width], U32, name, TAKES.get(name, name))
+            h_scales[first] = keep.tile([P, width], U8, name="h_scales%d" % first, align_bytes=64)
+            quantise(h_codes[first][:], h_scales[first][:], hidden[first][:])
 
         def second_layer(g):
-            cols = columns(g, g)
-            quantise(h_codes[:, cols], h_scales[:, cols], hidden[g][:])
-            noise[g] = psum.tile([P, N], F32, name="noise", bufs=NOISE_BANKS)
+            first = run_of(g, HIDDEN_RUNS)[0]
+            cols = columns(g - first, g - first)
+            noises[g] = in_bank(NOISE_BANK[g])
             nc.tensor.matmul_mx(
-                out=noise[g][:],
-                lhsT=h_codes[:, cols].bitcast(FP8X4),
-                lhsT_scale=h_scales[:, cols],
+                out=noises[g][:].rearrange("p t m -> p (t m)"),
+                lhsT=h_codes[first][:, cols].bitcast(FP8X4),
+                lhsT_scale=h_scales[first][:, cols],
                 rhs=w2_codes[:].bitcast(FP8X4),
                 rhs_scale=w2_scales[:],
                 start=True,
                 stop=True,
             )
 
-        def scale_lat(g):
-            h, c0 = divmod(g * P, HALF)
-            engine, width, tag = (nc.gpsimd, POOL_SLOTS, "hidden") if g in POOL_GROUPS else (nc.vector, PACK, "signal")
-            signal[g] = tagged([P, PACK, P], F32, "signal%d" % g, tag + "%d" % g)
-            factor = csig_of[:, columns(g, g)].unsqueeze(1).to_broadcast([P, width, P])
-            for t0 in range(0, PACK, width):
-                slots = slice(t0, t0 + width)
-                engine.tensor_tensor(signal[g][:, slots, :], lat_rows[h][:, slots, c0 : c0 + P], factor, ALU.mult)
+        def turn_back(g):
+            noise = noises[g]
+            scaled = keep.tile([P, PACK, P], F32, name="scaled%d" % g)
+            if g in VECTOR_SCALES:
+                nc.vector.tensor_scalar_mul(scaled[:], noise[:], coef[:, g, 1:2])
+            else:
+                nc.scalar.activation(scaled[:], noise[:], ACT.Copy, scale=coef[:, g, 1:2])
+            back[g] = in_bank(BACK_BANK[g])
+            for t in range(PACK):
+                nc.tensor.transpose(back[g][:, t, :], scaled[:, t, :], ident[:])
+
+        def scale_lat(number):
+            on_pool, first, last, t0, t1 = PRODUCTS[number]
+            h, c0 = divmod(first * P, HALF)
+            width = (last - first + 1) * P
+            start, end = run_of(first, SIGNAL_RUNS)
+            if start not in signal:
+                name = "signal%d" % start
+                signal[start] = tagged([P, PACK, (end - start + 1) * P], F32, name, TAKES.get(name, name))
+            if first not in FROM_PSUM:
+                row = csig_of[:, columns(first, last)]
+            else:
+                row = csig_banks[h][:].rearrange("p b j -> p (b j)")[:, c0 : c0 + width]
+            factor = row.unsqueeze(1).to_broadcast([P, t1 - t0, width])
+            engine = nc.gpsimd if on_pool else nc.vector
+            engine.tensor_tensor(signal[start][:, t0:t1, columns(first - start, last - start)], lat_rows[h][:, t0:t1, c0 : c0 + width], factor, ALU.mult)
 
         def combine(g):
-            scaled = keep.tile([P, PACK, P], F32, name="scaled%d" % g)
-            nc.scalar.activation(
-                scaled[:].rearrange("p t m -> p (t m)"), noise[g][:], ACT.Copy, scale=coef[:, g, 1:2]
-            )
-            if g >= GROUPS - ACC_BANKS:
-                back = psum.tile([P, PACK, P], F32, name="acc", bufs=ACC_BANKS)
-            else:
-                back = psum.tile([P, PACK, P], F32, name="back", bufs=BACK_BANKS)
-            for t in range(PACK):
-                nc.tensor.transpose(back[:, t, :], scaled[:, t, :], ident[:])
-            nc.vector.tensor_tensor(result[:, :, columns(g, g)], signal[g][:], back[:], ALU.subtract)
-            first, last = leaves_with(g)
+            start = run_of(g, SIGNAL_RUNS)[0]
+            own = signal[start][:, :, columns(g - start, g - start)]
+            nc.vector.tensor_tensor(result[:, :, columns(g, g)], own, back[g][:], ALU.subtract)
+            first, last = run_of(g, STORE_RUNS)
             if g == last:
                 done = columns(first, last)
                 nc.sync.dma_start(out=out_0[:, done].rearrange("(p t) s -> p t s", t=PACK), in_=result[:, :, done])
 
-        round_tags = {0: "hidden%d" % (GROUPS - 1), VECTOR_ROUNDS[0]: "first_w1"}
-
-        def hand_on(g):
-            first, last = leaves_with(g)
+        def round_result(g):
+            first, last = run_of(g, ROUND_RUNS)
             if g == first:
                 name = "rounded%d" % g
-                rounded[last] = tagged([P, (last - first + 1) * K_PASS], BF16, name, round_tags.get(g, name))
-            copy = nc.vector.tensor_copy if g in VECTOR_ROUNDS else nc.scalar.copy
-            place = rounded[last][:, (g - first) * K_PASS : (g - first + 1) * K_PASS]
+                rounded[first] = tagged([P, (last - first + 1) * K_PASS], BF16, name, TAKES.get(name, name))
+            copy = nc.vector.tensor_copy if g in VECTOR_ROUNDS else pool_copy if g in POOL_ROUNDS else nc.scalar.copy
+            place = rounded[first][:, (g - first) * K_PASS : (g - first + 1) * K_PASS]
             copy(words_order(place), slots_order(result[:, :, columns(g, g)]))
-            if g == last:
-                cols = columns(first, last)
-                quantise(out_codes[:, cols], out_scales[:, cols], rounded[g][:])
-            if g in CODES_FROM:
-                done = columns(CODES_FROM[g], g)
+
+        def hand_on(first):
+            last = run_of(first, OUT_RUNS)[1]
+            cols = columns(first, last)
+            start = run_of(first, ROUND_RUNS)[0]
+            values = rounded[start][:, (first - start) * K_PASS : (last + 1 - start) * K_PASS]
+            quantise(out_codes[:, cols], out_scales[:, cols], values)
+            if last in CODES_FROM:
+                done = columns(CODES_FROM[last], last)
                 nc.sync.dma_start(
                     out=out_1[0].rearrange("p c r -> p (c r)").bitcast(I32)[:, done],
                     in_=out_codes[:, done].bitcast(I32),
                 )
 
-        stages = (
-            (first_layer, 0),
-            (second_layer, LAG_SECOND),
-            (scale_lat, LAG_COMBINE),
-            (combine, LAG_COMBINE),
-            (hand_on, LAG_HAND_ON),
-        )
-        for s in range(GROUPS + LAG_HAND_ON):
-            for stage, lag in stages:
-                if 0 <= s - lag < GROUPS:
-                    stage(s - lag)
+        def quantise_w2(unused):
+            quantise(w2_codes[:], w2_scales[:], w2_dealt[:])
+
+        stage = {
+            "F": first_layer, "D": deal_w2, "W": quantise_w2, "H": quantise_hidden, "M": second_layer, "T": turn_back,
+            "L": scale_lat, "C": combine, "R": round_result, "O": hand_on,
+        }
+        for word in PROGRAM.split():
+            stage[word[0]](int(word[1:]))
         for r in range(4):
             nc.sync.dma_start(
                 out=out_2[0, r:SCALE_ROWS:4, :].bitcast(I32), in_=out_scales[r:P:QUADRANT, :].bitcast(I32)

@@ -23,6 +23,7 @@ PASSES = K // K_PASS
 QUADRANT = 32
 SCALE_ROWS = K_PASS // 32
 GROUPS = S // P
+ROW_STEP = P // (PASSES * SCALE_ROWS)
 HALF = S // 2
 LINE = 4
 WINDOW = HALF + 16
@@ -86,13 +87,13 @@ def tile_picked_yddpm_silu_po_kernel(
         xs = [xs_both[:, o * S : (o + 1) * S] for o in range(PASSES)]
 
         last_quadrant = P - QUADRANT
-        nc.gpsimd.memset(xs_all[:last_quadrant, :].bitcast(I32), 0)
+        nc.gpsimd.memset(xs_all[:, : T // 2].bitcast(I32), 0)
+        nc.vector.memset(xs_all[:, T // 2 :].bitcast(I32), 0)
+        nc.vector.memset(coef_rows[:], 0.0)
         make_identity(nc, ident[:])
         warm = keep.tile([P, 2], F32, name="warm")
         nc.vector.memset(warm[:, 0:1], 0.0)
         nc.scalar.activation(warm[:, 1:2], warm[:, 0:1], ACT.Silu)
-        nc.vector.memset(coef_rows[:last_quadrant, :R], 0.0)
-        nc.vector.memset(coef_rows[:, R:], 0.0)
         for t in range(1, PACK):
             nc.vector.memset(temb_rows[t][:, R:], 0.0)
         nc.vector.memset(xs_both[:].bitcast(I32), 0)
@@ -106,13 +107,13 @@ def tile_picked_yddpm_silu_po_kernel(
             nc.sync.dma_start(out=slots, in_=rows.rearrange("(p t) c -> p t c", t=PACK))
 
         nc.sync.dma_start(offs_list[:], offs)
-        nc.sync.dma_start(
-            out=xs_all[last_quadrant:, :].bitcast(I32), in_=x_scales.rearrange("o q c -> (o q) c").bitcast(I32)
-        )
         nc.sync.dma_start(step_list[:], step)
         nc.sync.dma_start(out=temb_rows[0][:], in_=temb.rearrange("(p t) r -> p (t r)", t=PACK))
-        nc.sync.dma_start(out=coef_rows[last_quadrant : P - COEF_ROWS, :R], in_=csig[:COEF_ROWS, :])
-        nc.sync.dma_start(out=coef_rows[P - COEF_ROWS :, :R], in_=cnoise[:COEF_ROWS, :])
+        nc.sync.dma_start(
+            out=xs_all[0:P:ROW_STEP, :].bitcast(I32), in_=x_scales.rearrange("o q c -> (o q) c").bitcast(I32)
+        )
+        nc.sync.dma_start(out=coef_rows[last_quadrant : last_quadrant + 1, :R], in_=csig[:1, :])
+        nc.sync.dma_start(out=coef_rows[P - COEF_ROWS : P - COEF_ROWS + 1, :R], in_=cnoise[:1, :])
         load_words(0)
         load_slots(w1_first[:], w1[:K_PASS, :])
 
@@ -124,10 +125,10 @@ def tile_picked_yddpm_silu_po_kernel(
 
         def move_scales(o):
             for r in range(4):
-                first = last_quadrant + SCALE_ROWS * o + r
+                first = ROW_STEP * (SCALE_ROWS * o + r)
                 nc.sync.dma_start(
                     out=xs[o][r:P:QUADRANT, :].bitcast(I32),
-                    in_=picked[first : first + SCALE_ROWS - r : 4, :].bitcast(I32),
+                    in_=picked[first : ROW_STEP * SCALE_ROWS * (o + 1) : 4 * ROW_STEP, :].bitcast(I32),
                 )
 
         move_scales(1)

@@ -23,6 +23,7 @@ PASSES = K // K_PASS
 QUADRANT = 32
 SCALE_ROWS = K_PASS // 32
 GROUPS = S // P
+EARLY = 768
 ROW_STEP = P // (PASSES * SCALE_ROWS)
 HALF = S // 2
 LINE = 4
@@ -30,6 +31,7 @@ WINDOW = HALF + 16
 COEF_ROWS = QUADRANT // 2
 W_HALF = 256
 M_HALF = W_HALF // PACK
+SCALAR_HALVES = 7
 SCALAR_SLOTS = 3
 VECTOR_DEALS = 2
 W2_SCALAR = (4, 0)
@@ -149,7 +151,7 @@ def tile_picked_yddpm_silu_po_kernel(
         def gather_temb(t):
             for h in range(halves):
                 looked_up = temb_rows[t][:].indirect(half_of_step(h))
-                if t < SCALAR_SLOTS:
+                if t * halves + h < SCALAR_HALVES:
                     nc.scalar.activation(temb_of[:, t, h * HALF : (h + 1) * HALF], looked_up, ACT.Copy)
                 else:
                     nc.vector.tensor_copy(temb_of[:, t, h * HALF : (h + 1) * HALF], looked_up)
@@ -183,7 +185,7 @@ def tile_picked_yddpm_silu_po_kernel(
             return raw.rearrange("p j (m t) -> p m t j", t=PACK)
 
         def deal(copy, values, name):
-            dealt = keep.tile([P, values.shape[1] * values.shape[2] * PACK], BF16, name=name, align_bytes=64)
+            dealt = tagged([P, values.shape[1] * values.shape[2] * PACK], BF16, name, name)
             copy(dealt[:].rearrange("p (t m j) -> p m t j", t=values.shape[2], j=PACK), values)
             return dealt
 
@@ -195,12 +197,12 @@ def tile_picked_yddpm_silu_po_kernel(
         def quantise(codes, scales, values):
             nc.vector.quantize_mx(out=codes.bitcast(FP8X4), scales=scales, in_=values)
 
-        xw = [keep.tile([P, S], U32, name="xw%d" % o, align_bytes=64) for o in range(PASSES)]
+        xw = [keep.tile([P, width], U32, name="xw%d" % o, align_bytes=64) for o, width in enumerate((S, EARLY))]
         w1_q = [planes(H, "w1_%d" % o) for o in range(PASSES)]
         nc.vector.tensor_copy(xw[0][:], xw_all[0][:].indirect(offs_list[:]))
         first_dealt = deal(pool_copy, by_slot(w1_first[:]), "w1_first_dealt")
         quantise(w1_q[0][0][:], w1_q[0][1][:], first_dealt[:])
-        nc.vector.tensor_copy(xw[1][:], xw_all[1][:].indirect(offs_list[:]))
+        nc.vector.tensor_copy(xw[1][:, :EARLY], xw_all[1][:].indirect(offs_list[:, : EARLY // 16]))
 
         shares = (
             (nc.scalar.copy, 0, 0, PACK),
@@ -216,6 +218,14 @@ def tile_picked_yddpm_silu_po_kernel(
                 cols = slice(t * P + u * M_HALF, t * P + (u + 1) * M_HALF)
                 values = dealt[:, (t - first) * W_HALF : (t - first + 1) * W_HALF]
                 quantise(w1_q[1][0][:, cols], w1_q[1][1][:, cols], values)
+
+        xw_late = tagged([P, S - EARLY], U32, "xw_late", "w1_last_dealt2")
+        nc.vector.tensor_copy(xw_late[:], xw_all[1][:].indirect(offs_list[:, EARLY // 16 :]))
+
+        def words_of(o, g):
+            if o == PASSES - 1 and g * P >= EARLY:
+                return xw_late[:, g * P - EARLY : (g + 1) * P - EARLY]
+            return xw[o][:, g * P : (g + 1) * P]
 
         w2_codes, w2_scales = planes(N, "w2")
         w2_dealt = keep.tile([P, PACK * N], BF16, name="w2_dealt", align_bytes=64)
@@ -254,7 +264,7 @@ def tile_picked_yddpm_silu_po_kernel(
                         out=acc[:, t, :],
                         lhsT=codes[:, t * P : (t + 1) * P].bitcast(FP8X4),
                         lhsT_scale=scales[:, t * P : (t + 1) * P],
-                        rhs=xw[o][:, cols].bitcast(FP8X4),
+                        rhs=words_of(o, g).bitcast(FP8X4),
                         rhs_scale=xs[o][:, cols],
                         start=(o == 0 and place == 0),
                         stop=(o == PASSES - 1 and place == PACK - 1),

@@ -45,14 +45,16 @@ VECTOR_ROUNDS = (5, 7)
 POOL_ROUNDS = ()
 VECTOR_SCALES = ()
 FROM_PSUM = ()
-PRODUCTS = ((False, 0, 0, 0, 4), (False, 1, 1, 0, 4), (True, 2, 2, 0, 2), (True, 2, 2, 2, 4), (True, 3, 3, 0, 2), (True, 3, 3, 2, 4), (True, 4, 4, 0, 2), (True, 4, 4, 2, 4), (False, 5, 5, 0, 4), (False, 6, 6, 0, 4), (False, 7, 7, 0, 4))
+PRODUCTS = ((False, 0, 0, 0, 4), (True, 1, 1, 0, 2), (True, 1, 1, 2, 4), (False, 2, 2, 0, 4), (True, 3, 3, 0, 2), (True, 3, 3, 2, 4), (False, 4, 4, 0, 4), (True, 5, 5, 0, 2), (True, 5, 5, 2, 4), (False, 6, 6, 0, 4), (False, 7, 7, 0, 4))
 ACC_BANK = (0, 1, 2, 3, 0, 1, 2, 0)
 NOISE_BANK = (6, 7, 6, 7, 6, 7, 6, 7)
 BACK_BANK = (4, 5, 3, 4, 5, 3, 1, 2)
-TAKES = {"h_codes0": "temb2", "signal2": "hidden2", "signal3": "hidden3", "signal4": "hidden4", "rounded0": "hidden7", "rounded4": "first_w1"}
-PROGRAM = "D0 D1 W0 F0 F1 H0 M0 F2 H1 M1 L0 T0 C0 F3 H2 M2 L1 T1 C1 F4 H3 M3 L2 L3 T2 C2 F5 H4 M4 L4 L5 T3 C3 F6 H5 M5 L6 L7 T4 C4 F7 H6 M6 L8 T5 C5 H7 M7 L9 T6 C6 R0 L10 T7 C7 R1 O0 R2 R3 O2 R4 R5 O4 R6 O6 R7 O7"
+TAKES = {"h_codes0": "temb2", "rounded0": "hidden7", "rounded4": "first_w1"}
+PROGRAM = "D0 D1 W0 F0 F1 H0 M0 F2 H1 M1 F3 H2 M2 L0 T0 C0 F4 H3 M3 L1 L2 T1 C1 F5 H4 M4 L3 T2 C2 F6 H5 M5 L4 L5 T3 C3 F7 H6 M6 L6 T4 C4 H7 M7 L7 L8 T5 C5 R0 L9 T6 C6 R1 O0 L10 T7 C7 R2 R3 O2 R4 R5 O4 R6 O6 R7 O7"
 FIRST_ORDER = (0, 1, 2, 3)
 LATER_ORDER = (0, 1, 2, 3)
+SHARED = (1, 3, 5,)
+SIGNAL_IN = {1: 1, 3: 3, 5: 5}
 
 
 def tile_picked_yddpm_silu_po_kernel(
@@ -231,6 +233,7 @@ def tile_picked_yddpm_silu_po_kernel(
         w2_dealt = keep.tile([P, PACK * N], BF16, name="w2_dealt", align_bytes=64)
         out_codes, out_scales = planes(S, "out")
         result = keep.tile([P, PACK, S], F32, name="result")
+        shared = {}
         hidden, h_codes, h_scales, back, signal, rounded, noises = {}, {}, {}, {}, {}, {}, {}
 
         def words_order(ap):
@@ -269,12 +272,17 @@ def tile_picked_yddpm_silu_po_kernel(
                         start=(o == 0 and place == 0),
                         stop=(o == PASSES - 1 and place == PACK - 1),
                     )
-            pre = keep.tile([P, PACK, P], F32, name="pre%d" % g)
+            pre = tagged([P, PACK, P], F32, "pre%d" % g, "pre%d" % g)
             nc.vector.tensor_tensor(pre[:], temb_of[:, :, cols], acc[:], ALU.add)
             first, last = run_of(g, HIDDEN_RUNS)
-            if g == first:
-                hidden[first] = tagged([P, (last - first + 1) * K_PASS], BF16, "hidden%d" % g, "hidden%d" % g)
-            place = hidden[first][:, (g - first) * K_PASS : (g - first + 1) * K_PASS]
+            if g in SHARED:
+                shared[g] = keep.tile([P, K_PASS], F32, name="shared%d" % g, align_bytes=64)
+                hidden[g] = shared[g][:, : K_PASS // 2].bitcast(BF16)
+            elif g - 1 in SHARED:
+                hidden[g] = shared[g - 1][:, K_PASS // 2 :].bitcast(BF16)
+            else:
+                hidden[g] = tagged([P, K_PASS], BF16, "hidden%d" % g, "hidden%d" % g)[:]
+            place = hidden[g]
             nc.scalar.activation(words_order(place), slots_order(pre[:]), ACT.Silu)
 
         def quantise_hidden(first):
@@ -283,7 +291,7 @@ def tile_picked_yddpm_silu_po_kernel(
             name = "h_codes%d" % first
             h_codes[first] = tagged([P, width], U32, name, TAKES.get(name, name))
             h_scales[first] = keep.tile([P, width], U8, name="h_scales%d" % first, align_bytes=64)
-            quantise(h_codes[first][:], h_scales[first][:], hidden[first][:])
+            quantise(h_codes[first][:], h_scales[first][:], hidden[first])
 
         def second_layer(g):
             first = run_of(g, HIDDEN_RUNS)[0]
@@ -315,9 +323,11 @@ def tile_picked_yddpm_silu_po_kernel(
             h, c0 = divmod(first * P, HALF)
             width = (last - first + 1) * P
             start, end = run_of(first, SIGNAL_RUNS)
-            if start not in signal:
+            if start in SIGNAL_IN:
+                signal[start] = shared[SIGNAL_IN[start]][:].rearrange("p (t c) -> p t c", t=PACK)
+            elif start not in signal:
                 name = "signal%d" % start
-                signal[start] = tagged([P, PACK, (end - start + 1) * P], F32, name, TAKES.get(name, name))
+                signal[start] = tagged([P, PACK, (end - start + 1) * P], F32, name, TAKES.get(name, name))[:]
             if first not in FROM_PSUM:
                 row = csig_of[:, columns(first, last)]
             else:

@@ -45,12 +45,12 @@ VECTOR_ROUNDS = (5, 7)
 POOL_ROUNDS = ()
 VECTOR_SCALES = ()
 FROM_PSUM = ()
-PRODUCTS = ((False, 0, 0, 0, 4), (True, 1, 1, 0, 2), (True, 1, 1, 2, 4), (False, 2, 2, 0, 4), (True, 3, 3, 0, 2), (True, 3, 3, 2, 4), (False, 4, 4, 0, 4), (True, 5, 5, 0, 2), (True, 5, 5, 2, 4), (False, 6, 6, 0, 4), (False, 7, 7, 0, 4))
+PRODUCTS = ((False, 0, 0, 0, 4), (True, 1, 1, 0, 2), (True, 1, 1, 2, 4), (False, 2, 2, 0, 4), (True, 3, 3, 0, 2), (True, 3, 3, 2, 4), (False, 4, 4, 0, 4), (True, 5, 5, 0, 2), (True, 5, 5, 2, 4), (False, 6, 6, 0, 4), (True, 7, 7, 0, 2), (True, 7, 7, 2, 4))
 ACC_BANK = (0, 1, 2, 3, 0, 1, 2, 0)
 NOISE_BANK = (6, 7, 6, 7, 6, 7, 6, 7)
 BACK_BANK = (4, 5, 3, 4, 5, 3, 1, 2)
-TAKES = {"h_codes0": "temb2", "rounded0": "hidden7", "rounded4": "first_w1"}
-PROGRAM = "D0 D1 W0 F0 F1 H0 M0 F2 H1 M1 F3 H2 M2 L0 T0 C0 F4 H3 M3 L1 L2 T1 C1 F5 H4 M4 L3 T2 C2 F6 H5 M5 L4 L5 T3 C3 F7 H6 M6 L6 T4 C4 H7 M7 L7 L8 T5 C5 R0 L9 T6 C6 R1 O0 L10 T7 C7 R2 R3 O2 R4 R5 O4 R6 O6 R7 O7"
+TAKES = {"h_codes0": "temb2", "rounded0": "pre7", "rounded4": "first_w1", "signal7": "hidden7"}
+PROGRAM = "D0 D1 W0 F0 F1 H0 M0 F2 H1 M1 F3 H2 M2 L0 T0 C0 F4 H3 M3 L1 L2 T1 C1 F5 H4 M4 L3 T2 C2 F6 H5 M5 L4 L5 T3 C3 F7 H6 M6 L6 T4 C4 H7 M7 L7 L8 T5 C5 R0 L9 T6 C6 R1 O0 L10 L11 T7 C7 R2 R3 O2 R4 R5 O4 R6 O6 R7 O7"
 FIRST_ORDER = (0, 1, 2, 3)
 LATER_ORDER = (0, 1, 2, 3)
 SHARED = (1, 3, 5,)

@@ -23,38 +23,26 @@ PASSES = K // K_PASS
 QUADRANT = 32
 SCALE_ROWS = K_PASS // 32
 GROUPS = S // P
-EARLY = 768
-ROW_STEP = P // (PASSES * SCALE_ROWS)
 HALF = S // 2
 LINE = 4
 WINDOW = HALF + 16
-COEF_ROWS = QUADRANT // 2
+ROW_STEP = P // (PASSES * SCALE_ROWS)
+CSIG_ROW, CNOISE_ROW = 96, 112
 W_HALF = 256
 M_HALF = W_HALF // PACK
-SCALAR_HALVES = 7
-SCALAR_SLOTS = 3
+SCALAR_GATHERS = 7
 VECTOR_DEALS = 2
-W2_SCALAR = (4, 0)
-HIDDEN_RUNS = tuple((g, g) for g in range(8))
-SIGNAL_RUNS = tuple((g, g) for g in range(8))
-OUT_RUNS = ((0, 1), (2, 3), (4, 5), (6, 6), (7, 7))
-ROUND_RUNS = ((0, 1), (2, 3), (4, 5), (6, 6), (7, 7))
-STORE_RUNS = ((0, 1), (2, 3), (4, 5), (6, 6), (7, 7))
-CODES_FROM = {3: 0, 5: 4, 7: 6}
+EARLY = 6 * P
+POOL_SLOTS = 2
 VECTOR_ROUNDS = (5, 7)
-POOL_ROUNDS = ()
-VECTOR_SCALES = ()
-FROM_PSUM = ()
-PRODUCTS = ((False, 0, 0, 0, 4), (True, 1, 1, 0, 2), (True, 1, 1, 2, 4), (False, 2, 2, 0, 4), (True, 3, 3, 0, 2), (True, 3, 3, 2, 4), (False, 4, 4, 0, 4), (True, 5, 5, 0, 2), (True, 5, 5, 2, 4), (False, 6, 6, 0, 4), (True, 7, 7, 0, 2), (True, 7, 7, 2, 4))
+PAIRED = GROUPS - 2
+LAG_SECOND, LAG_COMBINE, LAG_HAND_ON = 1, 3, GROUPS
 ACC_BANK = (0, 1, 2, 3, 0, 1, 2, 0)
-NOISE_BANK = (6, 7, 6, 7, 6, 7, 6, 7)
-BACK_BANK = (4, 5, 3, 4, 5, 3, 1, 2)
-TAKES = {"h_codes0": "temb2", "rounded0": "pre7", "rounded4": "first_w1", "signal7": "hidden7"}
-PROGRAM = "D0 D1 W0 F0 F1 H0 M0 F2 H1 M1 F3 H2 M2 L0 T0 C0 F4 H3 M3 L1 L2 T1 C1 F5 H4 M4 L3 T2 C2 F6 H5 M5 L4 L5 T3 C3 F7 H6 M6 L6 T4 C4 H7 M7 L7 L8 T5 C5 R0 L9 T6 C6 R1 O0 L10 L11 T7 C7 R2 R3 O2 R4 R5 O4 R6 O6 R7 O7"
-FIRST_ORDER = (0, 1, 2, 3)
-LATER_ORDER = (0, 1, 2, 3)
-SHARED = (1, 3, 5,)
-SIGNAL_IN = {1: 1, 3: 3, 5: 5}
+NOISE_BANK = (5, 6)
+BACK_BANK = (4, 3, 4, 3, 1, 2, 4, 0)
+COEF_BANK = (4, 5)
+ODD_BANK, EVEN_BANK = 6, 7
+CODES_FROM = {3: 0, 5: 4, 7: 6}
 
 
 def tile_picked_yddpm_silu_po_kernel(
@@ -90,7 +78,6 @@ def tile_picked_yddpm_silu_po_kernel(
         xs_both = keep.tile([P, PASSES * S], U8, name="xs_both", align_bytes=64)
         xs = [xs_both[:, o * S : (o + 1) * S] for o in range(PASSES)]
 
-        last_quadrant = P - QUADRANT
         nc.gpsimd.memset(xs_all[:, : T // 2].bitcast(I32), 0)
         nc.vector.memset(xs_all[:, T // 2 :].bitcast(I32), 0)
         nc.vector.memset(coef_rows[:], 0.0)
@@ -116,12 +103,12 @@ def tile_picked_yddpm_silu_po_kernel(
         nc.sync.dma_start(
             out=xs_all[0:P:ROW_STEP, :].bitcast(I32), in_=x_scales.rearrange("o q c -> (o q) c").bitcast(I32)
         )
-        nc.sync.dma_start(out=coef_rows[last_quadrant : last_quadrant + 1, :R], in_=csig[:1, :])
-        nc.sync.dma_start(out=coef_rows[P - COEF_ROWS : P - COEF_ROWS + 1, :R], in_=cnoise[:1, :])
+        nc.sync.dma_start(out=coef_rows[CSIG_ROW : CSIG_ROW + 1, :R], in_=csig[:1, :])
+        nc.sync.dma_start(out=coef_rows[CNOISE_ROW : CNOISE_ROW + 1, :R], in_=cnoise[:1, :])
         load_words(0)
         load_slots(w1_first[:], w1[:K_PASS, :])
 
-        for t in list(range(SCALAR_SLOTS, PACK)) + list(range(1, SCALAR_SLOTS)):
+        for t in [PACK - 1] + list(range(1, PACK - 1)):
             nc.gpsimd.tensor_copy(temb_rows[t][:, :R], temb_rows[0][:, t * R : (t + 1) * R])
 
         picked = keep.tile([P, S], U8, name="picked", align_bytes=64)
@@ -153,7 +140,7 @@ def tile_picked_yddpm_silu_po_kernel(
         def gather_temb(t):
             for h in range(halves):
                 looked_up = temb_rows[t][:].indirect(half_of_step(h))
-                if t * halves + h < SCALAR_HALVES:
+                if t * halves + h < SCALAR_GATHERS:
                     nc.scalar.activation(temb_of[:, t, h * HALF : (h + 1) * HALF], looked_up, ACT.Copy)
                 else:
                     nc.vector.tensor_copy(temb_of[:, t, h * HALF : (h + 1) * HALF], looked_up)
@@ -162,23 +149,26 @@ def tile_picked_yddpm_silu_po_kernel(
         gather_temb(1)
         coef_of = keep.tile([P, S], F32, name="coef_of")
         coef = keep.tile([P, GROUPS, 2], F32, name="coef")
-        csig_of = keep.tile([P, S], F32, name="csig_of")
-        csig_banks = []
+        csig_odd = keep.tile([P, GROUPS // 2, P], F32, name="csig_odd")
         for h in range(halves):
             nc.vector.tensor_copy(coef_of[:, h * HALF : (h + 1) * HALF], coef_rows[:].indirect(half_of_step(h)))
-            bank = in_bank(4 + h)
+            bank = in_bank(COEF_BANK[h])
             for b in range(per_half):
                 g = h * per_half + b
                 nc.tensor.transpose(bank[:, b, :], coef_of[:, g * P : (g + 1) * P], ident[:])
-            nc.scalar.copy(coef[:, h * per_half : (h + 1) * per_half, :], bank[:, :, last_quadrant:P:COEF_ROWS])
+            both = bank[:, :, CSIG_ROW : P : CNOISE_ROW - CSIG_ROW]
+            nc.scalar.copy(coef[:, h * per_half : (h + 1) * per_half, :], both)
         gather_temb(2)
         gather_temb(3)
-        for h in range(halves):
-            bank = in_bank(6 + h)
-            csig_banks.append(bank)
-            for b in range(per_half):
-                nc.tensor.transpose(bank[:, b, :], coef[:, h * per_half + b, 0:1].to_broadcast([P, P]), ident[:])
-            nc.scalar.copy(csig_of[:, h * HALF : (h + 1) * HALF], bank[:].rearrange("p b j -> p (b j)"))
+        def spread_csig(number, parity):
+            bank = in_bank(number)
+            for b in range(GROUPS // 2):
+                nc.tensor.transpose(bank[:, b, :], coef[:, 2 * b + parity, 0:1].to_broadcast([P, P]), ident[:])
+            return bank
+
+        turned_odd = spread_csig(ODD_BANK, 1)
+        csig_even = spread_csig(EVEN_BANK, 0)
+        nc.scalar.copy(csig_odd[:], turned_odd[:])
 
         def pool_copy(out, in_):
             nc.gpsimd.tensor_scalar(out, in_, 1.0, 0.0, ALU.mult, ALU.add)
@@ -204,7 +194,7 @@ def tile_picked_yddpm_silu_po_kernel(
         nc.vector.tensor_copy(xw[0][:], xw_all[0][:].indirect(offs_list[:]))
         first_dealt = deal(pool_copy, by_slot(w1_first[:]), "w1_first_dealt")
         quantise(w1_q[0][0][:], w1_q[0][1][:], first_dealt[:])
-        nc.vector.tensor_copy(xw[1][:, :EARLY], xw_all[1][:].indirect(offs_list[:, : EARLY // 16]))
+        nc.vector.tensor_copy(xw[1][:], xw_all[1][:].indirect(offs_list[:, : EARLY // 16]))
 
         shares = (
             (nc.scalar.copy, 0, 0, PACK),
@@ -221,7 +211,7 @@ def tile_picked_yddpm_silu_po_kernel(
                 values = dealt[:, (t - first) * W_HALF : (t - first + 1) * W_HALF]
                 quantise(w1_q[1][0][:, cols], w1_q[1][1][:, cols], values)
 
-        xw_late = tagged([P, S - EARLY], U32, "xw_late", "w1_last_dealt2")
+        xw_late = tagged([P, S - EARLY], U32, "xw_late", "w1_last_dealt%d" % (len(shares) - 1))
         nc.vector.tensor_copy(xw_late[:], xw_all[1][:].indirect(offs_list[:, EARLY // 16 :]))
 
         def words_of(o, g):
@@ -233,8 +223,11 @@ def tile_picked_yddpm_silu_po_kernel(
         w2_dealt = keep.tile([P, PACK * N], BF16, name="w2_dealt", align_bytes=64)
         out_codes, out_scales = planes(S, "out")
         result = keep.tile([P, PACK, S], F32, name="result")
-        shared = {}
-        hidden, h_codes, h_scales, back, signal, rounded, noises = {}, {}, {}, {}, {}, {}, {}
+        for u, copy in enumerate((nc.scalar.copy, pool_copy)):
+            copy(w2_dealt[:].rearrange("p (t u m j) -> p u m t j", t=PACK, u=2, j=PACK)[:, u], by_slot(w2_raw[u][:]))
+        quantise(w2_codes[:], w2_scales[:], w2_dealt[:])
+        shared, hidden, noise, signal, rounded = {}, {}, {}, {}, {}
+        last_group = GROUPS - 1
 
         def words_order(ap):
             return ap.rearrange("p (c i t) -> p c t i", i=LINE, t=PACK)
@@ -245,137 +238,109 @@ def tile_picked_yddpm_silu_po_kernel(
         def columns(first, last):
             return slice(first * P, (last + 1) * P)
 
-        def deal_w2(u):
-            view = w2_dealt[:].rearrange("p (t u m j) -> p u m t j", t=PACK, u=2, j=PACK)[:, u]
-            split = W2_SCALAR[u]
-            if split:
-                nc.scalar.copy(view[:, :, :split, :], by_slot(w2_raw[u][:])[:, :, :split, :])
-            if split < PACK:
-                pool_copy(view[:, :, split:, :], by_slot(w2_raw[u][:])[:, :, split:, :])
+        def leaves_with(g):
+            return (g - g % 2, g - g % 2 + 1) if g < PAIRED else (g, g)
 
-        def run_of(g, runs):
-            return [run for run in runs if run[0] <= g <= run[1]][0]
+        def hidden_place(g):
+            if g in (0, last_group):
+                return tagged([P, K_PASS], BF16, "hidden%d" % g, "hidden%d" % g)[:]
+            if g % 2:
+                shared[g] = keep.tile([P, K_PASS], F32, name="shared%d" % g, align_bytes=64)
+                return shared[g][:, : K_PASS // 2].bitcast(BF16)
+            return shared[g - 1][:, K_PASS // 2 :].bitcast(BF16)
 
         def first_layer(g):
             cols = columns(g, g)
             acc = in_bank(ACC_BANK[g])
-            order = FIRST_ORDER if g == 0 else LATER_ORDER
             for o in range(PASSES):
                 codes, scales = w1_q[o]
-                for place, t in enumerate(order):
+                for t in range(PACK):
                     nc.tensor.matmul_mx(
                         out=acc[:, t, :],
                         lhsT=codes[:, t * P : (t + 1) * P].bitcast(FP8X4),
                         lhsT_scale=scales[:, t * P : (t + 1) * P],
                         rhs=words_of(o, g).bitcast(FP8X4),
                         rhs_scale=xs[o][:, cols],
-                        start=(o == 0 and place == 0),
-                        stop=(o == PASSES - 1 and place == PACK - 1),
+                        start=(o == 0 and t == 0),
+                        stop=(o == PASSES - 1 and t == PACK - 1),
                     )
             pre = tagged([P, PACK, P], F32, "pre%d" % g, "pre%d" % g)
             nc.vector.tensor_tensor(pre[:], temb_of[:, :, cols], acc[:], ALU.add)
-            first, last = run_of(g, HIDDEN_RUNS)
-            if g in SHARED:
-                shared[g] = keep.tile([P, K_PASS], F32, name="shared%d" % g, align_bytes=64)
-                hidden[g] = shared[g][:, : K_PASS // 2].bitcast(BF16)
-            elif g - 1 in SHARED:
-                hidden[g] = shared[g - 1][:, K_PASS // 2 :].bitcast(BF16)
-            else:
-                hidden[g] = tagged([P, K_PASS], BF16, "hidden%d" % g, "hidden%d" % g)[:]
-            place = hidden[g]
-            nc.scalar.activation(words_order(place), slots_order(pre[:]), ACT.Silu)
-
-        def quantise_hidden(first):
-            last = run_of(first, HIDDEN_RUNS)[1]
-            width = (last - first + 1) * P
-            name = "h_codes%d" % first
-            h_codes[first] = tagged([P, width], U32, name, TAKES.get(name, name))
-            h_scales[first] = keep.tile([P, width], U8, name="h_scales%d" % first, align_bytes=64)
-            quantise(h_codes[first][:], h_scales[first][:], hidden[first])
+            hidden[g] = hidden_place(g)
+            nc.scalar.activation(words_order(hidden[g]), slots_order(pre[:]), ACT.Silu)
 
         def second_layer(g):
-            first = run_of(g, HIDDEN_RUNS)[0]
-            cols = columns(g - first, g - first)
-            noises[g] = in_bank(NOISE_BANK[g])
+            name = "h_codes%d" % g
+            h_codes = tagged([P, P], U32, name, name if g else "temb2")
+            h_scales = keep.tile([P, P], U8, name="h_scales%d" % g, align_bytes=64)
+            quantise(h_codes[:], h_scales[:], hidden[g])
+            noise[g] = in_bank(NOISE_BANK[g % 2])
             nc.tensor.matmul_mx(
-                out=noises[g][:].rearrange("p t m -> p (t m)"),
-                lhsT=h_codes[first][:, cols].bitcast(FP8X4),
-                lhsT_scale=h_scales[first][:, cols],
+                out=noise[g][:].rearrange("p t m -> p (t m)"),
+                lhsT=h_codes[:].bitcast(FP8X4),
+                lhsT_scale=h_scales[:],
                 rhs=w2_codes[:].bitcast(FP8X4),
                 rhs_scale=w2_scales[:],
                 start=True,
                 stop=True,
             )
 
-        def turn_back(g):
-            noise = noises[g]
-            scaled = keep.tile([P, PACK, P], F32, name="scaled%d" % g)
-            if g in VECTOR_SCALES:
-                nc.vector.tensor_scalar_mul(scaled[:], noise[:], coef[:, g, 1:2])
+        def scale_lat(g):
+            h, c0 = divmod(g * P, HALF)
+            if g in shared:
+                signal[g] = shared[g][:].rearrange("p (t c) -> p t c", t=PACK)
             else:
-                nc.scalar.activation(scaled[:], noise[:], ACT.Copy, scale=coef[:, g, 1:2])
-            back[g] = in_bank(BACK_BANK[g])
-            for t in range(PACK):
-                nc.tensor.transpose(back[g][:, t, :], scaled[:, t, :], ident[:])
-
-        def scale_lat(number):
-            on_pool, first, last, t0, t1 = PRODUCTS[number]
-            h, c0 = divmod(first * P, HALF)
-            width = (last - first + 1) * P
-            start, end = run_of(first, SIGNAL_RUNS)
-            if start in SIGNAL_IN:
-                signal[start] = shared[SIGNAL_IN[start]][:].rearrange("p (t c) -> p t c", t=PACK)
-            elif start not in signal:
-                name = "signal%d" % start
-                signal[start] = tagged([P, PACK, (end - start + 1) * P], F32, name, TAKES.get(name, name))[:]
-            if first not in FROM_PSUM:
-                row = csig_of[:, columns(first, last)]
-            else:
-                row = csig_banks[h][:].rearrange("p b j -> p (b j)")[:, c0 : c0 + width]
-            factor = row.unsqueeze(1).to_broadcast([P, t1 - t0, width])
-            engine = nc.gpsimd if on_pool else nc.vector
-            engine.tensor_tensor(signal[start][:, t0:t1, columns(first - start, last - start)], lat_rows[h][:, t0:t1, c0 : c0 + width], factor, ALU.mult)
+                tag = "hidden%d" % g if g == last_group else "signal%d" % g
+                signal[g] = tagged([P, PACK, P], F32, "signal%d" % g, tag)[:]
+            engine, width, csig_rows = (nc.gpsimd, POOL_SLOTS, csig_odd) if g % 2 else (nc.vector, PACK, csig_even)
+            factor = csig_rows[:, g // 2, :].unsqueeze(1).to_broadcast([P, width, P])
+            for t0 in range(0, PACK, width):
+                slots = slice(t0, t0 + width)
+                engine.tensor_tensor(signal[g][:, slots, :], lat_rows[h][:, slots, c0 : c0 + P], factor, ALU.mult)
 
         def combine(g):
-            start = run_of(g, SIGNAL_RUNS)[0]
-            own = signal[start][:, :, columns(g - start, g - start)]
-            nc.vector.tensor_tensor(result[:, :, columns(g, g)], own, back[g][:], ALU.subtract)
-            first, last = run_of(g, STORE_RUNS)
+            scaled = keep.tile([P, PACK, P], F32, name="scaled%d" % g)
+            nc.scalar.activation(scaled[:], noise[g][:], ACT.Copy, scale=coef[:, g, 1:2])
+            back = in_bank(BACK_BANK[g])
+            for t in range(PACK):
+                nc.tensor.transpose(back[:, t, :], scaled[:, t, :], ident[:])
+            nc.vector.tensor_tensor(result[:, :, columns(g, g)], signal[g], back[:], ALU.subtract)
+            first, last = leaves_with(g)
             if g == last:
                 done = columns(first, last)
                 nc.sync.dma_start(out=out_0[:, done].rearrange("(p t) s -> p t s", t=PACK), in_=result[:, :, done])
 
-        def round_result(g):
-            first, last = run_of(g, ROUND_RUNS)
+        round_tags = {0: "pre%d" % last_group, leaves_with(VECTOR_ROUNDS[0])[0]: "first_w1"}
+
+        def hand_on(g):
+            first, last = leaves_with(g)
             if g == first:
                 name = "rounded%d" % g
-                rounded[first] = tagged([P, (last - first + 1) * K_PASS], BF16, name, TAKES.get(name, name))
-            copy = nc.vector.tensor_copy if g in VECTOR_ROUNDS else pool_copy if g in POOL_ROUNDS else nc.scalar.copy
-            place = rounded[first][:, (g - first) * K_PASS : (g - first + 1) * K_PASS]
+                rounded[last] = tagged([P, (last - first + 1) * K_PASS], BF16, name, round_tags.get(g, name))
+            copy = nc.vector.tensor_copy if g in VECTOR_ROUNDS else nc.scalar.copy
+            place = rounded[last][:, (g - first) * K_PASS : (g - first + 1) * K_PASS]
             copy(words_order(place), slots_order(result[:, :, columns(g, g)]))
-
-        def hand_on(first):
-            last = run_of(first, OUT_RUNS)[1]
-            cols = columns(first, last)
-            start = run_of(first, ROUND_RUNS)[0]
-            values = rounded[start][:, (first - start) * K_PASS : (last + 1 - start) * K_PASS]
-            quantise(out_codes[:, cols], out_scales[:, cols], values)
-            if last in CODES_FROM:
-                done = columns(CODES_FROM[last], last)
+            if g == last:
+                cols = columns(first, last)
+                quantise(out_codes[:, cols], out_scales[:, cols], rounded[g][:])
+            if g in CODES_FROM:
+                done = columns(CODES_FROM[g], g)
                 nc.sync.dma_start(
                     out=out_1[0].rearrange("p c r -> p (c r)").bitcast(I32)[:, done],
                     in_=out_codes[:, done].bitcast(I32),
                 )
 
-        def quantise_w2(unused):
-            quantise(w2_codes[:], w2_scales[:], w2_dealt[:])
-
-        stage = {
-            "F": first_layer, "D": deal_w2, "W": quantise_w2, "H": quantise_hidden, "M": second_layer, "T": turn_back,
-            "L": scale_lat, "C": combine, "R": round_result, "O": hand_on,
-        }
-        for word in PROGRAM.split():
-            stage[word[0]](int(word[1:]))
+        stages = (
+            (first_layer, 0),
+            (second_layer, LAG_SECOND),
+            (scale_lat, LAG_COMBINE),
+            (combine, LAG_COMBINE),
+            (hand_on, LAG_HAND_ON),
+        )
+        for s in range(GROUPS + LAG_HAND_ON):
+            for stage, lag in stages:
+                if 0 <= s - lag < GROUPS:
+                    stage(s - lag)
         for r in range(4):
             nc.sync.dma_start(
                 out=out_2[0, r:SCALE_ROWS:4, :].bitcast(I32), in_=out_scales[r:P:QUADRANT, :].bitcast(I32)

@@ -73,7 +73,7 @@ def tile_picked_yddpm_silu_po_kernel(
         w1_first = tagged([P, PACK, H], F32, "w1_first", "first_w1")
         w1_last = tagged([P, 2, PACK, W_HALF], F32, "w1_last", "coef_window")
         w2_raw = [tagged([P, PACK, W_HALF], F32, "w2_raw%d" % u, "temb%d" % (u + 1)) for u in range(2)]
-        lat_rows = [tagged([P, PACK, HALF], F32, "lat_rows%d" % h, tag) for h, tag in enumerate(("temb3", "first_w1"))]
+        lat_rows = [tagged([P, PACK, HALF], F32, "lat_rows0", "temb3")]
         ident = keep.tile([P, P], F32, name="ident")
         xs_both = keep.tile([P, PASSES * S], U8, name="xs_both", align_bytes=64)
         xs = [xs_both[:, o * S : (o + 1) * S] for o in range(PASSES)]
@@ -129,8 +129,7 @@ def tile_picked_yddpm_silu_po_kernel(
             load_slots(w1_last[:, u], w1[K_PASS:, u * W_HALF : (u + 1) * W_HALF])
         for u in range(2):
             load_slots(w2_raw[u][:], w2[:, u * W_HALF : (u + 1) * W_HALF])
-        for h in range(halves):
-            load_slots(lat_rows[h][:], lat[:, h * HALF : (h + 1) * HALF])
+        load_slots(lat_rows[0][:], lat[:, :HALF])
 
         def half_of_step(h):
             return step_list[:, h * HALF // 16 : (h + 1) * HALF // 16]
@@ -194,6 +193,12 @@ def tile_picked_yddpm_silu_po_kernel(
         nc.vector.tensor_copy(xw[0][:], xw_all[0][:].indirect(offs_list[:]))
         first_dealt = deal(pool_copy, by_slot(w1_first[:]), "w1_first_dealt")
         quantise(w1_q[0][0][:], w1_q[0][1][:], first_dealt[:])
+        lat_rows.append(tagged([P, PACK, HALF], F32, "lat_rows1", "w1_first_dealt"))
+        load_slots(lat_rows[1][:], lat[:, HALF:])
+        temb_words = []
+        for h, (copy, tag) in enumerate(((nc.scalar.copy, "temb_words"), (pool_copy, "first_w1"))):
+            temb_words.append(tagged([P, HALF, PACK], F32, "temb_words%d" % h, tag))
+            copy(temb_words[h][:], temb_of[:, :, h * HALF : (h + 1) * HALF].rearrange("p t c -> p c t"))
         nc.vector.tensor_copy(xw[1][:], xw_all[1][:].indirect(offs_list[:, : EARLY // 16]))
 
         shares = (
@@ -264,10 +269,10 @@ def tile_picked_yddpm_silu_po_kernel(
                         start=(o == 0 and t == 0),
                         stop=(o == PASSES - 1 and t == PACK - 1),
                     )
-            pre = tagged([P, PACK, P], F32, "pre%d" % g, "pre%d" % g)
-            nc.vector.tensor_tensor(pre[:], temb_of[:, :, cols], acc[:], ALU.add)
+            pre = tagged([P, P, PACK], F32, "pre%d" % g, "pre%d" % g)
+            nc.vector.tensor_tensor(pre[:], temb_words[g // per_half][:, g % per_half * P : (g % per_half + 1) * P, :], acc[:].rearrange("p t c -> p c t"), ALU.add)
             hidden[g] = hidden_place(g)
-            nc.scalar.activation(words_order(hidden[g]), slots_order(pre[:]), ACT.Silu)
+            nc.scalar.activation(hidden[g], pre[:].rearrange("p c t -> p (c t)"), ACT.Silu)
 
         def second_layer(g):
             name = "h_codes%d" % g
@@ -310,7 +315,7 @@ def tile_picked_yddpm_silu_po_kernel(
                 done = columns(first, last)
                 nc.sync.dma_start(out=out_0[:, done].rearrange("(p t) s -> p t s", t=PACK), in_=result[:, :, done])
 
-        round_tags = {0: "pre%d" % last_group, leaves_with(VECTOR_ROUNDS[0])[0]: "first_w1"}
+        round_tags = {0: "pre%d" % last_group, leaves_with(VECTOR_ROUNDS[0])[0]: "w1_first_dealt"}
 
         def hand_on(g):
             first, last = leaves_with(g)

from contextlib import ExitStack

import concourse.mybir as mybir
from concourse.masks import make_identity

K, T, S, H, N, R = 1024, 4096, 1024, 512, 512, 256
FLOPS = 2 * S * (K * H + H * N)

F32 = mybir.dt.float32
BF16 = mybir.dt.bfloat16
I32 = mybir.dt.int32
U32 = mybir.dt.uint32
U16 = mybir.dt.uint16
U8 = mybir.dt.uint8
FP8X4 = mybir.dt.float8_e4m3fn_x4
ALU = mybir.AluOpType
ACT = mybir.ActivationFunctionType

P = 128
PACK = 4
K_PASS = P * PACK
PASSES = K // K_PASS
QUADRANT = 32
SCALE_ROWS = K_PASS // 32
GROUPS = S // P
HALF = S // 2
LINE = 4
WINDOW = HALF + 16
ROW_STEP = P // (PASSES * SCALE_ROWS)
CSIG_ROW, CNOISE_ROW = 96, 112
W_HALF = 256
M_HALF = W_HALF // PACK
SCALAR_GATHERS = 7
VECTOR_DEALS = 2
EARLY = 6 * P
POOL_SLOTS = 2
VECTOR_ROUNDS = (5, 7)
PAIRED = GROUPS - 2
LAG_SECOND, LAG_COMBINE, LAG_HAND_ON = 1, 3, GROUPS
ACC_BANK = (0, 1, 2, 3, 0, 1, 2, 0)
NOISE_BANK = (5, 6)
BACK_BANK = (4, 3, 4, 3, 1, 2, 4, 0)
COEF_BANK = (4, 5)
ODD_BANK, EVEN_BANK = 6, 7
CODES_FROM = {3: 0, 5: 4, 7: 6}


def tile_picked_yddpm_silu_po_kernel(
    tc, x_words, x_scales, w1, w2, temb, lat, csig, cnoise, offs, step, out_0, out_1, out_2
):
    nc = tc.nc
    halves = S // HALF
    per_half = HALF // P

    with ExitStack() as ctx:
        keep = ctx.enter_context(tc.tile_pool(name="keep", bufs=1))
        psum = ctx.enter_context(tc.psum_pool(name="psum", bufs=1))

        def tagged(shape, dtype, name, tag):
            return keep.tile(shape, dtype, name=name, tag=tag, align_bytes=64)

        def in_bank(number):
            return psum.tile([P, PACK, P], F32, name="bank%d" % number)

        step_list = keep.tile([P, S // 16], U16, name="step_list")
        offs_list = keep.tile([P, S // 16], U16, name="offs_list")
        temb_rows = [keep.tile([P, PACK * R], F32, name="temb_rows0")] + [
            tagged([P, WINDOW], F32, "temb_rows%d" % t, "temb%d" % t) for t in range(1, PACK)
        ]
        coef_rows = tagged([P, WINDOW], F32, "coef_rows", "coef_window")
        xs_all = tagged([P, T], U8, "xs_all", "last_words")
        xw_all = [keep.tile([P, T], U32, name="xw_all0", align_bytes=64), tagged([P, T], U32, "xw_all1", "last_words")]
        w1_first = tagged([P, PACK, H], F32, "w1_first", "first_w1")
        w1_last = tagged([P, 2, PACK, W_HALF], F32, "w1_last", "coef_window")
        w2_raw = [tagged([P, PACK, W_HALF], F32, "w2_raw%d" % u, "temb%d" % (u + 1)) for u in range(2)]
        lat_rows = [tagged([P, PACK, HALF], F32, "lat_rows0", "temb3")]
        ident = keep.tile([P, P], F32, name="ident")
        xs_both = keep.tile([P, PASSES * S], U8, name="xs_both", align_bytes=64)
        xs = [xs_both[:, o * S : (o + 1) * S] for o in range(PASSES)]

        nc.gpsimd.memset(xs_all[:, : T // 2].bitcast(I32), 0)
        nc.vector.memset(xs_all[:, T // 2 :].bitcast(I32), 0)
        nc.vector.memset(coef_rows[:], 0.0)
        make_identity(nc, ident[:])
        warm = keep.tile([P, 2], F32, name="warm")
        nc.vector.memset(warm[:, 0:1], 0.0)
        nc.scalar.activation(warm[:, 1:2], warm[:, 0:1], ACT.Silu)
        for t in range(1, PACK):
            nc.vector.memset(temb_rows[t][:, R:], 0.0)
        nc.vector.memset(xs_both[:].bitcast(I32), 0)

        def load_words(o):
            nc.sync.dma_start(
                out=xw_all[o][:].bitcast(I32), in_=x_words[o].rearrange("p c r -> p (c r)").bitcast(I32)
            )

        def load_slots(slots, rows):
            nc.sync.dma_start(out=slots, in_=rows.rearrange("(p t) c -> p t c", t=PACK))

        nc.sync.dma_start(offs_list[:], offs)
        nc.sync.dma_start(step_list[:], step)
        nc.sync.dma_start(out=temb_rows[0][:], in_=temb.rearrange("(p t) r -> p (t r)", t=PACK))
        nc.sync.dma_start(
            out=xs_all[0:P:ROW_STEP, :].bitcast(I32), in_=x_scales.rearrange("o q c -> (o q) c").bitcast(I32)
        )
        nc.sync.dma_start(out=coef_rows[CSIG_ROW : CSIG_ROW + 1, :R], in_=csig[:1, :])
        nc.sync.dma_start(out=coef_rows[CNOISE_ROW : CNOISE_ROW + 1, :R], in_=cnoise[:1, :])
        load_words(0)
        load_slots(w1_first[:], w1[:K_PASS, :])

        for t in [PACK - 1] + list(range(1, PACK - 1)):
            nc.gpsimd.tensor_copy(temb_rows[t][:, :R], temb_rows[0][:, t * R : (t + 1) * R])

        picked = keep.tile([P, S], U8, name="picked", align_bytes=64)
        nc.vector.tensor_copy(picked[:], xs_all[:].indirect(offs_list[:]))

        def move_scales(o):
            for r in range(4):
                first = ROW_STEP * (SCALE_ROWS * o + r)
                nc.sync.dma_start(
                    out=xs[o][r:P:QUADRANT, :].bitcast(I32),
                    in_=picked[first : ROW_STEP * SCALE_ROWS * (o + 1) : 4 * ROW_STEP, :].bitcast(I32),
                )

        move_scales(1)
        load_words(1)
        move_scales(0)
        for u in range(2):
            load_slots(w1_last[:, u], w1[K_PASS:, u * W_HALF : (u + 1) * W_HALF])
        for u in range(2):
            load_slots(w2_raw[u][:], w2[:, u * W_HALF : (u + 1) * W_HALF])
        load_slots(lat_rows[0][:], lat[:, :HALF])

        def half_of_step(h):
            return step_list[:, h * HALF // 16 : (h + 1) * HALF // 16]

        temb_of = keep.tile([P, PACK, S], F32, name="temb_of")

        def gather_temb(t):
            for h in range(halves):
                looked_up = temb_rows[t][:].indirect(half_of_step(h))
                if t * halves + h < SCALAR_GATHERS:
                    nc.scalar.activation(temb_of[:, t, h * HALF : (h + 1) * HALF], looked_up, ACT.Copy)
                else:
                    nc.vector.tensor_copy(temb_of[:, t, h * HALF : (h + 1) * HALF], looked_up)

        gather_temb(0)
        gather_temb(1)
        coef_of = keep.tile([P, S], F32, name="coef_of")
        coef = keep.tile([P, GROUPS, 2], F32, name="coef")
        csig_odd = keep.tile([P, GROUPS // 2, P], F32, name="csig_odd")
        for h in range(halves):
            nc.vector.tensor_copy(coef_of[:, h * HALF : (h + 1) * HALF], coef_rows[:].indirect(half_of_step(h)))
            bank = in_bank(COEF_BANK[h])
            for b in range(per_half):
                g = h * per_half + b
                nc.tensor.transpose(bank[:, b, :], coef_of[:, g * P : (g + 1) * P], ident[:])
            both = bank[:, :, CSIG_ROW : P : CNOISE_ROW - CSIG_ROW]
            nc.scalar.copy(coef[:, h * per_half : (h + 1) * per_half, :], both)
        gather_temb(2)
        gather_temb(3)
        def spread_csig(number, parity):
            bank = in_bank(number)
            for b in range(GROUPS // 2):
                nc.tensor.transpose(bank[:, b, :], coef[:, 2 * b + parity, 0:1].to_broadcast([P, P]), ident[:])
            return bank

        turned_odd = spread_csig(ODD_BANK, 1)
        csig_even = spread_csig(EVEN_BANK, 0)
        nc.scalar.copy(csig_odd[:], turned_odd[:])

        def pool_copy(out, in_):
            nc.gpsimd.tensor_scalar(out, in_, 1.0, 0.0, ALU.mult, ALU.add)

        def by_slot(raw):
            return raw.rearrange("p j (m t) -> p m t j", t=PACK)

        def deal(copy, values, name):
            dealt = tagged([P, values.shape[1] * values.shape[2] * PACK], BF16, name, name)
            copy(dealt[:].rearrange("p (t m j) -> p m t j", t=values.shape[2], j=PACK), values)
            return dealt

        def planes(width, name):
            codes = keep.tile([P, width], U32, name=name + "_codes", align_bytes=64)
            scales = keep.tile([P, width], U8, name=name + "_scales", align_bytes=64)
            return codes, scales

        def quantise(codes, scales, values):
            nc.vector.quantize_mx(out=codes.bitcast(FP8X4), scales=scales, in_=values)

        xw = [keep.tile([P, width], U32, name="xw%d" % o, align_bytes=64) for o, width in enumerate((S, EARLY))]
        w1_q = [planes(H, "w1_%d" % o) for o in range(PASSES)]
        nc.vector.tensor_copy(xw[0][:], xw_all[0][:].indirect(offs_list[:]))
        first_dealt = deal(pool_copy, by_slot(w1_first[:]), "w1_first_dealt")
        quantise(w1_q[0][0][:], w1_q[0][1][:], first_dealt[:])
        lat_rows.append(tagged([P, PACK, HALF], F32, "lat_rows1", "w1_first_dealt"))
        load_slots(lat_rows[1][:], lat[:, HALF:])
        temb_words = []
        for h, (copy, tag) in enumerate(((nc.scalar.copy, "temb_words"), (pool_copy, "first_w1"))):
            temb_words.append(tagged([P, HALF, PACK], F32, "temb_words%d" % h, tag))
            copy(temb_words[h][:], temb_of[:, :, h * HALF : (h + 1) * HALF].rearrange("p t c -> p c t"))
        nc.vector.tensor_copy(xw[1][:], xw_all[1][:].indirect(offs_list[:, : EARLY // 16]))

        shares = (
            (nc.scalar.copy, 0, 0, PACK),
            (nc.scalar.copy, 1, VECTOR_DEALS, PACK),
            (nc.vector.tensor_copy, 1, 0, VECTOR_DEALS),
        )
        last_dealt = [
            deal(copy, by_slot(w1_last[:, u])[:, :, first:end, :], "w1_last_dealt%d" % place)
            for place, (copy, u, first, end) in enumerate(shares)
        ]
        for dealt, (copy, u, first, end) in zip(last_dealt, shares):
            for t in range(first, end):
                cols = slice(t * P + u * M_HALF, t * P + (u + 1) * M_HALF)
                values = dealt[:, (t - first) * W_HALF : (t - first + 1) * W_HALF]
                quantise(w1_q[1][0][:, cols], w1_q[1][1][:, cols], values)

        xw_late = tagged([P, S - EARLY], U32, "xw_late", "w1_last_dealt%d" % (len(shares) - 1))
        nc.vector.tensor_copy(xw_late[:], xw_all[1][:].indirect(offs_list[:, EARLY // 16 :]))

        def words_of(o, g):
            if o == PASSES - 1 and g * P >= EARLY:
                return xw_late[:, g * P - EARLY : (g + 1) * P - EARLY]
            return xw[o][:, g * P : (g + 1) * P]

        w2_codes, w2_scales = planes(N, "w2")
        w2_dealt = keep.tile([P, PACK * N], BF16, name="w2_dealt", align_bytes=64)
        out_codes, out_scales = planes(S, "out")
        result = keep.tile([P, PACK, S], F32, name="result")
        for u, copy in enumerate((nc.scalar.copy, pool_copy)):
            copy(w2_dealt[:].rearrange("p (t u m j) -> p u m t j", t=PACK, u=2, j=PACK)[:, u], by_slot(w2_raw[u][:]))
        quantise(w2_codes[:], w2_scales[:], w2_dealt[:])
        shared, hidden, noise, signal, rounded = {}, {}, {}, {}, {}
        last_group = GROUPS - 1

        def words_order(ap):
            return ap.rearrange("p (c i t) -> p c t i", i=LINE, t=PACK)

        def slots_order(ap):
            return ap.rearrange("p t (c i) -> p c t i", i=LINE)

        def columns(first, last):
            return slice(first * P, (last + 1) * P)

        def leaves_with(g):
            return (g - g % 2, g - g % 2 + 1) if g < PAIRED else (g, g)

        def hidden_place(g):
            if g in (0, last_group):
                return tagged([P, K_PASS], BF16, "hidden%d" % g, "hidden%d" % g)[:]
            if g % 2:
                shared[g] = keep.tile([P, K_PASS], F32, name="shared%d" % g, align_bytes=64)
                return shared[g][:, : K_PASS // 2].bitcast(BF16)
            return shared[g - 1][:, K_PASS // 2 :].bitcast(BF16)

        def first_layer(g):
            cols = columns(g, g)
            acc = in_bank(ACC_BANK[g])
            for o in range(PASSES):
                codes, scales = w1_q[o]
                for t in range(PACK):
                    nc.tensor.matmul_mx(
                        out=acc[:, t, :],
                        lhsT=codes[:, t * P : (t + 1) * P].bitcast(FP8X4),
                        lhsT_scale=scales[:, t * P : (t + 1) * P],
                        rhs=words_of(o, g).bitcast(FP8X4),
                        rhs_scale=xs[o][:, cols],
                        start=(o == 0 and t == 0),
                        stop=(o == PASSES - 1 and t == PACK - 1),
                    )
            pre = tagged([P, P, PACK], F32, "pre%d" % g, "pre%d" % g)
            nc.vector.tensor_tensor(pre[:], temb_words[g // per_half][:, g % per_half * P : (g % per_half + 1) * P, :], acc[:].rearrange("p t c -> p c t"), ALU.add)
            hidden[g] = hidden_place(g)
            nc.scalar.activation(hidden[g], pre[:].rearrange("p c t -> p (c t)"), ACT.Silu)

        def second_layer(g):
            name = "h_codes%d" % g
            h_codes = tagged([P, P], U32, name, name if g else "temb2")
            h_scales = keep.tile([P, P], U8, name="h_scales%d" % g, align_bytes=64)
            quantise(h_codes[:], h_scales[:], hidden[g])
            noise[g] = in_bank(NOISE_BANK[g % 2])
            nc.tensor.matmul_mx(
                out=noise[g][:].rearrange("p t m -> p (t m)"),
                lhsT=h_codes[:].bitcast(FP8X4),
                lhsT_scale=h_scales[:],
                rhs=w2_codes[:].bitcast(FP8X4),
                rhs_scale=w2_scales[:],
                start=True,
                stop=True,
            )

        def scale_lat(g):
            h, c0 = divmod(g * P, HALF)
            if g in shared:
                signal[g] = shared[g][:].rearrange("p (t c) -> p t c", t=PACK)
            else:
                tag = "hidden%d" % g if g == last_group else "signal%d" % g
                signal[g] = tagged([P, PACK, P], F32, "signal%d" % g, tag)[:]
            engine, width, csig_rows = (nc.gpsimd, POOL_SLOTS, csig_odd) if g % 2 else (nc.vector, PACK, csig_even)
            factor = csig_rows[:, g // 2, :].unsqueeze(1).to_broadcast([P, width, P])
            for t0 in range(0, PACK, width):
                slots = slice(t0, t0 + width)
                engine.tensor_tensor(signal[g][:, slots, :], lat_rows[h][:, slots, c0 : c0 + P], factor, ALU.mult)

        def combine(g):
            scaled = keep.tile([P, PACK, P], F32, name="scaled%d" % g)
            nc.scalar.activation(scaled[:], noise[g][:], ACT.Copy, scale=coef[:, g, 1:2])
            back = in_bank(BACK_BANK[g])
            for t in range(PACK):
                nc.tensor.transpose(back[:, t, :], scaled[:, t, :], ident[:])
            nc.vector.tensor_tensor(result[:, :, columns(g, g)], signal[g], back[:], ALU.subtract)
            first, last = leaves_with(g)
            if g == last:
                done = columns(first, last)
                nc.sync.dma_start(out=out_0[:, done].rearrange("(p t) s -> p t s", t=PACK), in_=result[:, :, done])

        round_tags = {0: "pre%d" % last_group, leaves_with(VECTOR_ROUNDS[0])[0]: "w1_first_dealt"}

        def hand_on(g):
            first, last = leaves_with(g)
            if g == first:
                name = "rounded%d" % g
                rounded[last] = tagged([P, (last - first + 1) * K_PASS], BF16, name, round_tags.get(g, name))
            copy = nc.vector.tensor_copy if g in VECTOR_ROUNDS else nc.scalar.copy
            place = rounded[last][:, (g - first) * K_PASS : (g - first + 1) * K_PASS]
            copy(words_order(place), slots_order(result[:, :, columns(g, g)]))
            if g == last:
                cols = columns(first, last)
                quantise(out_codes[:, cols], out_scales[:, cols], rounded[g][:])
            if g in CODES_FROM:
                done = columns(CODES_FROM[g], g)
                nc.sync.dma_start(
                    out=out_1[0].rearrange("p c r -> p (c r)").bitcast(I32)[:, done],
                    in_=out_codes[:, done].bitcast(I32),
                )

        stages = (
            (first_layer, 0),
            (second_layer, LAG_SECOND),
            (scale_lat, LAG_COMBINE),
            (combine, LAG_COMBINE),
            (hand_on, LAG_HAND_ON),
        )
        for s in range(GROUPS + LAG_HAND_ON):
            for stage, lag in stages:
                if 0 <= s - lag < GROUPS:
                    stage(s - lag)
        for r in range(4):
            nc.sync.dma_start(
                out=out_2[0, r:SCALE_ROWS:4, :].bitcast(I32), in_=out_scales[r:P:QUADRANT, :].bitcast(I32)
            )
